import numpy as np, ml_dtypes
CORES = [25,29,65,69,153,157,193,197]
N = 8
import mx_ref
BF = ml_dtypes.bfloat16
def entries(a):
    return np.ascontiguousarray(a.T).reshape(-1)
def table(e):
    return np.ascontiguousarray(np.reshape(e, (-1, 16)).T).astype(np.int32)
def gentries(a):
    return np.ascontiguousarray(a.reshape(8, 16, -1).transpose(0, 2, 1)).reshape(8, -1)
def gtable(e):
    e = np.asarray(e); return np.ascontiguousarray(e.reshape(8, -1, 16).transpose(0, 2, 1)).reshape(128, -1).astype(np.int32)
def tile(rs):
    return np.stack(rs, axis=2).reshape(128, -1).astype(BF)
def pick(q, e):
    c = np.concatenate([q[0].reshape(128, -1, 4), np.zeros((128, 1, 4), np.uint8)], axis=1); s = np.concatenate([q[1], np.ones((16, 1), np.uint8)], axis=1)
    return (np.ascontiguousarray(c[:, e].reshape(128, -1)), np.ascontiguousarray(s[:, e]))
def join(*qs):
    return (np.concatenate([q[0] for q in qs], axis=1), np.concatenate([q[1] for q in qs], axis=1))
def put(q, e, v):
    c, s = q[0].reshape(128, -1, 4).copy(), q[1].copy(); c[:, e] = v[0].reshape(128, -1, 4); s[:, e] = v[1]
    return (c.reshape(128, -1), s)
def pk(c, s):
    return (np.ascontiguousarray(c), mx_ref.live(s))
def emit(q):
    return q[0], q[1]
def packed(v, rng):
    q = [mx_ref.quantize(np.ascontiguousarray(v[r])) for r in range(N)]
    return np.stack([a for a, b in q]), np.stack([mx_ref.plane(b, rng) for a, b in q])
def values_of_codes():
    e, c = np.zeros((128, 128, 4), np.float32), np.zeros((128, 2, 4), np.uint8)
    e[np.arange(128), np.arange(128), 0] = 1
    c[:127, :, 0] = np.arange(256).reshape(2, 128).T[:127]
    return mx_ref.matmul(mx_ref.quantize(e.reshape(128, 512).astype(BF)), (c.reshape(128, 8), np.full((16, 2), 127, np.uint8))).T.reshape(-1).astype(np.float64)
CODE_VALUE, SCALE_VALUE = values_of_codes(), 2.0 ** (np.arange(256) - 127.0)
def decode(q):
    return (CODE_VALUE[q[0]].reshape(16, 8, -1, 4) * SCALE_VALUE[q[1]][:, None, :, None] + 0.0).reshape(128, -1).astype(np.float32)
def f(rng, *shape):
    return mx_ref.flush((rng.standard_normal(shape, dtype=np.float32) * np.exp2(rng.integers(-2, 3, shape[:-1] + (1,)))).astype(BF))
def wide(rng, *shape, cols=0):
    v = rng.standard_normal(shape, dtype=np.float32) * np.exp2(rng.integers(-12, 13, shape)).astype(np.float32)
    if cols: v *= np.repeat(np.exp2(rng.integers(-cols, cols + 1, shape[:-2] + (1, shape[-1] // 4))) * (rng.random(shape[:-2] + (1, shape[-1] // 4)) > 0.0625), 4, axis=-1).astype(np.float32)
    return mx_ref.flush(v.astype(BF))
C, T, K, STEPS = 400, 320, 96, 3
MATES = [1, 2, 4]
DECIDE = [16 * i + k for i in range(STEPS) for k in range(2)]
def numbers_of(rng):
    return {"x": np.array(f(rng, N, 128, 4 * C)), "u": np.array(f(rng, N, 128, 512)), "v": np.array(f(rng, N, 128, 512))}
def lists(rng):
    return {"p": np.stack([gtable(np.stack([rng.permutation(C) for g in range(8)])) for r in range(N)]),
            "ln": np.stack([table(np.concatenate([rng.permutation(T) for i in range(STEPS)])) for r in range(N)])}
def layers(rng):
    k = np.exp2(rng.permuted(np.tile(np.arange(128) % 5 - 2.0, (N, 1)), axis=1))[:, :, None]
    return np.array(mx_ref.flush((rng.standard_normal((N, 128, 2048)) * k).astype(np.float32).astype(BF))).reshape(N, 8, 16, 4, 8, 16, 4)
def weights(rng, w):
    c, s = packed(np.ascontiguousarray(w).reshape(N, 128, 2048), rng)
    return {"wc": c, "ws": s}
def setup_inputs(rng):
    return {**numbers_of(rng), **lists(rng), **weights(rng, layers(rng))}
def setup_inputs_ties(rng):
    d = numbers_of(rng)
    x = d["x"].reshape(N, 8, 16, C, 4)
    x[:, :, 0] = 0
    x[:, :, 0, :, 0] = rng.integers(-1, 2, (N, 8, C)).astype(np.float32).astype(BF)
    x[:, :, :, ::8] = 0
    u = d["u"].reshape(N, 128, 128, 4)
    u[:, :, DECIDE] = 0
    o = rng.permutation(N)
    for r in range(N):
        g = rng.permutation(8)
        for i, c in enumerate(DECIDE): u[r, 16 * g[i], c, 0] = 0.0 if r == o[0] else -1.0 if r == o[1] else 1.0
    w = layers(rng)
    w[:, :, 0] = 0
    w[:, :, :, :, :, 0] = 0
    return {"x": x.reshape(N, 128, 4 * C), "u": u.reshape(N, 128, 512), "v": d["v"], **lists(rng), **weights(rng, w)}
def setup_inputs_near(rng):
    d = numbers_of(rng)
    x = d["x"].reshape(N, 8, 16, C, 4)
    u = d["u"].reshape(N, 128, 128, 4)
    x[:, :, :8] = 0
    u[:, :, DECIDE] = 0
    o = rng.permutation(N)
    for r in range(N):
        k = 2.0 ** -30 if o[r] % 2 == 0 else 1.0
        s = rng.integers(-1, 2, (8, C)) * k
        x[r, :, 0, :, 0] = (1.125 * s).astype(np.float32).astype(BF)
        x[r, :, 1, :, 0] = (-s).astype(np.float32).astype(BF)
        for g in rng.permutation(8)[:4]:
            c = rng.integers(T)
            x[r, g, 0, c, 0] = 2.0 ** 16 * rng.choice([-1.0, 1.0])
            x[r, g, 1, c, 0] = 0
        g = rng.permutation(8)
        for i, c in enumerate(DECIDE):
            u[r, 16 * g[i], c, 0] = 1.125 * k
            u[r, 16 * g[i] + 1, c, 0] = 1.25 * k
    w = layers(rng)
    w[:, :, :8] = 0
    w[:, :, :, :, :, :8] = 0
    return {"x": x.reshape(N, 128, 4 * C), "u": u.reshape(N, 128, 512), "v": d["v"], **lists(rng), **weights(rng, w)}
def setup_inputs_twice(rng):
    d = numbers_of(rng)
    x = d["x"].reshape(N, 8, 16, C, 4)
    a = (2 * rng.integers(2, 8, (N, 8, 8, C, 4)) + 1) * np.exp2(rng.integers(-5, -3, (N, 8, 8, C, 4)))
    a[:, :, 0, :, 0] = 1.96875 * 2.0 ** 12
    x[:, :, :8] = (a * rng.choice([-1.0, 1.0], a.shape)).astype(np.float32).astype(BF)
    w = layers(rng)
    w[:, :, 0] = 0
    w[:, :, :, :, :, :8] = 0
    return {"x": x.reshape(N, 128, 4 * C), "u": d["u"], "v": d["v"], **lists(rng), **weights(rng, w)}
def setup_inputs_ends(rng):
    d = numbers_of(rng)
    e = rng.permutation(N) % 4
    x, w = np.zeros((N, 8, 16, C, 4)), np.zeros((N, 128, 4, 128, 4), np.float32)
    u = d["u"].reshape(N, 128, 128, 4)
    v, p, n, j, i = [], [], [], np.arange(C), np.arange(128)
    for r in range(N):
        k = e[r]
        s = rng.choice([-1.0, 1.0], (8, 1, C, 1))
        x[r] = 2.0 ** 17 * (1.0, s[:1], 2.0 ** -47, s)[k]
        for c in DECIDE:
            a = (2.0 ** 30, 0.0, 2.0 ** -30 if c % 16 else -2.0 ** -30, 2.0 ** 30 * rng.choice([-1.0, 1.0], (128, 4)))[k]
            u[r, :, c] = np.asarray(a, np.float32).astype(BF)
        v.append((1.0 if k == 0 else rng.choice([-1.0, 1.0], (128, 512))) * np.full((128, 512), 2.0 ** (-30 if k == 2 else 30)))
        if k == 3:
            for b in range(4): w[r, (i + 16) % 128, b, i, b] = -1024
        else: w[r] = (2, 0, -2)[k]
        p.append(gtable((np.tile(j, (8, 1)), np.tile(j[::-1], (8, 1)), (j + 16 * np.arange(8)[:, None] + 1) % C, np.stack([rng.permutation(C) for g in range(8)]))[k]))
        n.append(table((np.tile(np.arange(T), STEPS), np.tile(np.arange(T)[::-1], STEPS), np.tile(rng.permutation(T), STEPS), np.concatenate([rng.permutation(T) for g in range(STEPS)]))[k]))
    return {"x": x.astype(np.float32).reshape(N, 128, 4 * C).astype(BF), "u": u.reshape(N, 128, 512), "v": np.stack(v).astype(np.float32).astype(BF), "p": np.stack(p), "ln": np.stack(n), **weights(rng, w.astype(BF))}
def setup_inputs_spread(rng):
    d = setup_inputs(rng)
    d["x"] = wide(rng, N, 128, 4 * C, cols=2)
    return d
def check_inputs(d):
    b = []
    for k, most in (("x", 2.0 ** 17), ("u", 2.0 ** 30), ("v", 2.0 ** 30)):
        a = np.abs(d[k].astype(np.float32))
        if not (np.isfinite(a).all() and ((a == 0) | (a >= 2.0 ** -30) & (a <= most)).all()): b.append("a value of " + k)
    none, least, most = [emit(mx_ref.quantize(np.full((128, 16), k, np.float32).astype(BF)))[1][0, 0] for k in (0.0, 2.0 ** -30, 2.0 ** 30)]
    for r in range(N):
        if (np.sort(gentries(d["p"][r]), axis=1) != np.arange(C)).any(): b.append("p: a group's entries aren't a permutation")
        if (np.sort(entries(d["ln"][r]).reshape(STEPS, T), axis=1) != np.arange(T)).any(): b.append("ln: a step's entries aren't a permutation")
        if ((d["wc"][r] & 0x7F) == 0x7F).any(): b.append("wc: a code that is no number")
        s = mx_ref.live(d["ws"][r])
        if ((s != none) & ((s < least) | (s > most))).any(): b.append("ws: a scale out of range")
        with np.errstate(all="ignore"):
            w = np.abs(decode(pk(d["wc"][r], d["ws"][r]))).astype(np.float64).reshape(128, 512, 4)
            if not np.max(np.sum(w, axis=(0, 2))) <= 1024: b.append("W: the sizes of a column add up to more than 1024")
    return b
def moves(s, p, ln):
    at = C * np.arange(8)[:, None] + p
    has = at.copy()
    for i in range(STEPS):
        link = 2 * ln[T * i:T * i + T] + (s[16 * i + 1] > 0)
        push, stack, own = s[16 * i] > 0, has[:, :T].copy(), has[link % 8, T + link // 8]
        has[:, :T] = np.where(push, np.concatenate([own[None], stack[:7]]), np.concatenate([stack[1:], own[None]]))
        has[link % 8, T + link // 8] = np.where(push, stack[7], stack[0])
    m = np.zeros(8 * C, np.int64)
    m[at] = has
    return m
def moved(t, m):
    z = t.reshape(8, 16, C, 4).transpose(0, 2, 1, 3).reshape(8 * C, 16, 4)[m]
    return np.ascontiguousarray(z.reshape(8, C, 16, 4).transpose(0, 2, 1, 3)).reshape(128, 4 * C)
def reference(x, u, v, p, ln, wc, ws):
    qu = [mx_ref.quantize(u[r]) for r in range(N)]
    lay = [pk(wc[r], ws[r]) for r in range(N)]
    now = [x[r] for r in range(N)]
    for a in MATES:
        m, qz = [], []
        for r in range(N):
            s = mx_ref.matmul(qu[r], mx_ref.quantize(np.ascontiguousarray(now[r][:, :4 * T])))
            m.append(moves(s, gentries(p[r]), entries(ln[r])))
            qz.append(mx_ref.quantize(moved(now[r], m[r])))
        for r in range(N):
            h = join(pick(qz[r ^ a], np.arange(K)), pick(qz[r], np.arange(K, C)))
            has = decode(h)
            made = tile([np.maximum(mx_ref.matmul(pick(lay[r], np.arange(128 * b, 128 * b + 128)), h), np.float32(0.0)) * np.float32(0.015625) + has[:, b::4] for b in range(4)])
            now[r] = moved(made, np.argsort(m[r]))
    y, op = np.zeros((N, 128, C), np.float32), np.zeros((N, 8, C), np.float32)
    oc, osc = np.zeros((N, 128, 4 * C), np.uint8), np.zeros((N, 16, C), np.uint8)
    for r in range(N):
        q = mx_ref.quantize(now[r])
        y[r] = mx_ref.matmul(mx_ref.quantize(v[r]), q)
        op[r] = m[r].reshape(8, C)
        oc[r], osc[r] = emit(q)
    return {"y": y, "op": op, "oc": oc, "osc": osc}

@@ -1,0 +1,645 @@
+from concourse.mybir import dt, AluOpType, ActivationFunctionType
+
+C, ST, KX, STEPS, N = 400, 320, 96, 3, 8
+MATES = [1, 2, 4]
+W8 = 8 * 4 * C
+LW = 512
+OP = AluOpType
+COPY, RELU = ActivationFunctionType.Copy, ActivationFunctionType.Relu
+CODES = "float8_e4m3fn_x4"
+
+SCRATCH = {
+    "R": ("sbuf", [128, W8], "bfloat16"), "XT": ("sbuf", [128, 4 * C], "bfloat16"), "ZT": ("sbuf", [128, 4 * C], "bfloat16"),
+    "UT": ("sbuf", [128, 512], "bfloat16"), "VT": ("sbuf", [128, 512], "bfloat16"),
+    "ET": ("sbuf", [128, 2048], "bfloat16"), "ONE": ("sbuf", [128, 512], "bfloat16"),
+    "KWT": ("sbuf", [128, 2048], "bfloat16"), "BT": ("sbuf", [128, 768], "bfloat16"),
+    "LP": ("sbuf", [128, 25], "int32"), "LN": ("sbuf", [128, 60], "int32"),
+    "PU": ("sbuf", [128, 26], "uint16"), "LNU": ("sbuf", [128, 60], "uint16"),
+    "LOF0": ("sbuf", [128, 60], "uint16"), "LOF1": ("sbuf", [128, 60], "uint16"),
+    "LX0": ("sbuf", [128, 60], "uint16"), "LX1": ("sbuf", [128, 60], "uint16"),
+    "CM0": ("sbuf", [128, 26], "uint16"), "CM1": ("sbuf", [128, 26], "uint16"), "LTL": ("sbuf", [128, 6], "uint16"),
+    "UL": ("sbuf", [128, 8], "uint16"), "CLU": ("sbuf", [128, 6], "uint16"),
+    "KU0": ("sbuf", [128, 20], "uint16"), "KU1": ("sbuf", [128, 20], "uint16"),
+    "LU0": ("sbuf", [128, 40], "uint16"), "LU1": ("sbuf", [128, 40], "uint16"),
+    "OFZ": ("sbuf", [128, 104], "uint16"), "OFX": ("sbuf", [128, 104], "uint16"),
+    "IQ": ("sbuf", [128, 960], "bfloat16"), "MASK": ("sbuf", [128, 960], "bfloat16"), "SEG": ("sbuf", [128, 960], "bfloat16"),
+    "IDT": ("sbuf", [128, 512], "float32"), "ID5": ("sbuf", [128, 320], "float32"), "GI": ("sbuf", [128, 64], "bfloat16"),
+    "THR": ("sbuf", [128, 64], "float32"), "IDX": ("sbuf", [128, 128], "int32"), "SC": ("sbuf", [128, 24], "float32"),
+    "SJ": ("sbuf", [128, 60], "float32"), "KC": ("sbuf", [128, 3], "float32"),
+    "QQ": ("sbuf", [128, 1280], "float32"), "VA": ("sbuf", [128, 640], "float32"), "MF": ("sbuf", [128, 400], "float32"), "ML": ("sbuf", [128, 240], "float32"),
+    "CF": ("sbuf", [128, 400], "float32"), "MG": ("sbuf", [128, 960], "float32"), "SN": ("sbuf", [128, 960], "float32"),
+    "KF0": ("sbuf", [128, 320], "bfloat16"), "KF1": ("sbuf", [128, 320], "bfloat16"),
+    "MK": ("sbuf", [128, 960], "bfloat16"), "SCK": ("sbuf", [128, 960], "bfloat16"),
+    "DF0": ("sbuf", [128, 2048], "float32"), "DF1": ("sbuf", [128, 2048], "float32"),
+    "DI0": ("sbuf", [128, 704], "int32"), "DI1": ("sbuf", [128, 704], "int32"),
+    "T0": ("sbuf", [128, 8 * LW], "float32"), "TN": ("sbuf", [128, 8 * LW], "float32"),
+    "FL0": ("sbuf", [128, 640], "float32"), "FL1": ("sbuf", [128, 640], "float32"), "FLO": ("sbuf", [128, 640], "float32"),
+    "OPF": ("sbuf", [128, 400], "float32"), "RL": ("sbuf", [128, 1216], "float32"), "RL2": ("sbuf", [128, 512], "float32"), "YO": ("sbuf", [128, 400], "float32"),
+    "PS": ("psum", [128, 4096], "float32"),
+}
+for _n, _w in (("U", 128), ("UP", 128), ("V", 128), ("W", 512), ("E", 512), ("K", 512), ("B", 192), ("X", C), ("S", 128), ("R", KX)):
+    SCRATCH["Q" + _n] = ("sbuf", [128, _w], CODES)
+    SCRATCH["S" + _n] = ("sbuf", [128, _w], "uint8")
+for _r in range(STEPS):
+    SCRATCH["HQ%d" % _r] = ("sbuf", [128, C], CODES)
+    SCRATCH["HS%d" % _r] = ("sbuf", [128, C], "uint8")
+DMAS = ["d_ln", "d_p", "d_u", "d_x", "d_xs", "d_v", "d_w", "d_t0", "d_tn0", "d_tn1", "d_out", "d_op"]
+DMAS += ["d_%s%d" % (k, r) for k in ("ye", "yl") for r in range(STEPS)]
+SEMAPHORES = ["ev", "es", "et", "eg", "rarr", "rsent"] + DMAS + ["arr%d" % r for r in range(STEPS)] + ["snt%d" % r for r in range(STEPS)]
+
+
+def hops(T, topo, i, r):
+    src, dst = T.cores[i], T.cores[i ^ MATES[r]]
+    if topo.may_write(src, dst):
+        return None, None
+    c = [k for k in topo.cores_of(src) if k not in T.cores and topo.die(k) == topo.die(src) and topo.may_write(k, dst)]
+    return c[0], c[-1]
+
+
+def mask_of(topo, src, dst):
+    e = topo.engines(src, dst)[:8]
+    return sum(1 << k for k in e), len(e)
+
+
+def relay(g, core, T, topo):
+    for i in range(N):
+        for r in range(STEPS):
+            pair = hops(T, topo, i, r)
+            if core not in pair:
+                continue
+            src, dst = T.cores[i], T.cores[i ^ MATES[r]]
+            jobs = [k for k in range(2) if pair[k] == core]
+            n_in = mask_of(topo, src, core)[1]
+            m, n = mask_of(topo, core, dst)
+            rid, pid = topo.addr(dst, core)
+            g.wait_ge(T.sem.rarr, n_in * len(jobs))
+            for k in jobs:
+                if k == 0:
+                    o, s = T["HQ%d" % r][:, 0:KX].bitcast(dt.uint8), T.QR[:, 0:KX].bitcast(dt.uint8)
+                else:
+                    o, s = T["HS%d" % r][:, 0:KX], T.SR[:, 0:KX]
+                g.remote_dma(out_ap=o, in_ap=s, remote_sem=T.sem["arr%d" % r], local_sem=T.sem.rsent, pid=pid, routing_id=rid, dma_engine_mask=m)
+            g.wait_ge(T.sem.rsent, n * len(jobs))
+
+
+def A(name, a, b, s=1):
+    return ("A", name, a, b, s)
+
+
+def IND(win, off):
+    return ("I", win, off)
+
+
+def CW(name, a, b):
+    return ("C", name, a, b, 1)
+
+
+def is_ap(x):
+    return isinstance(x, tuple) and len(x) > 0 and x[0] in ("A", "I", "C")
+
+
+def builder(g, T):
+    Q = {"v": g.vector, "s": g.scalar, "t": g.tensor, "g": g, "y": g.sync}
+    known = {q: {} for q in Q}
+    total, clock, hist, waited, pending = {}, {}, {}, {}, {}
+
+    def ap(x):
+        if x[0] == "A":
+            _, n, a, b, s = x
+            return T[n][:, a:b] if s == 1 else T[n][:, a:b:s]
+        if x[0] == "C":
+            return T[x[1]][:, x[2]:x[3]].bitcast(dt.uint32)
+        return ap(x[1]).indirect(ap(x[2]))
+
+    def region(x):
+        _, n, a, b, s = x
+        if n == "PS":
+            return n, (a // 512 * 512, (b + 511) // 512 * 512, 1)
+        return n, (a, b, s)
+
+    def meet(p, q):
+        if p[1] <= q[0] or q[1] <= p[0]:
+            return False
+        return not (p[2] == q[2] > 1 and (p[0] - q[0]) % p[2])
+
+    def wait(q, evs):
+        best = {}
+        for s, v in set(evs):
+            if known[q].get(s, 0) < v:
+                best[s] = max(v, best.get(s, 0))
+        evs = [e for e in best.items() if not any(o != e[0] and clock[(o, w)].get(e[0], 0) >= e[1] for o, w in best.items())]
+        for s, v in sorted(evs):
+            Q[q].wait_ge(T.sem[s], v)
+            waited[s] = max(v, waited.get(s, 0))
+            for k, w in clock[(s, v)].items():
+                known[q][k] = max(w, known[q].get(k, 0))
+
+    def hazards(q, reads, writes, acc=False):
+        evs = []
+        for x, w in [(r, False) for r in reads] + [(r, True) for r in writes]:
+            n, reg = region(x)
+            for reg2, w2, ev, q2 in hist.get(n, []):
+                if meet(reg, reg2) and (w or w2 or (n == "PS" and q2 != q)) and not (acc and q2 == q):
+                    evs.append(ev)
+        wait(q, evs)
+
+    def note(q, reads, writes, ev):
+        for x, w in [(r, False) for r in reads] + [(r, True) for r in writes]:
+            n, reg = region(x)
+            h = hist.setdefault(n, [])
+            if w and reg[2] == 1:
+                h[:] = [e for e in h if not (reg[0] <= e[0][0] and e[0][1] <= reg[1])]
+            h[:] = [e for e in h if not (e[0] == reg and e[1] == w and e[3] == q and e[2][0] == ev[0])]
+            h.append((reg, w, ev, q))
+
+    def parts(xs):
+        out = []
+        for x in xs:
+            if is_ap(x):
+                out += [("A",) + x[1][1:], x[2]] if x[0] == "I" else [("A",) + x[1:]]
+        return out
+
+    def emit(q, fn, nout, *args, acc=False, **kw):
+        writes, reads = [], parts(args[nout:]) + parts(kw.values())
+        for x in args[:nout]:
+            if x[0] == "I":
+                writes.append(("A",) + x[1][1:])
+                reads.append(x[2])
+            else:
+                writes.append(("A",) + x[1:])
+        hazards(q, reads, writes, acc)
+        s = "e" + q
+        i = fn(*[ap(x) if is_ap(x) else x for x in args], **{k: ap(x) if is_ap(x) else x for k, x in kw.items()})
+        i.then_inc(T.sem[s], 1)
+        total[s] = total.get(s, 0) + 1
+        c = dict(known[q])
+        c[s] = total[s]
+        clock[(s, total[s])] = c
+        note(q, reads, writes, (s, total[s]))
+
+    def batch(sem, q, reads, writes):
+        o = pending.setdefault(sem, [[], [], {}])
+        o[0] += list(reads)
+        o[1] += list(writes)
+        for k, v in known[q].items():
+            o[2][k] = max(v, o[2].get(k, 0))
+
+    def dma(q, sem, out, in_, reads=(), writes=()):
+        hazards(q, reads, writes)
+        Q[q].dma_start(out, in_).then_inc(T.sem[sem], 16)
+        total[sem] = total.get(sem, 0) + 16
+        batch(sem, q, reads, writes)
+
+    def close(sem):
+        reads, writes, c = pending.pop(sem)
+        c[sem] = total[sem]
+        clock[(sem, total[sem])] = c
+        note("dma", reads, writes, (sem, total[sem]))
+
+    def remote(out, in_, reads, rsem, lsem, addr, m, n):
+        hazards("g", reads, [])
+        g.remote_dma(out_ap=out, in_ap=in_, remote_sem=T.sem[rsem], local_sem=T.sem[lsem], pid=addr[1], routing_id=addr[0], dma_engine_mask=m)
+        total[lsem] = total.get(lsem, 0) + n
+        batch(lsem, "g", reads, [])
+
+    def arrives(writes, sem, n):
+        total[sem] = n
+        clock[(sem, n)] = {sem: n}
+        note("remote", [], writes, (sem, n))
+
+    def finish():
+        for s in sorted(total):
+            if waited.get(s, 0) < total[s]:
+                g.wait_ge(T.sem[s], total[s])
+
+    return emit, dma, close, remote, arrives, finish
+
+
+def rank_program(g, core, T, topo):
+    rank = T.rank_of(core)
+    if rank is None:
+        relay(g, core, T, topo)
+        return
+    emit, dma, close, remote, arrives, finish = builder(g, T)
+    V, S = g.vector, g.scalar
+
+    def ts(out, x, s1, op0, s2=None, op1=None):
+        if op1 is None:
+            emit("v", V.tensor_scalar, 1, out, x, s1, None, op0)
+        else:
+            emit("v", V.tensor_scalar, 1, out, x, s1, s2, op0, op1)
+
+    def tt(out, x, y, op):
+        emit("v", V.tensor_tensor, 1, out, x, y, op)
+
+    def cp(out, x):
+        emit("v", V.tensor_copy, 1, out, x)
+
+    def act(out, x, func=COPY, **kw):
+        emit("s", S.activation, 1, out, x, func, **kw)
+
+    def quant(n, a, b, x, sn=None):
+        emit("v", V.quantize_mx, 2, A(n, a, b), A(sn or "S" + n[1:], a, b), x)
+
+    def mm(out, l, ls, r, rs, start=True, stop=True):
+        emit("t", g.tensor.matmul_mx, 1, out, l, ls, r, rs, start, stop, acc=not start)
+
+    def iota(out, pattern, base, cm, whole=False):
+        if whole:
+            emit("g", g.iota, 1, out, pattern, base, cm)
+        else:
+            emit("g", g.iota, 1, out, pattern, base, cm, allow_small_or_imprecise_dtypes=True)
+
+    def sc(i):
+        return A("SC", i, i + 1)
+
+    def ix(a, b):
+        return A("IDX", a, b)
+
+    def sj(i):
+        return A("SJ", 20 * i, 20 * i + 20)
+
+    def shifted(sem, queues, name, width, src, a, b, reads):
+        n = 0
+        for k in range(1, 8):
+            for d0, s0, rows in ((0, 16 * k, 128 - 16 * k), (128 - 16 * k, 0, 16 * k)):
+                dma(queues[n % len(queues)], sem, T[name][d0:d0 + rows, width * k + a:width * k + b], src[s0:s0 + rows, a:b],
+                    reads=reads, writes=[A(name, width * k + a, width * k + b)])
+                n += 1
+        close(sem)
+
+    for k in range(8):
+        dma("sy"[k % 2], "d_ln", T.LN[16 * k:16 * k + 16, :], T.ln[:, :], writes=[A("LN", 0, 60)])
+    close("d_ln")
+    dma("s", "d_p", T.LP[:, :], T.p[:, :], writes=[A("LP", 0, 25)])
+    close("d_p")
+    dma("y", "d_u", T.UT[:, :], T.u[:, :], writes=[A("UT", 0, 512)])
+    close("d_u")
+    dma("y", "d_x", T.R[:, 0:4 * C], T.x[:, :], writes=[A("R", 0, 4 * C)])
+    close("d_x")
+
+    iota(ix(0, 1), [[0, 1]], 0, 1, True)
+    iota(A("GI", 0, 64), [[0, 2], [1, 8], [0, 4]], 0, 0)
+    iota(ix(16, 36), [[16, 20]], 0, 0, True)
+    iota(ix(36, 41), [[64, 5]], 0, 0, True)
+    iota(ix(48, 56), [[0, 8]], 0, 0, True)
+    iota(A("IDT", 0, 512), [[1, 512]], 0, 0)
+    iota(A("ID5", 0, 320), [[512, 320]], 0, 0)
+    iota(A("IQ", 0, 960), [[0, 60], [1, 16]], 0, 0)
+    for i, k in enumerate((1536.0, -512.0, 512.0)):
+        emit("v", V.memset, 1, A("KC", i, i + 1), k)
+    iota(A("ONE", 0, 512), [[0, 512]], 1, 0)
+    iota(A("BT", 0, 768), [[0, 768]], 0, 0)
+    for i, seq in enumerate((((16, -1), (32, 7), (48, -1), (80, 0), (96, -1), (112, 4)), ((16, 2), (32, -1), (96, 0), (112, -1)), ((16, -1), (112, 0)))):
+        for p0, k in seq:
+            emit("g", g.affine_select, 1, A("KC", i, i + 1), A("KC", i, i + 1), [[0, 1]], OP.is_gt, 512.0 * k, p0, -1)
+    for b in range(4):
+        emit("g", g.affine_select, 1, A("ET", 512 * b, 512 * b + 512), A("ONE", 0, 512), [[-1, 512]], OP.is_equal, 0.0, b, 4)
+    for n in ("T0", "TN"):
+        for k in range(8):
+            iota(A(n, LW * k + C, LW * k + LW), [[0, LW - C]], 0, 0)
+
+    ts(ix(1, 2), ix(0, 1), 15, OP.bitwise_and)
+    ts(ix(2, 3), ix(0, 1), 4, OP.logical_shift_right)
+    ts(ix(3, 4), ix(0, 1), 5, OP.logical_shift_right)
+    ts(ix(4, 5), ix(0, 1), 3, OP.bitwise_and)
+    ts(ix(5, 6), ix(0, 1), 4, OP.logical_shift_right, 1, OP.bitwise_and)
+    cp(sc(0), ix(1, 2))
+    cp(sc(1), ix(2, 3))
+    ts(sc(2), ix(2, 3), 400, OP.mult)
+    ts(sc(4), ix(5, 6), LW, OP.mult)
+    ts(sc(12), ix(2, 3), LW, OP.mult, -8192, OP.add)
+    cp(sc(9), ix(3, 4))
+    ts(sc(5), ix(4, 5), 3, OP.is_equal, -47, OP.mult)
+    ts(sc(6), ix(4, 5), 16, OP.mult)
+    tt(sc(7), sc(6), sc(5), OP.add)
+    ts(sc(8), sc(6), 17, OP.add)
+    ts(sc(10), sc(0), 4, OP.mult)
+    tt(sc(11), sc(10), sc(9), OP.add)
+    ts(sj(2), ix(16, 36), sc(0), OP.add)
+    ts(sj(0), sj(2), 9728, OP.add)
+    ts(sj(1), sj(2), sc(12), OP.subtract, 1024, OP.add)
+
+    cp(A("PU", 0, 25), A("LP", 0, 25))
+    act(A("T0", 0, C), IND(A("IDT", 0, 512), A("PU", 0, 25)), ActivationFunctionType.Identity, bias=sc(2))
+    shifted("d_t0", "y", "T0", LW, T.T0, 0, C, [A("T0", 0, C)])
+    shifted("d_xs", "y", "R", 4 * C, T.x, 0, 4 * C, [])
+    dma("y", "d_w", T.QW[:, :].bitcast(dt.uint8), T.wc[:, :], writes=[A("QW", 0, 512)])
+    dma("y", "d_w", T.SW[:, :], T.ws[:, :], writes=[A("SW", 0, 512)])
+    close("d_w")
+    dma("y", "d_v", T.VT[:, :], T.v[:, :], writes=[A("VT", 0, 512)])
+    close("d_v")
+
+    cp(A("LNU", 0, 60), A("LN", 0, 60))
+    emit("v", V.tensor_copy, 1, IND(A("QQ", 0, 320), A("LNU", 0, 20)), A("IDT", 0, 320))
+    tt(A("VA", 0, 320), IND(A("ID5", 0, 320), A("LNU", 0, 20)), A("IDT", 0, 320), OP.add)
+    cp(A("LOF0", 0, 40), A("LN", 20, 60))
+    ts(A("LOF0", 40, 60), A("LN", 40, 60), 320, OP.add)
+    emit("v", V.tensor_copy, 1, IND(A("QQ", 320, 640), A("LNU", 20, 40)), A("VA", 0, 320))
+    ts(A("MASK", 0, 960), A("IQ", 0, 960), sc(0), OP.is_equal)
+    act(A("SEG", 0, 960), A("IQ", 0, 960), ActivationFunctionType.Sign)
+    ts(A("THR", 0, 64), A("GI", 0, 64), sc(1), OP.not_equal, 1.0e29, OP.mult)
+    ts(A("UL", 0, 8), ix(48, 56), sc(7), OP.add)
+    ts(A("UL", 2, 4), ix(48, 50), sc(8), OP.add)
+    ts(A("CLU", 0, 5), ix(36, 41), sc(11), OP.add)
+    for i, ws in enumerate(((1, 2, 4, 8), (16, 32, 0, 0), (-4, -2, -1, 32), (16, 8, 0, 0))):
+        for t in range(4):
+            act(A("KWT", 512 * i + t, 512 * i + 512, 4), A("MASK", 0, 128), scale=float(ws[t]))
+
+    def spread(out, in_, n):
+        emit("v", V.tensor_tensor_scan, 1, out, A("SEG", 0, n), in_, 0.0, OP.mult, OP.add)
+
+    off = {}
+    for buf, pairs in (
+        ("DF", [("ST", 80), ("BASE", 60), ("VV", 80), ("OR0", 20), ("OR1", 40), ("f0", 20), ("f1", 40), ("fB", 40), ("s12", 20), ("cnt", 20),
+                ("t1", 20), ("t2", 20), ("t3", 20), ("t4", 20), ("n2", 20), ("nb", 20), ("t6", 20), ("t7", 20),
+                ("X", 20), ("ZZ", 40), ("m1", 20), ("t9", 20), ("ta", 20), ("v1", 40), ("ne", 20), ("tb", 20), ("oe", 20), ("on", 20),
+                ("td", 20), ("te", 20), ("o1", 40), ("mz", 40), ("tf", 40), ("tg", 40), ("w", 40), ("my", 40), ("th", 40), ("ti", 40), ("v2", 40),
+                ("u1", 40), ("u2", 40), ("u3", 40), ("u4", 40), ("u5", 40), ("q3", 60), ("q4", 60)]),
+        ("DI", [("P", 120), ("k7", 20), ("KG", 60), ("gb", 60), ("c0x", 20), ("c0y", 20), ("c0z", 20), ("c1y", 20), ("yb1", 20), ("KO", 20),
+                ("a1", 60), ("a2", 60), ("pk", 20), ("pa", 20), ("pr", 20), ("pb", 20), ("RES", 40), ("RSM", 40)])):
+        at = 0
+        for n, w in pairs:
+            off[n] = (buf, at, w)
+            at += w
+
+    def d_(d, n, a=0, b=None):
+        buf, at, w = off[n]
+        return A("%s%d" % (buf, d), at + a, at + (w if b is None else b))
+
+    def statics(d):
+        D = lambda n, a=0, b=None: d_(d, n, a, b)
+        tt(A("MG", 0, 960), IND(A("QQ", 0, 640 if d == 0 else 1280), A("LOF%d" % d, 0, 60)), A("MASK", 0, 960), OP.mult)
+        spread(A("SN", 0, 960), A("MG", 0, 960), 960)
+        cp(D("pk"), A("SN", 655, 960, 16))
+        cp(A("LX%d" % d, 0, 40), A("SN", 15, 640, 16))
+        ts(D("ST", 0, 40), A("SN", 15, 640, 16), sc(12), OP.subtract)
+        ts(D("pa"), D("pk"), 511, OP.bitwise_and)
+        ts(D("pr"), D("pk"), 9, OP.logical_shift_right, 3, OP.bitwise_and)
+        ts(D("pb"), D("pk"), 11, OP.logical_shift_right)
+        cp(A("LX%d" % d, 40, 60), D("pa"))
+        ts(D("ST", 40, 60), D("pa"), sc(12), OP.subtract, LW, OP.add)
+        ts(D("q3", 0, 20), D("pr"), 1024, OP.mult, 320, OP.add)
+        ts(D("q4", 0, 20), D("pb"), sc(12), OP.subtract)
+        tt(D("ST", 60, 80), D("q3", 0, 20), D("q4", 0, 20), OP.add)
+        if d == 0:
+            ts(D("a1"), A("LN", 0, 60), 3, OP.bitwise_and)
+            ts(D("a2"), A("LN", 0, 60), 2, OP.logical_shift_right)
+            ts(D("q3"), D("a1"), 1024, OP.mult, 320, OP.add)
+            ts(D("q4"), D("a2"), sc(12), OP.subtract)
+            tt(D("BASE"), D("q3"), D("q4"), OP.add)
+        else:
+            for i in range(3):
+                cp(D("BASE", 20 * i, 20 * i + 20), d_(0, "BASE", 40 - 20 * i, 60 - 20 * i))
+        ts(D("VV", 60, 80), D("BASE", 40, 60), sc(4), OP.add)
+
+    def early(d):
+        D = lambda n, a=0, b=None: d_(d, n, a, b)
+        P = lambda r, k=1: d_(d, "P", 20 * r, 20 * r + 20 * k)
+        ops = [lambda r=r: ts(P(r), D("KO"), r, OP.logical_shift_right, LW, OP.bitwise_and) for r in range(6)]
+        return ops + [
+            lambda: ts(D("k7"), D("KO"), 7 * LW, OP.bitwise_and),
+            lambda: tt(D("s12"), P(1), P(2), OP.add),
+            lambda: ts(D("t2"), P(1), -3, OP.mult),
+            lambda: ts(D("t3"), P(0), -2, OP.mult),
+            lambda: ts(D("n2"), P(5), sc(4), OP.is_equal),
+            lambda: ts(D("fB", 0, 20), P(2), A("KC", 2, 3), OP.is_equal),
+            lambda: tt(D("cnt"), D("s12"), P(0), OP.add),
+            lambda: tt(D("VV", 0, 60), P(3, 3), D("BASE"), OP.add),
+            lambda: ts(D("f0"), D("k7"), A("KC", 0, 1), OP.is_equal),
+            lambda: ts(D("f1", 0, 20), D("s12"), A("KC", 1, 2), OP.is_equal),
+            lambda: ts(D("nb"), D("s12"), LW, OP.is_equal),
+            lambda: tt(D("t4"), D("t2"), D("t3"), OP.add),
+            lambda: ts(D("t1"), D("cnt"), -2, OP.mult),
+            lambda: ts(D("fB", 20, 40), P(5), sc(4), OP.not_equal),
+            lambda: tt(D("f1", 20, 40), D("n2"), D("nb"), OP.mult),
+            lambda: tt(D("OR1", 20, 40), D("t4"), sj(1), OP.add),
+            lambda: tt(D("OR0"), D("t1"), sj(0), OP.add),
+            lambda: tt(D("t6"), D("VV", 0, 20), D("OR0"), OP.subtract),
+            lambda: tt(D("t7"), D("t6"), D("f0"), OP.mult),
+            lambda: tt(D("OR1", 0, 20), D("t7"), D("OR0"), OP.add),
+        ]
+
+    def gather_k(d):
+        tt(A("MK", 0, 960), IND(A("KF%d" % d, 0, 320), A("LX%d" % d, 0, 60)), A("MASK", 0, 960), OP.mult)
+
+    def late(d):
+        D = lambda n, a=0, b=None: d_(d, n, a, b)
+        V1, x, z, y = D("VV", 20, 40), D("KG", 0, 20), D("KG", 20, 40), D("KG", 40, 60)
+        sh, an = OP.logical_shift_right, OP.bitwise_and
+        spread(A("SCK", 0, 960), A("MK", 0, 960), 960)
+        cp(D("KG"), A("SCK", 15, 960, 16))
+        ts(D("c0x"), x, 3, sh, LW, an)
+        ts(D("gb"), D("KG"), LW, an)
+        ts(D("yb1"), y, 1, sh, LW, an)
+        ts(D("c0y"), y, 3, sh, LW, an)
+        ts(D("c0z"), z, 3, sh, LW, an)
+        ts(D("c1y"), y, 4, sh, LW, an)
+        tt(D("m1"), D("c0x"), D("P", 80, 100), OP.is_equal)
+        tt(D("ne"), D("gb", 40, 60), D("yb1"), OP.not_equal)
+        ts(D("tb"), D("gb", 40, 60), -3, OP.mult)
+        for m, c in (("mz", "c0z"), ("my", "c1y")):
+            tt(D(m, 0, 20), D(c), D("P", 100, 120), OP.is_equal)
+            ts(D(m, 20, 40), D(c), sc(4), OP.is_equal)
+        tt(D("X"), D("ST", 0, 20), D("gb", 0, 20), OP.subtract)
+        for h in (0, 20):
+            tt(D("ZZ", h, h + 20), D("ST", 20, 40), D("gb", 20, 40), OP.subtract)
+        tt(D("oe"), D("tb"), D("ST", 40, 60), OP.add)
+        tt(D("on"), D("c0y"), D("ST", 60, 80), OP.add)
+        tt(D("t9"), D("X"), V1, OP.subtract)
+        tt(D("tf"), D("ZZ"), D("VV", 40, 80), OP.subtract)
+        tt(D("td"), D("on"), D("oe"), OP.subtract)
+        tt(D("ta"), D("t9"), D("m1"), OP.mult)
+        tt(D("tg"), D("tf"), D("mz"), OP.mult)
+        tt(D("te"), D("td"), D("ne"), OP.mult)
+        for h in (0, 20):
+            tt(D("v1", h, h + 20), D("ta"), V1, OP.add)
+        tt(D("w"), D("tg"), D("VV", 40, 80), OP.add)
+        for h in (0, 20):
+            tt(D("o1", h, h + 20), D("te"), D("oe"), OP.add)
+        tt(D("u1"), D("v1"), D("OR1"), OP.subtract)
+        tt(D("th"), D("o1"), D("w"), OP.subtract)
+        tt(D("u2"), D("u1"), D("f1"), OP.mult)
+        tt(D("ti"), D("th"), D("my"), OP.mult)
+        tt(D("u3"), D("u2"), D("OR1"), OP.add)
+        tt(D("v2"), D("ti"), D("w"), OP.add)
+        tt(D("u4"), D("v2"), D("OR1"), OP.subtract)
+        tt(D("u5"), D("u4"), D("fB"), OP.mult)
+        tt(D("RES"), D("u3"), D("u5"), OP.add)
+        ts(D("RSM"), D("RES"), 8 * LW - 1, an)
+        cp(A("LU%d" % d, 0, 40), D("RSM"))
+
+    def lookup(d, table, out, scalar_only=False):
+        a = (A(out, 0, 320), IND(A(table, 0, 8 * LW), A("LU%d" % d, 0, 20)))
+        if scalar_only:
+            act(*a)
+        else:
+            cp(*a)
+        act(A(out, 320, 640), IND(A(table, 0, 8 * LW), A("LU%d" % d, 20, 40)))
+
+    def offsets(out, d, flat, cm, cols):
+        n = cols // 16
+        tt(A("MG", 0, cols), IND(A(flat, 0, 640), A(cm, 0, n)), A("MASK", 0, cols), OP.mult)
+        spread(A("SN", 0, cols), A("MG", 0, cols), cols)
+        ts(d_(d, "u1", 0, n), A("SN", 15, cols, 16), sc(2), OP.subtract)
+        ts(d_(d, "u2", 0, n), d_(d, "u1", 0, n), 0.0, OP.is_lt, 8 * C, OP.mult)
+        tt(d_(d, "u3", 0, n), d_(d, "u1", 0, n), d_(d, "u2", 0, n), OP.add)
+        for t in (2, 3, 0, 1):
+            ts(A(out, 26 * t, 26 * t + n), d_(d, "u3", 0, n), 4, OP.mult, t, OP.add)
+
+    def pull(dst, offs, c0, c1):
+        for t in (2, 0, 3, 1):
+            a = (A(dst, 4 * c0 + t, 4 * c1, 4), IND(A("R", 0, W8), A(offs, 26 * t + c0 // 16, 26 * t + c1 // 16)))
+            if t >= 2:
+                act(*a)
+            else:
+                cp(*a)
+
+    def scores(src, first=None, second=None):
+        quant("QX", 0, ST, A(src, 0, 4 * ST))
+        for n, c0 in enumerate((0, 128, 192)):
+            mm(A("PS", 512 * n, 512 * n + 128), A("QX", c0, c0 + 128), A("SX", c0, c0 + 128), A("QUP", 0, 128), A("SUP", 0, 128))
+        if first:
+            first()
+        for n in range(3):
+            h = 16 if n == 2 else 0
+            for s in (0, 32):
+                o = 8 * s + 32 * n
+                tt(A("BT", o, o + 32 - h), A("PS", 512 * n + s + h, 512 * n + s + 32), A("THR", s + h, s + 32), OP.is_gt)
+        quant("QB", 0, 192, A("BT", 0, 768))
+        if second:
+            second()
+        for d in range(2):
+            for i in range(2):
+                k = 256 * d + 128 * i
+                mm(A("PS", 1536 + 2048 * d, 1664 + 2048 * d), A("QK", k, k + 128), A("SK", k, k + 128), A("QB", 64 * i, 64 * i + 128), A("SB", 64 * i, 64 * i + 128), i == 0, i == 1)
+        cp(A("KU0", 0, 20), A("PS", 1536, 1556))
+        ts(d_(0, "KO"), A("PS", 1536, 1556), LW, OP.mult)
+        act(A("KF0", 0, 320), IND(A("IDT", 0, 512), A("KU0", 0, 20)), scale=512.0)
+
+    def back_signs():
+        ts(A("KU1", 0, 20), A("PS", 3584, 3604), 7.0, OP.add)
+        ts(d_(1, "KO"), A("PS", 3584, 3604), 7, OP.add, LW, OP.mult)
+        act(A("KF1", 0, 320), IND(A("IDT", 0, 512), A("KU1", 0, 20)), scale=512.0)
+
+    statics(0)
+    quant("QU", 0, 128, A("UT", 0, 512))
+    emit("v", V.tensor_copy, 1, CW("QUP", 0, 128), IND(CW("QU", 0, 128), A("UL", 0, 8)))
+    act(A("SUP", 0, 128), IND(A("SU", 0, 128), A("UL", 0, 8)))
+    quant("QK", 0, 512, A("KWT", 0, 2048))
+    act(A("MF", 0, 320), A("IDT", 0, 320), scale=1025.0)
+
+    def inverse2():
+        emit("v", V.tensor_copy, 1, IND(A("QQ", 640, 960), A("LNU", 40, 60)), A("IDT", 0, 320))
+
+    def columns():
+        ts(A("ML", 0, 80), IND(A("QQ", 640, 960), A("CLU", 0, 5)), 320.0, OP.add)
+        ts(A("ML", 80, 160), IND(A("QQ", 0, 320), A("CLU", 0, 5)), 320.0, OP.add)
+        ts(A("ML", 160, 240), A("ML", 80, 160), 1024.0, OP.mult)
+        tt(A("MF", 320, 400), A("ML", 160, 240), A("ML", 0, 80), OP.add)
+        emit("v", V.tensor_copy, 1, IND(A("CF", 0, 400), A("PU", 0, 25)), A("MF", 0, 400))
+
+    scores("R", inverse2, columns)
+    tt(A("MG", 0, 400), A("CF", 0, 400), A("MASK", 0, 400), OP.mult)
+    spread(A("SN", 0, 400), A("MG", 0, 400), 400)
+    cp(ix(64, 89), A("SN", 15, 400, 16))
+    ts(ix(96, 121), ix(64, 89), 1023, OP.bitwise_and)
+    cp(A("CM0", 0, 25), ix(96, 121))
+
+    def statics_back():
+        tt(A("VA", 320, 640), IND(A("ID5", 0, 320), A("LNU", 40, 60)), A("IDT", 0, 320), OP.add)
+        for i, (k, o) in enumerate(((20, 640), (0, 640), (0, 960))):
+            ts(A("LOF1", 20 * i, 20 * i + 20), A("LN", k, k + 20), o, OP.add)
+        emit("v", V.tensor_copy, 1, IND(A("QQ", 960, 1280), A("LNU", 20, 40)), A("VA", 320, 640))
+        statics(1)
+        ts(ix(96, 121), ix(64, 89), 10, OP.logical_shift_right)
+        cp(A("CM1", 0, 25), ix(96, 121))
+        tt(A("MG", 0, 80), A("ML", 80, 160), A("MASK", 0, 80), OP.mult)
+        spread(A("SN", 0, 80), A("MG", 0, 80), 80)
+        cp(A("LTL", 0, 5), A("SN", 15, 80, 16))
+        quant("QV", 0, 128, A("VT", 0, 512))
+
+    quant("QE", 0, 512, A("ET", 0, 2048))
+
+    for r in range(STEPS):
+        HQ, HS = "HQ%d" % r, "HS%d" % r
+        peer = rank ^ MATES[r]
+        n_arr = sum(mask_of(topo, T.cores[peer] if c is None else c, core)[1] for c in hops(T, topo, peer, r))
+        arrives([A(HQ, 0, KX), A(HS, 0, KX)], "arr%d" % r, n_arr)
+        if r:
+            scores("XT")
+        own = early(0)
+        for f in own[:14]:
+            f()
+        gather_k(0)
+        for f in own[14:]:
+            f()
+        late(0)
+        lookup(0, "TN" if r else "T0", "FL0")
+        offsets("OFZ", 0, "FL0", "CM0", C)
+        pull("ZT", "OFZ", 0, 128)
+        quant("QS", 0, 128, A("ZT", 0, 512))
+        for k, c in enumerate(hops(T, topo, rank, r)):
+            to = T.cores[peer] if c is None else c
+            m, n = mask_of(topo, core, to)
+            if k == 0:
+                o = T[HQ if c is None else "QR"][:, 0:KX].bitcast(dt.uint8)
+                i, rd = T.QS[:, 0:KX].bitcast(dt.uint8), [A("QS", 0, KX)]
+            else:
+                o = T[HS if c is None else "SR"][:, 0:KX]
+                i, rd = T.SS[:, 0:KX], [A("SS", 0, KX)]
+            remote(o, i, rd, "arr%d" % r if c is None else "rarr", "snt%d" % r, topo.addr(to, core), m, n)
+        close("snt%d" % r)
+        pull("ZT", "OFZ", 128, C)
+        quant(HQ, KX, C, A("ZT", 4 * KX, 4 * C), HS)
+
+        def layer(c0, c1, m1, buf, w, meanwhile=()):
+            for b in range(4):
+                for n, p in (("W", 0), ("E", 2048)):
+                    mm(A("PS", p + 512 * b, p + 512 * b + m1), A("Q" + n, 128 * b, 128 * b + 128), A("S" + n, 128 * b, 128 * b + 128), A(HQ, c0, c0 + m1), A(HS, c0, c0 + m1))
+            for b in range(4):
+                l = A(buf, w * b, w * b + c1 - c0)
+                act(l, A("PS", 512 * b, 512 * b + c1 - c0), RELU, scale=0.015625)
+                k = 5 if b else 12
+                for f in meanwhile[:k]:
+                    f()
+                meanwhile = meanwhile[k:]
+                tt(A("R", 4 * c0 + b, 4 * c1, 4), l, A("PS", 2048 + 512 * b, 2048 + 512 * b + c1 - c0), OP.add)
+            for f in meanwhile:
+                f()
+
+        back_signs()
+        layer(KX, C, C - KX, "RL", 304, early(1) if r else [])
+        shifted("d_ye%d" % r, "y", "R", 4 * C, T.R, 4 * KX, 4 * C, [A("R", 4 * KX, 4 * C)])
+        if r == 0:
+            statics_back()
+            for f in early(1):
+                f()
+        gather_k(1)
+        layer(0, KX, 128, "RL2", 128)
+        shifted("d_yl%d" % r, "sy", "R", 4 * C, T.R, 0, 4 * KX, [A("R", 0, 4 * KX)])
+        late(1)
+        lookup(1, "T0", "FL1")
+        cols = ST if r < STEPS - 1 else C
+        offsets("OFX", 1, "FL1", "CM1", cols)
+        if r < STEPS - 1:
+            act(A("TN", 0, ST), A("FL1", 0, ST))
+            act(A("TN", ST, C), IND(A("FL1", 0, 640), A("LTL", 0, 5)))
+            shifted("d_tn%d" % r, "y", "TN", LW, T.TN, 0, C, [A("TN", 0, C)])
+        else:
+            lookup(0, "T0", "FLO", True)
+            act(A("OPF", 0, C), IND(A("FLO", 0, 640), A("CM0", 0, 25)))
+            for k in range(8):
+                dma("y", "d_op", T.op[k:k + 1, :], T.OPF[16 * k:16 * k + 1, :], reads=[A("OPF", 0, C)])
+            close("d_op")
+        pull("XT", "OFX", 0, cols)
+
+    quant("QX", 0, C, A("XT", 0, 4 * C))
+    mm(A("PS", 0, C), A("QV", 0, 128), A("SV", 0, 128), A("QX", 0, C), A("SX", 0, C))
+    dma("s", "d_out", T.oc[:, :], T.QX[:, :].bitcast(dt.uint8), reads=[A("QX", 0, C)])
+    for k in range(4):
+        dma("y", "d_out", T.osc[4 * k:4 * k + 4, :], T.SX[32 * k:32 * k + 4, :], reads=[A("SX", 0, C)])
+    cp(A("YO", 0, C), A("PS", 0, C))
+    dma("y", "d_out", T.y[:, :], T.YO[:, :], reads=[A("YO", 0, C)])
+    close("d_out")
+    finish()

@@ -5,46 +5,53 @@ MATES = [1, 2, 4]
 W8 = 8 * 4 * C
 LW = 512
 OP = AluOpType
-COPY, RELU = ActivationFunctionType.Copy, ActivationFunctionType.Relu
+ACT = ActivationFunctionType
 CODES = "float8_e4m3fn_x4"
+NK = 7
+LEVEL, NEVER = 24 * LW, 512 * LW
 
-SCRATCH = {
-    "R": ("sbuf", [128, W8], "bfloat16"), "XT": ("sbuf", [128, 4 * C], "bfloat16"), "ZT": ("sbuf", [128, 4 * C], "bfloat16"),
-    "UT": ("sbuf", [128, 512], "bfloat16"), "VT": ("sbuf", [128, 512], "bfloat16"),
-    "ET": ("sbuf", [128, 2048], "bfloat16"), "ONE": ("sbuf", [128, 512], "bfloat16"),
-    "KWT": ("sbuf", [128, 2048], "bfloat16"), "BT": ("sbuf", [128, 768], "bfloat16"),
-    "LP": ("sbuf", [128, 25], "int32"), "LN": ("sbuf", [128, 60], "int32"),
-    "PU": ("sbuf", [128, 26], "uint16"), "LNU": ("sbuf", [128, 60], "uint16"),
-    "LOF0": ("sbuf", [128, 60], "uint16"), "LOF1": ("sbuf", [128, 60], "uint16"),
-    "LX0": ("sbuf", [128, 60], "uint16"), "LX1": ("sbuf", [128, 60], "uint16"),
-    "CM0": ("sbuf", [128, 26], "uint16"), "CM1": ("sbuf", [128, 26], "uint16"), "LTL": ("sbuf", [128, 6], "uint16"),
-    "UL": ("sbuf", [128, 8], "uint16"), "CLU": ("sbuf", [128, 6], "uint16"),
-    "KU0": ("sbuf", [128, 20], "uint16"), "KU1": ("sbuf", [128, 20], "uint16"),
-    "LU0": ("sbuf", [128, 40], "uint16"), "LU1": ("sbuf", [128, 40], "uint16"),
-    "OFZ": ("sbuf", [128, 104], "uint16"), "OFX": ("sbuf", [128, 104], "uint16"),
-    "IQ": ("sbuf", [128, 960], "bfloat16"), "MASK": ("sbuf", [128, 960], "bfloat16"), "SEG": ("sbuf", [128, 960], "bfloat16"),
-    "IDT": ("sbuf", [128, 512], "float32"), "ID5": ("sbuf", [128, 320], "float32"), "GI": ("sbuf", [128, 64], "bfloat16"),
-    "THR": ("sbuf", [128, 64], "float32"), "IDX": ("sbuf", [128, 128], "int32"), "SC": ("sbuf", [128, 24], "float32"),
-    "SJ": ("sbuf", [128, 60], "float32"), "KC": ("sbuf", [128, 3], "float32"),
-    "QQ": ("sbuf", [128, 1280], "float32"), "VA": ("sbuf", [128, 640], "float32"), "MF": ("sbuf", [128, 400], "float32"), "ML": ("sbuf", [128, 240], "float32"),
-    "CF": ("sbuf", [128, 400], "float32"), "MG": ("sbuf", [128, 960], "float32"), "SN": ("sbuf", [128, 960], "float32"),
-    "KF0": ("sbuf", [128, 320], "bfloat16"), "KF1": ("sbuf", [128, 320], "bfloat16"),
-    "MK": ("sbuf", [128, 960], "bfloat16"), "SCK": ("sbuf", [128, 960], "bfloat16"),
-    "DF0": ("sbuf", [128, 2048], "float32"), "DF1": ("sbuf", [128, 2048], "float32"),
-    "DI0": ("sbuf", [128, 704], "int32"), "DI1": ("sbuf", [128, 704], "int32"),
-    "T0": ("sbuf", [128, 8 * LW], "float32"), "TN": ("sbuf", [128, 8 * LW], "float32"),
-    "FL0": ("sbuf", [128, 640], "float32"), "FL1": ("sbuf", [128, 640], "float32"), "FLO": ("sbuf", [128, 640], "float32"),
-    "OPF": ("sbuf", [128, 400], "float32"), "RL": ("sbuf", [128, 1216], "float32"), "RL2": ("sbuf", [128, 512], "float32"), "YO": ("sbuf", [128, 400], "float32"),
-    "PS": ("psum", [128, 4096], "float32"),
-}
-for _n, _w in (("U", 128), ("UP", 128), ("V", 128), ("W", 512), ("E", 512), ("K", 512), ("B", 192), ("X", C), ("S", 128), ("R", KX)):
+G2, G1B, G1A, EX, E1, E0, NE = 11, 12, 13, 15, 17, 19, 21
+FIELDS = [(0, 1, (G2, E1, NE)), (1, 3, (G2, E1)), (3, 1, (G2, E0)), (4, 1, (G2,)), (5, 1, (G1B, G1A, EX)), (6, 1, (G1B, G1A)), (7, 7, ())]
+EXTRA = (2 ** NE + 2 ** G2, 2 ** NE + 2 ** G1A)
+OWN, RZ, RY, RX = 0, 1, 2, 3
+B0, B1, B2, C0, C1, C2 = range(6)
+WEIGHTS = [
+    [(OWN, B0, 0, 48, 1, -256), (OWN, B1, 8, 16, 1, 640), (OWN, B2, 8, 16, 1, 0), (OWN, C0, 0, 8, 1, 32), (OWN, C0, 1, 7, 5, 0),
+     (OWN, C1, 0, 16, 1, 64), (OWN, C2, 0, 8, 1, 16), (OWN, C2, 8, 16, 2, -2 ** G2), (OWN, C2, 9, 16, 2, 2 ** G2),
+     (OWN, 8 + B0, 0, 4, 1, -2 ** EX), (OWN, 8 + B0, 4, 8, 1, 2 ** EX), (OWN, 8 + B0, 1, 7, 5, 0),
+     (OWN, 8 + B1, 0, 32, 1, 2 ** G1A), (OWN, 8 + B1, 0, 4, 1, -2 ** G1A),
+     (OWN, 8 + B2, 1, 4, 1, -2 ** G1B), (OWN, 8 + B2, 4, 7, 1, 2 ** G1B), (OWN, 8 + B2, 0, 1, 1, 2 ** G2), (OWN, 8 + B2, 7, 8, 1, -2 ** G2)],
+    [(OWN, 8 + C1, 8, 16, 1, 2 ** EX), (OWN, 8 + C1, 1, 7, 5, 2 ** EX), (OWN, 8 + C2, 0, 8, 1, 2 ** E1 + 2 ** E0),
+     (RX, B0, 8, 16, 1, -32), (RX, B0, 1, 7, 5, -32), (RX, 8 + C0, 8, 16, 1, 2 ** EX), (RX, 8 + C0, 1, 7, 5, 2 ** EX),
+     (RZ, C0, 0, 16, 1, 1), (RZ, B0, 0, 16, 1, -6), (RZ, 8 + B0, 0, 32, 1, 2 ** NE),
+     (RZ, 8 + C1, 0, 16, 1, 2 ** E1), (RZ, 8 + C1, 9, 16, 2, -2 ** E1),
+     (RY, B0, 0, 16, 1, -8), (RY, 8 + C0, 0, 16, 1, 2 ** E0), (RY, 8 + C0, 9, 16, 2, -2 ** E0)],
+]
+
+F32, B16, I32, U16 = "float32", "bfloat16", "int32", "uint16"
+SCRATCH = {}
+for _t, _l in (
+    (B16, (("R", W8), ("XT", 4 * C), ("ZT", 4 * C), ("UT", 512), ("VT", 512), ("ET", 1040), ("ONE", 520), ("WT", 1024), ("KW", 1056), ("MM", 32),
+           ("BT0", 592), ("BT1", 592), ("SG0", ST), ("SG1", ST), ("IQ", C), ("IQ4", C), ("M16", C), ("S16", 480), ("M4", C), ("S4", C), ("JK", 64))),
+    (I32, (("LP", 25), ("LN", 60), ("IDX", 160), ("KI0", 40), ("KI1", 40), ("KC0", 280), ("KC1", 280), ("RS0", 80), ("RS1", 80))),
+    (U16, (("PU", 26), ("LNU", 60), ("LC0", 20), ("LC1", 20), ("LB0", 20), ("LB1", 20), ("CL", 10), ("RL0", 10), ("RL1", 10), ("WL", 16), ("KL", 8),
+           ("UL", 16), ("CLU", 6), ("CM0", 26), ("CM1", 26), ("LTL", 6), ("LU0", 40), ("LU1", 40), ("OFZ", 100), ("OFX", 100))),
+    (F32, (("TAB", 720), ("SC", 32), ("CC", 4), ("WG", 256), ("WS", 256), ("QQ", 1280), ("VA", ST), ("FT", ST), ("MG", 480), ("SN", 480),
+           ("MG1", C), ("SN1", C), ("UO", 200), ("UO1", 200), ("WN", 20), ("SRC", 80), ("SRG", 80), ("BG", 100), ("TM", 80), ("RAW0", 280), ("RAW1", 280),
+           ("D0", 280), ("D1", 280), ("KF0", 280), ("KF1", 280), ("SK0", 280), ("SK1", 280), ("MF", C), ("ML", 240), ("CF", C),
+           ("T0", 8 * LW), ("TN", 8 * LW), ("FL0", 640), ("FL1", 640), ("FLO", 640), ("OPF", C), ("RA", 512), ("RB", 704), ("RC", 512), ("YO", C))),
+):
+    for _n, _w in _l:
+        SCRATCH[_n] = ("sbuf", [128, _w], _t)
+SCRATCH["PS"] = ("psum", [128, 4096], F32)
+for _n, _w in (("U", 128), ("UP", 256), ("V", 128), ("W", 512), ("E", 512), ("K", 264), ("B0", 148), ("B1", 148), ("X", C), ("S", 128), ("R", KX)):
     SCRATCH["Q" + _n] = ("sbuf", [128, _w], CODES)
     SCRATCH["S" + _n] = ("sbuf", [128, _w], "uint8")
 for _r in range(STEPS):
     SCRATCH["HQ%d" % _r] = ("sbuf", [128, C], CODES)
     SCRATCH["HS%d" % _r] = ("sbuf", [128, C], "uint8")
-DMAS = ["d_ln", "d_p", "d_u", "d_x", "d_xs", "d_v", "d_w", "d_t0", "d_tn0", "d_tn1", "d_out", "d_op"]
-DMAS += ["d_%s%d" % (k, r) for k in ("ye", "yl") for r in range(STEPS)]
+DMAS = ["d_ln", "d_p", "d_u", "d_x", "d_xs", "d_v", "d_w", "d_t0", "d_tn0", "d_tn1", "d_out", "d_op", "d_s0", "d_s1"]
+DMAS += ["d_%s%d" % (k, r) for k in ("ya", "yb", "yl") for r in range(STEPS)]
 SEMAPHORES = ["ev", "es", "et", "eg", "rarr", "rsent"] + DMAS + ["arr%d" % r for r in range(STEPS)] + ["snt%d" % r for r in range(STEPS)]
 
 
@@ -82,8 +89,8 @@ def relay(g, core, T, topo):
             g.wait_ge(T.sem.rsent, n * len(jobs))
 
 
-def A(name, a, b, s=1):
-    return ("A", name, a, b, s)
+def A(name, a, b, s=1, p=(0, 128)):
+    return ("A", name, a, b, s, p)
 
 
 def IND(win, off):
@@ -91,7 +98,7 @@ def IND(win, off):
 
 
 def CW(name, a, b):
-    return ("C", name, a, b, 1)
+    return ("C", name, a, b, 1, (0, 128))
 
 
 def is_ap(x):
@@ -105,20 +112,20 @@ def builder(g, T):
 
     def ap(x):
         if x[0] == "A":
-            _, n, a, b, s = x
-            return T[n][:, a:b] if s == 1 else T[n][:, a:b:s]
+            _, n, a, b, s, p = x
+            return T[n][p[0]:p[1], a:b] if s == 1 else T[n][p[0]:p[1], a:b:s]
         if x[0] == "C":
             return T[x[1]][:, x[2]:x[3]].bitcast(dt.uint32)
         return ap(x[1]).indirect(ap(x[2]))
 
     def region(x):
-        _, n, a, b, s = x
+        _, n, a, b, s, p = x
         if n == "PS":
-            return n, (a // 512 * 512, (b + 511) // 512 * 512, 1)
-        return n, (a, b, s)
+            return n, (a // 512 * 512, (b + 511) // 512 * 512, 1, p)
+        return n, (a, b, s, p)
 
     def meet(p, q):
-        if p[1] <= q[0] or q[1] <= p[0]:
+        if p[1] <= q[0] or q[1] <= p[0] or p[3][1] <= q[3][0] or q[3][1] <= p[3][0]:
             return False
         return not (p[2] == q[2] > 1 and (p[0] - q[0]) % p[2])
 
@@ -147,7 +154,7 @@ def builder(g, T):
         for x, w in [(r, False) for r in reads] + [(r, True) for r in writes]:
             n, reg = region(x)
             h = hist.setdefault(n, [])
-            if w and reg[2] == 1:
+            if w and reg[2] == 1 and reg[3] == (0, 128):
                 h[:] = [e for e in h if not (reg[0] <= e[0][0] and e[0][1] <= reg[1])]
             h[:] = [e for e in h if not (e[0] == reg and e[1] == w and e[3] == q and e[2][0] == ev[0])]
             h.append((reg, w, ev, q))
@@ -160,7 +167,8 @@ def builder(g, T):
         return out
 
     def emit(q, fn, nout, *args, acc=False, **kw):
-        writes, reads = [], parts(args[nout:]) + parts(kw.values())
+        writes = parts([kw.get("accum_out")])
+        reads = parts(args[nout:]) + parts(x for k, x in kw.items() if k != "accum_out")
         for x in args[:nout]:
             if x[0] == "I":
                 writes.append(("A",) + x[1][1:])
@@ -222,6 +230,7 @@ def rank_program(g, core, T, topo):
         return
     emit, dma, close, remote, arrives, finish = builder(g, T)
     V, S = g.vector, g.scalar
+    sh, an = OP.logical_shift_right, OP.bitwise_and
 
     def ts(out, x, s1, op0, s2=None, op1=None):
         if op1 is None:
@@ -235,14 +244,24 @@ def rank_program(g, core, T, topo):
     def cp(out, x):
         emit("v", V.tensor_copy, 1, out, x)
 
-    def act(out, x, func=COPY, **kw):
+    def fill(out, k):
+        emit("v", V.memset, 1, out, k)
+
+    def act(out, x, func=ACT.Copy, **kw):
         emit("s", S.activation, 1, out, x, func, **kw)
+
+    def plus(out, x, k):
+        act(out, x, ACT.Identity, bias=k)
 
     def quant(n, a, b, x, sn=None):
         emit("v", V.quantize_mx, 2, A(n, a, b), A(sn or "S" + n[1:], a, b), x)
 
-    def mm(out, l, ls, r, rs, start=True, stop=True):
-        emit("t", g.tensor.matmul_mx, 1, out, l, ls, r, rs, start, stop, acc=not start)
+    def mm(bank, l, a, r, b, n, start=True, stop=True, rs=None):
+        emit("t", g.tensor.matmul_mx, 1, A("PS", 512 * bank, 512 * bank + n), A("Q" + l, a, a + 128), A("S" + l, a, a + 128),
+             A(r, b, b + n), A(rs or "S" + r[1:], b, b + n), start, stop, acc=not start)
+
+    def ps(bank, a, b):
+        return A("PS", 512 * bank + a, 512 * bank + b)
 
     def iota(out, pattern, base, cm, whole=False):
         if whole:
@@ -250,14 +269,18 @@ def rank_program(g, core, T, topo):
         else:
             emit("g", g.iota, 1, out, pattern, base, cm, allow_small_or_imprecise_dtypes=True)
 
-    def sc(i):
-        return A("SC", i, i + 1)
+    def scan(out, d0, d1, op0=OP.mult, op1=OP.add):
+        emit("v", V.tensor_tensor_scan, 1, out, d0, d1, 0.0, op0, op1)
+
+    names = ["i", "g", "s", "q", "i4", "g1600", "off", "s4", "cl", "kl", "ul0", "ul1", "clu", "cg", "cgp", "a", "a1", "a02", "c4", "c5",
+             "fs", "fb", "t0", "t1", "t2", "t3"]
+
+    def sc(n):
+        k = names.index(n)
+        return A("SC", k, k + 1)
 
     def ix(a, b):
         return A("IDX", a, b)
-
-    def sj(i):
-        return A("SJ", 20 * i, 20 * i + 20)
 
     def shifted(sem, queues, name, width, src, a, b, reads):
         n = 0
@@ -269,297 +292,273 @@ def rank_program(g, core, T, topo):
         close(sem)
 
     for k in range(8):
-        dma("sy"[k % 2], "d_ln", T.LN[16 * k:16 * k + 16, :], T.ln[:, :], writes=[A("LN", 0, 60)])
+        dma("ys"[k % 2], "d_ln", T.LN[16 * k:16 * k + 16, :], T.ln[:, :], writes=[A("LN", 0, 60)])
     close("d_ln")
-    dma("s", "d_p", T.LP[:, :], T.p[:, :], writes=[A("LP", 0, 25)])
+    dma("y", "d_p", T.LP[:, :], T.p[:, :], writes=[A("LP", 0, 25)])
     close("d_p")
     dma("y", "d_u", T.UT[:, :], T.u[:, :], writes=[A("UT", 0, 512)])
     close("d_u")
     dma("y", "d_x", T.R[:, 0:4 * C], T.x[:, :], writes=[A("R", 0, 4 * C)])
     close("d_x")
+    shifted("d_xs", "y", "R", 4 * C, T.x, 0, 4 * C, [])
 
     iota(ix(0, 1), [[0, 1]], 0, 1, True)
-    iota(A("GI", 0, 64), [[0, 2], [1, 8], [0, 4]], 0, 0)
-    iota(ix(16, 36), [[16, 20]], 0, 0, True)
-    iota(ix(36, 41), [[64, 5]], 0, 0, True)
-    iota(ix(48, 56), [[0, 8]], 0, 0, True)
-    iota(A("IDT", 0, 512), [[1, 512]], 0, 0)
-    iota(A("ID5", 0, 320), [[512, 320]], 0, 0)
-    iota(A("IQ", 0, 960), [[0, 60], [1, 16]], 0, 0)
-    for i, k in enumerate((1536.0, -512.0, 512.0)):
-        emit("v", V.memset, 1, A("KC", i, i + 1), k)
-    iota(A("ONE", 0, 512), [[0, 512]], 1, 0)
-    iota(A("BT", 0, 768), [[0, 768]], 0, 0)
-    for i, seq in enumerate((((16, -1), (32, 7), (48, -1), (80, 0), (96, -1), (112, 4)), ((16, 2), (32, -1), (96, 0), (112, -1)), ((16, -1), (112, 0)))):
-        for p0, k in seq:
-            emit("g", g.affine_select, 1, A("KC", i, i + 1), A("KC", i, i + 1), [[0, 1]], OP.is_gt, 512.0 * k, p0, -1)
-    for b in range(4):
-        emit("g", g.affine_select, 1, A("ET", 512 * b, 512 * b + 512), A("ONE", 0, 512), [[-1, 512]], OP.is_equal, 0.0, b, 4)
+    iota(A("TAB", 0, C), [[1, C]], 0, 0)
+    iota(A("TAB", C, C + ST), [[1, 80], [1024, 4]], ST, 0)
+    iota(A("IQ", 0, C), [[0, 25], [1, 16]], 0, 0)
+    iota(ix(16, 32), [[1, 16]], 0, 16, True)
+    iota(ix(32, 42), [[8, 2], [64, 5]], 0, 0, True)
+    iota(ix(42, 62), [[16, 20]], 0, 0, True)
+    iota(A("MM", 0, 32), [[1, 8], [-1, 4]], 0, 0)
+    iota(ix(62, 70), [[8, 2], [256, 4]], 0, 16, True)
+    iota(ix(70, 75), [[64, 5]], 0, 0, True)
+    iota(A("IQ4", 0, C), [[0, 100], [1, 4]], 0, 0)
     for n in ("T0", "TN"):
         for k in range(8):
             iota(A(n, LW * k + C, LW * k + LW), [[0, LW - C]], 0, 0)
+    iota(A("ONE", 0, 520), [[0, 520]], 1, 0)
+    for h in range(2):
+        emit("g", g.affine_select, 1, A("ET", 520 * h, 520 * h + 520), A("ONE", 0, 520), [[-1, 520]], OP.is_equal, 0.0, 2 + h, 4)
 
-    ts(ix(1, 2), ix(0, 1), 15, OP.bitwise_and)
-    ts(ix(2, 3), ix(0, 1), 4, OP.logical_shift_right)
-    ts(ix(3, 4), ix(0, 1), 5, OP.logical_shift_right)
-    ts(ix(4, 5), ix(0, 1), 3, OP.bitwise_and)
-    ts(ix(5, 6), ix(0, 1), 4, OP.logical_shift_right, 1, OP.bitwise_and)
-    cp(sc(0), ix(1, 2))
-    cp(sc(1), ix(2, 3))
-    ts(sc(2), ix(2, 3), 400, OP.mult)
-    ts(sc(4), ix(5, 6), LW, OP.mult)
-    ts(sc(12), ix(2, 3), LW, OP.mult, -8192, OP.add)
-    cp(sc(9), ix(3, 4))
-    ts(sc(5), ix(4, 5), 3, OP.is_equal, -47, OP.mult)
-    ts(sc(6), ix(4, 5), 16, OP.mult)
-    tt(sc(7), sc(6), sc(5), OP.add)
-    ts(sc(8), sc(6), 17, OP.add)
-    ts(sc(10), sc(0), 4, OP.mult)
-    tt(sc(11), sc(10), sc(9), OP.add)
-    ts(sj(2), ix(16, 36), sc(0), OP.add)
-    ts(sj(0), sj(2), 9728, OP.add)
-    ts(sj(1), sj(2), sc(12), OP.subtract, 1024, OP.add)
+    fill(A("WT", 0, 1024), 0.0)
+    fill(A("JK", 0, 64), 0.0)
+    for q, row, a, b, s, w in WEIGHTS[1]:
+        o = 256 * q + 16 * row
+        plus(A("WT", o + a, o + b, s), A("JK", 0, len(range(a, b, s))), float(w))
+    for q, row, a, b, s, w in WEIGHTS[0]:
+        o = 256 * q + 16 * row
+        fill(A("WT", o + a, o + b, s), float(w))
+
+    P = ix(0, 1)
+    for k, (s, m) in enumerate(((0, 15), (4, 7), (4, 1), (5, 3), (2, 3), (0, 3), (0, 7))):
+        ts(ix(1 + k, 2 + k), P, s, sh, m, an)
+    cp(A("SC", 0, 5), ix(1, 6))
+    R3, R7 = ix(6, 7), ix(7, 8)
+    cp(A("LNU", 0, 60), A("LN", 0, 60))
+    ts(sc("cg"), sc("g"), -LW, OP.mult, 8 * LW, OP.add)
+
+    def inverse(i):
+        cp(IND(A("QQ", ST * i, ST * i + ST), A("LNU", 20 * i, 20 * i + 20)), A("TAB", 0, ST))
+
+    def lists(d):
+        i0, i2 = (0, 40) if d == 0 else (40, 0)
+        ts(A("LC%d" % d, 0, 20), ix(42, 62), sc("i"), OP.add)
+        ts(A("LC%d" % d, 0, 20, p=(0, 32)), A("LN", i0, i0 + 20, p=(0, 32)), C, OP.add)
+        act(A("VA", 0, ST), IND(A("TAB", 0, 720), A("LC%d" % d, 0, 20)))
+        ts(A("LB%d" % d, 0, 20, p=(0, 64)), A("LN", i2, i2 + 20, p=(0, 64)), ST, OP.add)
+        cp(A("LB%d" % d, 0, 20, p=(64, 96)), A("LN", i2, i2 + 20, p=(64, 96)))
+        cp(A("LB%d" % d, 0, 20, p=(96, 128)), A("LN", 20, 40, p=(96, 128)))
+
+    def tables(d):
+        win = A("QQ", 640 * d, 640 * d + 640)
+        cp(IND(A("QQ", 640 * d + ST, 640 * d + 640), A("LNU", 20, 40)), A("VA", 0, ST))
+        act(A("FT", 0, ST), IND(win, A("LB%d" % d, 0, 20)))
+        tt(A("MG", 0, ST), IND(win, A("LB%d" % d, 0, 20)), A("M16", 0, ST), OP.mult)
+        scan(A("SN", 0, ST), A("S16", 0, ST), A("MG", 0, ST))
+        cp(A("WN", 0, 20), A("SN", 15, ST, 16))
+        for a in range(4):
+            for b in range(4):
+                dma("sy"[b % 2], "d_s%d" % d, T.SRC[32 * b:32 * b + 32, 20 * a:20 * a + 20], T.WN[32 * a:32 * a + 32, :],
+                    reads=[A("WN", 0, 20)], writes=[A("SRC", 0, 80)])
+        close("d_s%d" % d)
+        tt(A("MG", ST, 480), IND(A("FT", 0, ST), A("CL", 0, 10)), A("M16", 0, 160), OP.mult)
+        scan(A("SN", ST, 480), A("S16", 0, 160), A("MG", ST, 480))
+        cp(A("RL%d" % d, 0, 10, p=(0, 32)), A("CL", 0, 10, p=(0, 32)))
+        cp(A("RL%d" % d, 0, 10, p=(32, 64)), A("SN", ST + 15, 480, 16, p=(32, 64)))
+        cp(A("RL%d" % d, 0, 10, p=(64, 128)), A("SN", ST + 15, 480, 16, p=(64, 128)))
+
+    def candidates(d):
+        i0, i2 = (0, 40) if d == 0 else (40, 0)
+        raw = lambda k, h: A("RAW%d" % d, 140 * h + k, 140 * h + 140, NK)
+        src = lambda q: A("SRG", 20 * q, 20 * q + 20)
+        plus(A("SRG", 0, 80), A("SRC", 0, 80), sc("cg"))
+        for h in range(2):
+            plus(raw(0, h), src(OWN), 0.0)
+            plus(raw(1, h), src(RZ), float(LEVEL + 6 * LW))
+            plus(raw(2, h), src(RY), float(2 * LEVEL + 7 * LW))
+        plus(raw(4, 1), src(RX), float(4 * LEVEL + 7 * LW))
+        ts(raw(3, 0), A("BG", i2, i2 + 20), 3 * LEVEL, OP.add)
+        ts(raw(3, 1), A("BG", i2, i2 + 20), sc("cgp"), OP.add)
+        ts(raw(5, 0), A("BG", 20, 40), sc("c5"), OP.add)
+        ts(raw(5, 1), A("BG", 20, 40), 5 * LEVEL, OP.add)
+        ts(raw(6, 0), A("BG", 60, 80), 6 * LEVEL + 13 * LW, OP.add)
+        ts(raw(6, 1), A("BG", 80, 100), 6 * LEVEL, OP.add)
+        ts(A("TM", 0, 20), A("BG", i0, i0 + 20), sc("a02"), OP.mult, sc("c4"), OP.add)
+        ts(A("TM", 20, 40), src(RX), sc("a1"), OP.mult)
+        tt(raw(4, 0), A("TM", 0, 20), A("TM", 20, 40), OP.add)
+        tt(A("D%d" % d, 1, 280), A("RAW%d" % d, 0, 279), A("RAW%d" % d, 1, 280), OP.subtract)
+        fill(A("D%d" % d, 0, 280, NK), 1.0e12)
+
+    lists(0)
+    inverse(0)
+    ts(A("M16", 0, C), A("IQ", 0, C), sc("i"), OP.is_equal)
+    act(A("S16", 0, C), A("IQ", 0, C), ACT.Sign)
+    ts(sc("s4"), sc("s"), 4, OP.mult)
+    ts(sc("t0"), sc("i4"), 16, OP.mult, sc("s4"), OP.add)
+    ts(sc("cl"), R3, sc("t0"), OP.add)
+    ts(A("CL", 0, 10), ix(32, 42), sc("cl"), OP.add)
+    tables(0)
+
+    ts(ix(80, 96), ix(16, 32), 1023, an)
+    ts(ix(96, 112), ix(80, 96), 8, sh, 0, sh)
+    ts(sc("t1"), sc("q"), 256, OP.mult)
+    ts(ix(112, 128), ix(16, 32), 255, an)
+    ts(A("WL", 0, 16), ix(112, 128), sc("t1"), OP.add)
+    tt(A("WG", 0, 256), IND(A("WT", 0, 1024), A("WL", 0, 16)), A("M16", 0, 256), OP.mult)
+    scan(A("WS", 0, 256), A("S16", 0, 256), A("WG", 0, 256))
+    ts(A("MM", 0, 32), A("MM", 0, 32), sc("s4"), OP.is_equal)
+    fill(A("KW", 0, 1056), 0.0)
+    for k in range(16):
+        act(A("KW", 32 + 64 * k, 64 + 64 * k), A("MM", 0, 32), scale=A("WS", 16 * k + 15, 16 * k + 16))
+    ts(sc("kl"), sc("g"), -255, OP.mult)
+    ts(A("KL", 0, 8), ix(62, 70), sc("kl"), OP.add)
+    for f in range(2):
+        w = IND(A("WT", 0, 1024), A("KL", 4 * f, 4 * f + 4))
+        act(A("WG", 0, 64), w, ACT.Relu, scale=-1.0, accum_out=sc("t%d" % (2 + f)))
+        plus(A("CC", f, f + 1), sc("t%d" % (2 + f)), float(EXTRA[f]))
+
+    quant("QU", 0, 128, A("UT", 0, 512))
+    ts(sc("t0"), R7, 2.5, OP.is_gt)
+    ts(sc("t1"), R7, 5.5, OP.is_gt, sc("t0"), OP.add)
+    ts(sc("a"), R7, 16, OP.mult)
+    ts(sc("ul0"), sc("t1"), -47, OP.mult, sc("a"), OP.add)
+    ts(sc("ul1"), sc("t1"), 49, OP.mult, sc("a"), OP.subtract)
+    ts(A("UL", 0, 8), A("JK", 0, 8), sc("ul0"), OP.add)
+    ts(A("UL", 8, 16), A("JK", 0, 8), sc("ul1"), OP.add, 32, OP.add)
+    for d in range(2):
+        cp(CW("QUP", 128 * d, 128 * d + 128), IND(CW("QU", 0, 128), A("UL", 8 * d, 8 * d + 8)))
+        act(A("SUP", 128 * d, 128 * d + 128), IND(A("SU", 0, 128), A("UL", 8 * d, 8 * d + 8)))
+    ts(sc("fs"), sc("t0"), 2, OP.mult, -1, OP.add)
+    ts(sc("fb"), sc("fs"), -0.5, OP.mult)
+    for d in range(2):
+        fill(A("BT%d" % d, 0, 592), 0.0)
+        quant("QB%d" % d, 20, 148, A("BT%d" % d, 80, 592))
+    fill(A("ZT", 4 * KX, 512), 0.0)
+    quant("QK", 0, 264, A("KW", 0, 1056))
 
     cp(A("PU", 0, 25), A("LP", 0, 25))
-    act(A("T0", 0, C), IND(A("IDT", 0, 512), A("PU", 0, 25)), ActivationFunctionType.Identity, bias=sc(2))
+    ts(sc("g1600"), sc("g"), 4 * C, OP.mult)
+    act(A("T0", 0, C), IND(A("TAB", 0, C), A("PU", 0, 25)), ACT.Identity, bias=sc("g1600"), scale=4.0)
     shifted("d_t0", "y", "T0", LW, T.T0, 0, C, [A("T0", 0, C)])
-    shifted("d_xs", "y", "R", 4 * C, T.x, 0, 4 * C, [])
     dma("y", "d_w", T.QW[:, :].bitcast(dt.uint8), T.wc[:, :], writes=[A("QW", 0, 512)])
     dma("y", "d_w", T.SW[:, :], T.ws[:, :], writes=[A("SW", 0, 512)])
     close("d_w")
     dma("y", "d_v", T.VT[:, :], T.v[:, :], writes=[A("VT", 0, 512)])
     close("d_v")
 
-    cp(A("LNU", 0, 60), A("LN", 0, 60))
-    emit("v", V.tensor_copy, 1, IND(A("QQ", 0, 320), A("LNU", 0, 20)), A("IDT", 0, 320))
-    tt(A("VA", 0, 320), IND(A("ID5", 0, 320), A("LNU", 0, 20)), A("IDT", 0, 320), OP.add)
-    cp(A("LOF0", 0, 40), A("LN", 20, 60))
-    ts(A("LOF0", 40, 60), A("LN", 40, 60), 320, OP.add)
-    emit("v", V.tensor_copy, 1, IND(A("QQ", 320, 640), A("LNU", 20, 40)), A("VA", 0, 320))
-    ts(A("MASK", 0, 960), A("IQ", 0, 960), sc(0), OP.is_equal)
-    act(A("SEG", 0, 960), A("IQ", 0, 960), ActivationFunctionType.Sign)
-    ts(A("THR", 0, 64), A("GI", 0, 64), sc(1), OP.not_equal, 1.0e29, OP.mult)
-    ts(A("UL", 0, 8), ix(48, 56), sc(7), OP.add)
-    ts(A("UL", 2, 4), ix(48, 50), sc(8), OP.add)
-    ts(A("CLU", 0, 5), ix(36, 41), sc(11), OP.add)
-    for i, ws in enumerate(((1, 2, 4, 8), (16, 32, 0, 0), (-4, -2, -1, 32), (16, 8, 0, 0))):
-        for t in range(4):
-            act(A("KWT", 512 * i + t, 512 * i + 512, 4), A("MASK", 0, 128), scale=float(ws[t]))
+    ts(ix(80, 140), A("LN", 0, 60), 3, an)
+    ts(A("TM", 0, 60), ix(80, 140), 1024, OP.mult, sc("cg"), OP.add)
+    ts(ix(80, 140), A("LN", 0, 60), 2, sh)
+    ts(A("BG", 60, 80), ix(42, 62), sc("i"), OP.add)
+    tt(A("UO", 0, 60), A("TM", 0, 60), ix(80, 140), OP.add)
+    ts(A("BG", 0, 60), A("UO", 0, 60), ST, OP.add)
+    ts(A("BG", 80, 100), A("BG", 60, 80), sc("cg"), OP.add)
+    ts(sc("cgp"), sc("s"), LW, OP.mult, 3 * LEVEL, OP.add)
+    ts(sc("t0"), sc("g"), -3.5, OP.add)
+    ts(sc("a"), sc("t0"), -1, OP.mult, sc("t0"), OP.max)
+    ts(sc("a1"), sc("a"), 2.5, OP.is_equal)
+    ts(sc("t0"), sc("a"), 0.5, OP.is_equal)
+    ts(sc("t1"), sc("a1"), -1, OP.mult, 1, OP.add)
+    ts(sc("a02"), sc("t1"), sc("t0"), OP.subtract)
+    ts(sc("c5"), sc("t1"), NEVER, OP.mult, 5 * LEVEL, OP.add)
+    ts(sc("t1"), sc("a1"), 7 * LW, OP.mult, 4 * LEVEL, OP.add)
+    ts(sc("c4"), sc("t0"), NEVER, OP.mult, sc("t1"), OP.add)
+    ts(A("M4", 0, C), A("IQ4", 0, C), sc("i4"), OP.is_equal)
+    act(A("S4", 0, C), A("IQ4", 0, C), ACT.Sign)
+    ts(sc("off"), R3, sc("g1600"), OP.subtract)
 
-    def spread(out, in_, n):
-        emit("v", V.tensor_tensor_scan, 1, out, A("SEG", 0, n), in_, 0.0, OP.mult, OP.add)
-
-    off = {}
-    for buf, pairs in (
-        ("DF", [("ST", 80), ("BASE", 60), ("VV", 80), ("OR0", 20), ("OR1", 40), ("f0", 20), ("f1", 40), ("fB", 40), ("s12", 20), ("cnt", 20),
-                ("t1", 20), ("t2", 20), ("t3", 20), ("t4", 20), ("n2", 20), ("nb", 20), ("t6", 20), ("t7", 20),
-                ("X", 20), ("ZZ", 40), ("m1", 20), ("t9", 20), ("ta", 20), ("v1", 40), ("ne", 20), ("tb", 20), ("oe", 20), ("on", 20),
-                ("td", 20), ("te", 20), ("o1", 40), ("mz", 40), ("tf", 40), ("tg", 40), ("w", 40), ("my", 40), ("th", 40), ("ti", 40), ("v2", 40),
-                ("u1", 40), ("u2", 40), ("u3", 40), ("u4", 40), ("u5", 40), ("q3", 60), ("q4", 60)]),
-        ("DI", [("P", 120), ("k7", 20), ("KG", 60), ("gb", 60), ("c0x", 20), ("c0y", 20), ("c0z", 20), ("c1y", 20), ("yb1", 20), ("KO", 20),
-                ("a1", 60), ("a2", 60), ("pk", 20), ("pa", 20), ("pr", 20), ("pb", 20), ("RES", 40), ("RSM", 40)])):
-        at = 0
-        for n, w in pairs:
-            off[n] = (buf, at, w)
-            at += w
-
-    def d_(d, n, a=0, b=None):
-        buf, at, w = off[n]
-        return A("%s%d" % (buf, d), at + a, at + (w if b is None else b))
-
-    def statics(d):
-        D = lambda n, a=0, b=None: d_(d, n, a, b)
-        tt(A("MG", 0, 960), IND(A("QQ", 0, 640 if d == 0 else 1280), A("LOF%d" % d, 0, 60)), A("MASK", 0, 960), OP.mult)
-        spread(A("SN", 0, 960), A("MG", 0, 960), 960)
-        cp(D("pk"), A("SN", 655, 960, 16))
-        cp(A("LX%d" % d, 0, 40), A("SN", 15, 640, 16))
-        ts(D("ST", 0, 40), A("SN", 15, 640, 16), sc(12), OP.subtract)
-        ts(D("pa"), D("pk"), 511, OP.bitwise_and)
-        ts(D("pr"), D("pk"), 9, OP.logical_shift_right, 3, OP.bitwise_and)
-        ts(D("pb"), D("pk"), 11, OP.logical_shift_right)
-        cp(A("LX%d" % d, 40, 60), D("pa"))
-        ts(D("ST", 40, 60), D("pa"), sc(12), OP.subtract, LW, OP.add)
-        ts(D("q3", 0, 20), D("pr"), 1024, OP.mult, 320, OP.add)
-        ts(D("q4", 0, 20), D("pb"), sc(12), OP.subtract)
-        tt(D("ST", 60, 80), D("q3", 0, 20), D("q4", 0, 20), OP.add)
-        if d == 0:
-            ts(D("a1"), A("LN", 0, 60), 3, OP.bitwise_and)
-            ts(D("a2"), A("LN", 0, 60), 2, OP.logical_shift_right)
-            ts(D("q3"), D("a1"), 1024, OP.mult, 320, OP.add)
-            ts(D("q4"), D("a2"), sc(12), OP.subtract)
-            tt(D("BASE"), D("q3"), D("q4"), OP.add)
-        else:
-            for i in range(3):
-                cp(D("BASE", 20 * i, 20 * i + 20), d_(0, "BASE", 40 - 20 * i, 60 - 20 * i))
-        ts(D("VV", 60, 80), D("BASE", 40, 60), sc(4), OP.add)
-
-    def early(d):
-        D = lambda n, a=0, b=None: d_(d, n, a, b)
-        P = lambda r, k=1: d_(d, "P", 20 * r, 20 * r + 20 * k)
-        ops = [lambda r=r: ts(P(r), D("KO"), r, OP.logical_shift_right, LW, OP.bitwise_and) for r in range(6)]
-        return ops + [
-            lambda: ts(D("k7"), D("KO"), 7 * LW, OP.bitwise_and),
-            lambda: tt(D("s12"), P(1), P(2), OP.add),
-            lambda: ts(D("t2"), P(1), -3, OP.mult),
-            lambda: ts(D("t3"), P(0), -2, OP.mult),
-            lambda: ts(D("n2"), P(5), sc(4), OP.is_equal),
-            lambda: ts(D("fB", 0, 20), P(2), A("KC", 2, 3), OP.is_equal),
-            lambda: tt(D("cnt"), D("s12"), P(0), OP.add),
-            lambda: tt(D("VV", 0, 60), P(3, 3), D("BASE"), OP.add),
-            lambda: ts(D("f0"), D("k7"), A("KC", 0, 1), OP.is_equal),
-            lambda: ts(D("f1", 0, 20), D("s12"), A("KC", 1, 2), OP.is_equal),
-            lambda: ts(D("nb"), D("s12"), LW, OP.is_equal),
-            lambda: tt(D("t4"), D("t2"), D("t3"), OP.add),
-            lambda: ts(D("t1"), D("cnt"), -2, OP.mult),
-            lambda: ts(D("fB", 20, 40), P(5), sc(4), OP.not_equal),
-            lambda: tt(D("f1", 20, 40), D("n2"), D("nb"), OP.mult),
-            lambda: tt(D("OR1", 20, 40), D("t4"), sj(1), OP.add),
-            lambda: tt(D("OR0"), D("t1"), sj(0), OP.add),
-            lambda: tt(D("t6"), D("VV", 0, 20), D("OR0"), OP.subtract),
-            lambda: tt(D("t7"), D("t6"), D("f0"), OP.mult),
-            lambda: tt(D("OR1", 0, 20), D("t7"), D("OR0"), OP.add),
-        ]
-
-    def gather_k(d):
-        tt(A("MK", 0, 960), IND(A("KF%d" % d, 0, 320), A("LX%d" % d, 0, 60)), A("MASK", 0, 960), OP.mult)
-
-    def late(d):
-        D = lambda n, a=0, b=None: d_(d, n, a, b)
-        V1, x, z, y = D("VV", 20, 40), D("KG", 0, 20), D("KG", 20, 40), D("KG", 40, 60)
-        sh, an = OP.logical_shift_right, OP.bitwise_and
-        spread(A("SCK", 0, 960), A("MK", 0, 960), 960)
-        cp(D("KG"), A("SCK", 15, 960, 16))
-        ts(D("c0x"), x, 3, sh, LW, an)
-        ts(D("gb"), D("KG"), LW, an)
-        ts(D("yb1"), y, 1, sh, LW, an)
-        ts(D("c0y"), y, 3, sh, LW, an)
-        ts(D("c0z"), z, 3, sh, LW, an)
-        ts(D("c1y"), y, 4, sh, LW, an)
-        tt(D("m1"), D("c0x"), D("P", 80, 100), OP.is_equal)
-        tt(D("ne"), D("gb", 40, 60), D("yb1"), OP.not_equal)
-        ts(D("tb"), D("gb", 40, 60), -3, OP.mult)
-        for m, c in (("mz", "c0z"), ("my", "c1y")):
-            tt(D(m, 0, 20), D(c), D("P", 100, 120), OP.is_equal)
-            ts(D(m, 20, 40), D(c), sc(4), OP.is_equal)
-        tt(D("X"), D("ST", 0, 20), D("gb", 0, 20), OP.subtract)
-        for h in (0, 20):
-            tt(D("ZZ", h, h + 20), D("ST", 20, 40), D("gb", 20, 40), OP.subtract)
-        tt(D("oe"), D("tb"), D("ST", 40, 60), OP.add)
-        tt(D("on"), D("c0y"), D("ST", 60, 80), OP.add)
-        tt(D("t9"), D("X"), V1, OP.subtract)
-        tt(D("tf"), D("ZZ"), D("VV", 40, 80), OP.subtract)
-        tt(D("td"), D("on"), D("oe"), OP.subtract)
-        tt(D("ta"), D("t9"), D("m1"), OP.mult)
-        tt(D("tg"), D("tf"), D("mz"), OP.mult)
-        tt(D("te"), D("td"), D("ne"), OP.mult)
-        for h in (0, 20):
-            tt(D("v1", h, h + 20), D("ta"), V1, OP.add)
-        tt(D("w"), D("tg"), D("VV", 40, 80), OP.add)
-        for h in (0, 20):
-            tt(D("o1", h, h + 20), D("te"), D("oe"), OP.add)
-        tt(D("u1"), D("v1"), D("OR1"), OP.subtract)
-        tt(D("th"), D("o1"), D("w"), OP.subtract)
-        tt(D("u2"), D("u1"), D("f1"), OP.mult)
-        tt(D("ti"), D("th"), D("my"), OP.mult)
-        tt(D("u3"), D("u2"), D("OR1"), OP.add)
-        tt(D("v2"), D("ti"), D("w"), OP.add)
-        tt(D("u4"), D("v2"), D("OR1"), OP.subtract)
-        tt(D("u5"), D("u4"), D("fB"), OP.mult)
-        tt(D("RES"), D("u3"), D("u5"), OP.add)
-        ts(D("RSM"), D("RES"), 8 * LW - 1, an)
-        cp(A("LU%d" % d, 0, 40), D("RSM"))
-
-    def lookup(d, table, out, scalar_only=False):
-        a = (A(out, 0, 320), IND(A(table, 0, 8 * LW), A("LU%d" % d, 0, 20)))
-        if scalar_only:
-            act(*a)
-        else:
-            cp(*a)
-        act(A(out, 320, 640), IND(A(table, 0, 8 * LW), A("LU%d" % d, 20, 40)))
-
-    def offsets(out, d, flat, cm, cols):
-        n = cols // 16
-        tt(A("MG", 0, cols), IND(A(flat, 0, 640), A(cm, 0, n)), A("MASK", 0, cols), OP.mult)
-        spread(A("SN", 0, cols), A("MG", 0, cols), cols)
-        ts(d_(d, "u1", 0, n), A("SN", 15, cols, 16), sc(2), OP.subtract)
-        ts(d_(d, "u2", 0, n), d_(d, "u1", 0, n), 0.0, OP.is_lt, 8 * C, OP.mult)
-        tt(d_(d, "u3", 0, n), d_(d, "u1", 0, n), d_(d, "u2", 0, n), OP.add)
-        for t in (2, 3, 0, 1):
-            ts(A(out, 26 * t, 26 * t + n), d_(d, "u3", 0, n), 4, OP.mult, t, OP.add)
-
-    def pull(dst, offs, c0, c1):
-        for t in (2, 0, 3, 1):
-            a = (A(dst, 4 * c0 + t, 4 * c1, 4), IND(A("R", 0, W8), A(offs, 26 * t + c0 // 16, 26 * t + c1 // 16)))
-            if t >= 2:
-                act(*a)
-            else:
-                cp(*a)
-
-    def scores(src, first=None, second=None):
-        quant("QX", 0, ST, A(src, 0, 4 * ST))
-        for n, c0 in enumerate((0, 128, 192)):
-            mm(A("PS", 512 * n, 512 * n + 128), A("QX", c0, c0 + 128), A("SX", c0, c0 + 128), A("QUP", 0, 128), A("SUP", 0, 128))
-        if first:
-            first()
-        for n in range(3):
-            h = 16 if n == 2 else 0
-            for s in (0, 32):
-                o = 8 * s + 32 * n
-                tt(A("BT", o, o + 32 - h), A("PS", 512 * n + s + h, 512 * n + s + 32), A("THR", s + h, s + 32), OP.is_gt)
-        quant("QB", 0, 192, A("BT", 0, 768))
-        if second:
-            second()
-        for d in range(2):
-            for i in range(2):
-                k = 256 * d + 128 * i
-                mm(A("PS", 1536 + 2048 * d, 1664 + 2048 * d), A("QK", k, k + 128), A("SK", k, k + 128), A("QB", 64 * i, 64 * i + 128), A("SB", 64 * i, 64 * i + 128), i == 0, i == 1)
-        cp(A("KU0", 0, 20), A("PS", 1536, 1556))
-        ts(d_(0, "KO"), A("PS", 1536, 1556), LW, OP.mult)
-        act(A("KF0", 0, 320), IND(A("IDT", 0, 512), A("KU0", 0, 20)), scale=512.0)
+    def scores(src):
+        for h in range(2):
+            quant("QX", 160 * h, 160 * h + 160, A(src, 640 * h, 640 * h + 640))
+            mm(h, "UP", 0, "QX", 160 * h, 160)
+        mm(4, "UP", 128, "QX", 0, ST)
+        ts(A("SG0", 0, 160), ps(0, 0, 160), 0.0, OP.is_gt)
+        act(A("SG0", 160, ST), ps(1, 0, 160), ACT.Sign)
+        ts(A("BT0", 0, 160), IND(A("SG0", 0, ST), A("RL0", 0, 10)), 0.0, OP.is_gt)
+        weigh(0)
 
     def back_signs():
-        ts(A("KU1", 0, 20), A("PS", 3584, 3604), 7.0, OP.add)
-        ts(d_(1, "KO"), A("PS", 3584, 3604), 7, OP.add, LW, OP.mult)
-        act(A("KF1", 0, 320), IND(A("IDT", 0, 512), A("KU1", 0, 20)), scale=512.0)
+        act(A("SG1", 0, ST), ps(4, 0, ST), ACT.Sign)
+        act(A("BT1", 0, 160), IND(A("SG1", 0, ST), A("RL1", 0, 10)), ACT.Sign, scale=sc("fs"), bias=sc("fb"))
 
-    statics(0)
-    quant("QU", 0, 128, A("UT", 0, 512))
-    emit("v", V.tensor_copy, 1, CW("QUP", 0, 128), IND(CW("QU", 0, 128), A("UL", 0, 8)))
-    act(A("SUP", 0, 128), IND(A("SU", 0, 128), A("UL", 0, 8)))
-    quant("QK", 0, 512, A("KWT", 0, 2048))
-    act(A("MF", 0, 320), A("IDT", 0, 320), scale=1025.0)
+    def weigh(d):
+        quant("QB%d" % d, 0, 128, A("BT%d" % d, 0, 512))
+        for f in range(2):
+            for m in range(2):
+                mm(2 + 3 * d + f, "K", 128 * f + 8 - 8 * m, "QB%d" % d, 20 * m, 128, m == 0, m == 1)
 
-    def inverse2():
-        emit("v", V.tensor_copy, 1, IND(A("QQ", 640, 960), A("LNU", 40, 60)), A("IDT", 0, 320))
+    def whole(d):
+        for f in range(2):
+            o, k = A("KI%d" % d, 20 * f, 20 * f + 20), ps(2 + 3 * d + f, 0, 20)
+            if d == 0:
+                ts(o, k, A("CC", f, f + 1), OP.add)
+            else:
+                ts(o, k, 0.5, OP.mult, A("CC", 2 + f, 3 + f), OP.add)
 
-    def columns():
-        ts(A("ML", 0, 80), IND(A("QQ", 640, 960), A("CLU", 0, 5)), 320.0, OP.add)
-        ts(A("ML", 80, 160), IND(A("QQ", 0, 320), A("CLU", 0, 5)), 320.0, OP.add)
-        ts(A("ML", 160, 240), A("ML", 80, 160), 1024.0, OP.mult)
-        tt(A("MF", 320, 400), A("ML", 160, 240), A("ML", 0, 80), OP.add)
-        emit("v", V.tensor_copy, 1, IND(A("CF", 0, 400), A("PU", 0, 25)), A("MF", 0, 400))
+    def choose(d):
+        ops = []
+        for k, (s, m, bits) in enumerate(FIELDS):
+            ops.append(lambda k=k, s=s, m=m + sum(1 << (b - s) for b in bits): ts(A("KC%d" % d, k, 280, NK), A("KI%d" % d, 0, 40), s, sh, m, an))
+        return ops + [
+            lambda: ts(A("KF%d" % d, 0, 280), A("KC%d" % d, 0, 280), LW, OP.mult),
+            lambda: scan(A("SK%d" % d, 0, 280), A("D%d" % d, 0, 280), A("KF%d" % d, 0, 280), OP.add, OP.min),
+            lambda: tt(A("RS%d" % d, 0, 40), A("SK%d" % d, NK - 1, 280, NK), A("RAW%d" % d, NK - 1, 280, NK), OP.add),
+            lambda: ts(A("RS%d" % d, 40, 80), A("RS%d" % d, 0, 40), 8 * LW - 1, an),
+            lambda: cp(A("LU%d" % d, 0, 40), A("RS%d" % d, 40, 80)),
+        ]
 
-    scores("R", inverse2, columns)
-    tt(A("MG", 0, 400), A("CF", 0, 400), A("MASK", 0, 400), OP.mult)
-    spread(A("SN", 0, 400), A("MG", 0, 400), 400)
-    cp(ix(64, 89), A("SN", 15, 400, 16))
-    ts(ix(96, 121), ix(64, 89), 1023, OP.bitwise_and)
-    cp(A("CM0", 0, 25), ix(96, 121))
+    def run(ops):
+        for f in ops:
+            f()
 
-    def statics_back():
-        tt(A("VA", 320, 640), IND(A("ID5", 0, 320), A("LNU", 40, 60)), A("IDT", 0, 320), OP.add)
-        for i, (k, o) in enumerate(((20, 640), (0, 640), (0, 960))):
-            ts(A("LOF1", 20 * i, 20 * i + 20), A("LN", k, k + 20), o, OP.add)
-        emit("v", V.tensor_copy, 1, IND(A("QQ", 960, 1280), A("LNU", 20, 40)), A("VA", 320, 640))
-        statics(1)
-        ts(ix(96, 121), ix(64, 89), 10, OP.logical_shift_right)
-        cp(A("CM1", 0, 25), ix(96, 121))
-        tt(A("MG", 0, 80), A("ML", 80, 160), A("MASK", 0, 80), OP.mult)
-        spread(A("SN", 0, 80), A("MG", 0, 80), 80)
+    def lookup(d, table, out, scalar_only=False):
+        act(A(out, ST, 640), IND(A(table, 0, 8 * LW), A("LU%d" % d, 20, 40)))
+        (act if scalar_only else cp)(A(out, 0, ST), IND(A(table, 0, 8 * LW), A("LU%d" % d, 0, 20)))
+
+    def offsets(out, d, c0, c1):
+        mg, sn, uo = ("MG", "SN", "UO") if d == 0 else ("MG1", "SN1", "UO1")
+        a, b, last = c0 // 4, c1 // 4, A(sn, c0 + 3, c1, 4)
+        return [
+            lambda: tt(A(mg, c0, c1), IND(A("FL%d" % d, 0, 640), A("CM%d" % d, c0 // 16, c1 // 16)), A("M4", c0, c1), OP.mult),
+            lambda: scan(A(sn, c0, c1), A("S4", c0, c1), A(mg, c0, c1)),
+            lambda: ts(A(uo, a, b), last, sc("g1600"), OP.is_lt, W8, OP.mult),
+            lambda: tt(A(uo, 100 + a, 100 + b), last, A(uo, a, b), OP.add),
+            lambda: ts(A(out, a, b), A(uo, 100 + a, 100 + b), sc("off"), OP.add),
+        ]
+
+    def pull(dst, offs, c0, cm, c1):
+        act(A(dst, 4 * cm, 4 * c1), IND(A("R", 0, W8), A(offs, cm // 4, c1 // 4)))
+        if cm > c0:
+            cp(A(dst, 4 * c0, 4 * cm), IND(A("R", 0, W8), A(offs, c0 // 4, cm // 4)))
+
+    inverse(2)
+    act(A("MF", 0, ST), A("TAB", 0, ST), scale=1025.0)
+    ts(sc("t0"), sc("i"), 4, OP.mult, sc("q"), OP.add)
+    ts(A("CLU", 0, 5), ix(70, 75), sc("t0"), OP.add)
+    act(A("ML", 0, 80), IND(A("QQ", 640, 960), A("CLU", 0, 5)), ACT.Identity, bias=float(ST))
+    act(A("ML", 80, 160), IND(A("QQ", 0, ST), A("CLU", 0, 5)), ACT.Identity, bias=float(ST))
+    act(A("ML", 160, 240), A("ML", 80, 160), scale=1024.0)
+    scores("R")
+    candidates(0)
+    whole(0)
+    tt(A("MF", ST, C), A("ML", 160, 240), A("ML", 0, 80), OP.add)
+    cp(IND(A("CF", 0, C), A("PU", 0, 25)), A("MF", 0, C))
+    tt(A("MG", 0, C), A("CF", 0, C), A("M16", 0, C), OP.mult)
+    scan(A("SN", 0, C), A("S16", 0, C), A("MG", 0, C))
+    cp(ix(80, 105), A("SN", 15, C, 16))
+    ts(ix(110, 135), ix(80, 105), 1023, an)
+    cp(A("CM0", 0, 25), ix(110, 135))
+
+    def once():
+        ts(ix(110, 135), ix(80, 105), 10, sh)
+        cp(A("CM1", 0, 25), ix(110, 135))
+        for f in range(2):
+            w = IND(A("WT", 0, 1024), A("KL", 4 * f, 4 * f + 4))
+            act(A("WG", 0, 64), w, ACT.Abs, scale=0.5, accum_out=sc("t%d" % (2 + f)))
+            plus(A("CC", 2 + f, 3 + f), sc("t%d" % (2 + f)), float(EXTRA[f]))
+        tt(A("MG", 0, 80), A("ML", 80, 160), A("M16", 0, 80), OP.mult)
+        scan(A("SN", 0, 80), A("S16", 0, 80), A("MG", 0, 80))
         cp(A("LTL", 0, 5), A("SN", 15, 80, 16))
-        quant("QV", 0, 128, A("VT", 0, 512))
-
-    quant("QE", 0, 512, A("ET", 0, 2048))
 
     for r in range(STEPS):
         HQ, HS = "HQ%d" % r, "HS%d" % r
@@ -568,16 +567,12 @@ def rank_program(g, core, T, topo):
         arrives([A(HQ, 0, KX), A(HS, 0, KX)], "arr%d" % r, n_arr)
         if r:
             scores("XT")
-        own = early(0)
-        for f in own[:14]:
-            f()
-        gather_k(0)
-        for f in own[14:]:
-            f()
-        late(0)
+            back_signs()
+            whole(0)
+        run(choose(0))
         lookup(0, "TN" if r else "T0", "FL0")
-        offsets("OFZ", 0, "FL0", "CM0", C)
-        pull("ZT", "OFZ", 0, 128)
+        run(offsets("OFZ", 0, 0, KX))
+        pull("ZT", "OFZ", 0, 48, KX)
         quant("QS", 0, 128, A("ZT", 0, 512))
         for k, c in enumerate(hops(T, topo, rank, r)):
             to = T.cores[peer] if c is None else c
@@ -590,56 +585,84 @@ def rank_program(g, core, T, topo):
                 i, rd = T.SS[:, 0:KX], [A("SS", 0, KX)]
             remote(o, i, rd, "arr%d" % r if c is None else "rarr", "snt%d" % r, topo.addr(to, core), m, n)
         close("snt%d" % r)
-        pull("ZT", "OFZ", 128, C)
-        quant(HQ, KX, C, A("ZT", 4 * KX, 4 * C), HS)
 
-        def layer(c0, c1, m1, buf, w, meanwhile=()):
+        def products(c0, n):
             for b in range(4):
-                for n, p in (("W", 0), ("E", 2048)):
-                    mm(A("PS", p + 512 * b, p + 512 * b + m1), A("Q" + n, 128 * b, 128 * b + 128), A("S" + n, 128 * b, 128 * b + 128), A(HQ, c0, c0 + m1), A(HS, c0, c0 + m1))
-            for b in range(4):
-                l = A(buf, w * b, w * b + c1 - c0)
-                act(l, A("PS", 512 * b, 512 * b + c1 - c0), RELU, scale=0.015625)
-                k = 5 if b else 12
-                for f in meanwhile[:k]:
-                    f()
-                meanwhile = meanwhile[k:]
-                tt(A("R", 4 * c0 + b, 4 * c1, 4), l, A("PS", 2048 + 512 * b, 2048 + 512 * b + c1 - c0), OP.add)
-            for f in meanwhile:
-                f()
+                mm(b, "W", 128 * b, HQ, c0, n, rs=HS)
+                mm(4 + b, "E", 128 * b, HQ, c0, n, rs=HS)
 
-        back_signs()
-        layer(KX, C, C - KX, "RL", 304, early(1) if r else [])
-        shifted("d_ye%d" % r, "y", "R", 4 * C, T.R, 4 * KX, 4 * C, [A("R", 4 * KX, 4 * C)])
+        def layer(c0, c1, buf, meanwhile=()):
+            n = c1 - c0
+            meanwhile = list(meanwhile)
+            for b in range(4):
+                l = A(buf, n * b, n * b + n)
+                act(l, ps(b, 0, n), ACT.Relu, scale=0.015625)
+                if meanwhile:
+                    run(meanwhile.pop(0))
+                tt(A("R", 4 * c0 + b, 4 * c1, 4), l, ps(4 + b, 0, n), OP.add)
+
+        CA = 224
         if r == 0:
-            statics_back()
-            for f in early(1):
-                f()
-        gather_k(1)
-        layer(0, KX, 128, "RL2", 128)
-        shifted("d_yl%d" % r, "sy", "R", 4 * C, T.R, 0, 4 * KX, [A("R", 0, 4 * KX)])
-        late(1)
-        lookup(1, "T0", "FL1")
+            for b in range(4):
+                o = 520 * (b % 2) + 2 - b // 2 * 2
+                quant("QE", 128 * b, 128 * b + 128, A("ET", o, o + 512))
+            lists(1)
+        else:
+            weigh(1)
+        run(offsets("OFZ", 0, KX, C))
+        pull("ZT", "OFZ", KX, 160, CA)
+        if r:
+            whole(1)
+        quant(HQ, KX, CA, A("ZT", 4 * KX, 4 * CA), HS)
+        if r == 0:
+            act(A("SG1", 0, ST), ps(4, 0, ST), ACT.Sign)
+        products(KX, CA - KX)
+        pull("ZT", "OFZ", CA, 312, C)
+        quant(HQ, CA, C, A("ZT", 4 * CA, 4 * C), HS)
+        ch = choose(1) if r else []
+        layer(KX, CA, "RA", [ch[:3], ch[3:5], ch[5:7]])
+        shifted("d_ya%d" % r, "y", "R", 4 * C, T.R, 4 * KX, 4 * CA, [A("R", 4 * KX, 4 * CA)])
+        products(CA, C - CA)
+        layer(CA, C, "RB", [ch[7:9], ch[9:12]])
+        shifted("d_yb%d" % r, "y", "R", 4 * C, T.R, 4 * CA, 4 * C, [A("R", 4 * CA, 4 * C)])
+        products(0, 128)
+        if r == 0:
+            tables(1)
+            act(A("BT1", 0, 160), IND(A("SG1", 0, ST), A("RL1", 0, 10)), ACT.Sign, scale=sc("fs"), bias=sc("fb"))
+            once()
+        else:
+            lookup(1, "T0", "FL1")
         cols = ST if r < STEPS - 1 else C
-        offsets("OFX", 1, "FL1", "CM1", cols)
+        of = offsets("OFX", 1, 0, cols)
+        layer(0, KX, "RC")
+        shifted("d_yl%d" % r, "sy", "R", 4 * C, T.R, 0, 4 * KX, [A("R", 0, 4 * KX)])
+        if r == 0:
+            weigh(1)
+            candidates(1)
+            whole(1)
+            run(choose(1))
+            lookup(1, "T0", "FL1")
+            quant("QV", 0, 128, A("VT", 0, 512))
+        run(of)
         if r < STEPS - 1:
             act(A("TN", 0, ST), A("FL1", 0, ST))
             act(A("TN", ST, C), IND(A("FL1", 0, 640), A("LTL", 0, 5)))
             shifted("d_tn%d" % r, "y", "TN", LW, T.TN, 0, C, [A("TN", 0, C)])
+            pull("XT", "OFX", 0, 160, ST)
         else:
             lookup(0, "T0", "FLO", True)
-            act(A("OPF", 0, C), IND(A("FLO", 0, 640), A("CM0", 0, 25)))
+            act(A("OPF", 0, C), IND(A("FLO", 0, 640), A("CM0", 0, 25)), scale=0.25)
             for k in range(8):
                 dma("y", "d_op", T.op[k:k + 1, :], T.OPF[16 * k:16 * k + 1, :], reads=[A("OPF", 0, C)])
             close("d_op")
-        pull("XT", "OFX", 0, cols)
+            pull("XT", "OFX", 0, 200, C)
 
     quant("QX", 0, C, A("XT", 0, 4 * C))
-    mm(A("PS", 0, C), A("QV", 0, 128), A("SV", 0, 128), A("QX", 0, C), A("SX", 0, C))
+    mm(0, "V", 0, "QX", 0, C)
     dma("s", "d_out", T.oc[:, :], T.QX[:, :].bitcast(dt.uint8), reads=[A("QX", 0, C)])
     for k in range(4):
         dma("y", "d_out", T.osc[4 * k:4 * k + 4, :], T.SX[32 * k:32 * k + 4, :], reads=[A("SX", 0, C)])
-    cp(A("YO", 0, C), A("PS", 0, C))
+    cp(A("YO", 0, C), ps(0, 0, C))
     dma("y", "d_out", T.y[:, :], T.YO[:, :], reads=[A("YO", 0, C)])
     close("d_out")
     finish()

@@ -1,6 +1,7 @@
 from concourse.mybir import dt, AluOpType, ActivationFunctionType
 
 C, ST, KX, STEPS, N = 400, 320, 96, 3, 8
+CA = 224
 MATES = [1, 2, 4]
 W8 = 8 * 4 * C
 LW = 512
@@ -8,7 +9,7 @@ OP = AluOpType
 ACT = ActivationFunctionType
 CODES = "float8_e4m3fn_x4"
 NK = 7
-LEVEL, NEVER = 24 * LW, 512 * LW
+LEVEL, NEVER, BIG = 24 * LW, 512 * LW, 2 ** 23
 
 G2, G1B, G1A, EX, E1, E0, NE = 11, 12, 13, 15, 17, 19, 21
 FIELDS = [(0, 1, (G2, E1, NE)), (1, 3, (G2, E1)), (3, 1, (G2, E0)), (4, 1, (G2,)), (5, 1, (G1B, G1A, EX)), (6, 1, (G1B, G1A)), (7, 7, ())]
@@ -17,8 +18,8 @@ OWN, RZ, RY, RX = 0, 1, 2, 3
 B0, B1, B2, C0, C1, C2 = range(6)
 WEIGHTS = [
     [(OWN, B0, 0, 48, 1, -256), (OWN, B1, 8, 16, 1, 640), (OWN, B2, 8, 16, 1, 0), (OWN, C0, 0, 8, 1, 32), (OWN, C0, 1, 7, 5, 0),
-     (OWN, C1, 0, 16, 1, 64), (OWN, C2, 0, 8, 1, 16), (OWN, C2, 8, 16, 2, -2 ** G2), (OWN, C2, 9, 16, 2, 2 ** G2),
-     (OWN, 8 + B0, 0, 4, 1, -2 ** EX), (OWN, 8 + B0, 4, 8, 1, 2 ** EX), (OWN, 8 + B0, 1, 7, 5, 0),
+     (OWN, C1, 0, 16, 1, 64), (OWN, C2, 0, 8, 1, 16), (OWN, C2, 8, 16, 2, -2 ** G2), (OWN, C2, 9, 16, 2, 2 ** G2)],
+    [(OWN, 8 + B0, 0, 4, 1, -2 ** EX), (OWN, 8 + B0, 4, 8, 1, 2 ** EX), (OWN, 8 + B0, 1, 7, 5, 0),
      (OWN, 8 + B1, 0, 32, 1, 2 ** G1A), (OWN, 8 + B1, 0, 4, 1, -2 ** G1A),
      (OWN, 8 + B2, 1, 4, 1, -2 ** G1B), (OWN, 8 + B2, 4, 7, 1, 2 ** G1B), (OWN, 8 + B2, 0, 1, 1, 2 ** G2), (OWN, 8 + B2, 7, 8, 1, -2 ** G2)],
     [(OWN, 8 + C1, 8, 16, 1, 2 ** EX), (OWN, 8 + C1, 1, 7, 5, 2 ** EX), (OWN, 8 + C2, 0, 8, 1, 2 ** E1 + 2 ** E0),
@@ -31,13 +32,13 @@ WEIGHTS = [
 F32, B16, I32, U16 = "float32", "bfloat16", "int32", "uint16"
 SCRATCH = {}
 for _t, _l in (
-    (B16, (("R", W8), ("XT", 4 * C), ("ZT", 4 * C), ("UT", 512), ("VT", 512), ("ET", 1040), ("ONE", 520), ("WT", 1024), ("KW", 1056), ("MM", 32),
-           ("BT0", 592), ("BT1", 592), ("SG0", ST), ("SG1", ST), ("IQ", C), ("IQ4", C), ("M16", C), ("S16", 480), ("M4", C), ("S4", C), ("JK", 64))),
-    (I32, (("LP", 25), ("LN", 60), ("IDX", 160), ("KI0", 40), ("KI1", 40), ("KC0", 280), ("KC1", 280), ("RS0", 80), ("RS1", 80))),
-    (U16, (("PU", 26), ("LNU", 60), ("LC0", 20), ("LC1", 20), ("LB0", 20), ("LB1", 20), ("CL", 10), ("RL0", 10), ("RL1", 10), ("WL", 16), ("KL", 8),
-           ("UL", 16), ("CLU", 6), ("CM0", 26), ("CM1", 26), ("LTL", 6), ("LU0", 40), ("LU1", 40), ("OFZ", 100), ("OFX", 100))),
-    (F32, (("TAB", 720), ("SC", 32), ("CC", 4), ("WG", 256), ("WS", 256), ("QQ", 1280), ("VA", ST), ("FT", ST), ("MG", 480), ("SN", 480),
-           ("MG1", C), ("SN1", C), ("UO", 200), ("UO1", 200), ("WN", 20), ("SRC", 80), ("SRG", 80), ("BG", 100), ("TM", 80), ("RAW0", 280), ("RAW1", 280),
+    (B16, (("R0", W8), ("R1", W8), ("XT", 4 * C), ("ZT", 4 * C), ("UT", 512), ("VT", 512), ("ET", 1040), ("ONE", 520), ("WT", 1024), ("KW", 1056), ("MM", 64),
+           ("BT", 1104), ("SG0", ST), ("SG1", ST), ("PAT", 96), ("K16", C), ("K4", C), ("JK", 32))),
+    (I32, (("LP", 25), ("LN", 60), ("IDX", 200), ("KI0", 40), ("KI1", 40), ("KC0", 280), ("KC1", 280), ("RS0", 80), ("RS1", 80))),
+    (U16, (("PU", 26), ("LNU", 60), ("LA", 20), ("LC0", 20), ("LC1", 20), ("LB0", 20), ("LB1", 20), ("CL", 10), ("RL0", 10), ("RL1", 10), ("WL", 16),
+           ("KL", 8), ("LI", 52), ("UL", 16), ("CLU", 6), ("CM0", 26), ("CM1", 26), ("LTL", 6), ("LU0", 40), ("LU1", 40), ("OFZ", 100), ("OFX", 100))),
+    (F32, (("TAB", 720), ("SC", 40), ("CC", 4), ("WG", 256), ("WS", 272), ("QQ", 960), ("QI", ST), ("VA", ST), ("FT", 480), ("MG0", C), ("SN0", 480),
+           ("MG1", C), ("SN1", C), ("UO0", 200), ("UO1", 200), ("WN", 20), ("SRC", 80), ("SRG", 80), ("BG", 100), ("TM", 80), ("RAW0", 280), ("RAW1", 280),
            ("D0", 280), ("D1", 280), ("KF0", 280), ("KF1", 280), ("SK0", 280), ("SK1", 280), ("MF", C), ("ML", 240), ("CF", C),
            ("T0", 8 * LW), ("TN", 8 * LW), ("FL0", 640), ("FL1", 640), ("FLO", 640), ("OPF", C), ("RA", 512), ("RB", 704), ("RC", 512), ("YO", C))),
 ):
@@ -50,7 +51,7 @@ for _n, _w in (("U", 128), ("UP", 256), ("V", 128), ("W", 512), ("E", 512), ("K"
 for _r in range(STEPS):
     SCRATCH["HQ%d" % _r] = ("sbuf", [128, C], CODES)
     SCRATCH["HS%d" % _r] = ("sbuf", [128, C], "uint8")
-DMAS = ["d_ln", "d_p", "d_u", "d_x", "d_xs", "d_v", "d_w", "d_t0", "d_tn0", "d_tn1", "d_out", "d_op", "d_s0", "d_s1"]
+DMAS = ["d_ln", "d_p", "d_u", "d_x", "d_xa", "d_xb", "d_v", "d_w", "d_t0", "d_tn0", "d_tn1", "d_out", "d_op", "d_s0", "d_s1", "d_qi"]
 DMAS += ["d_%s%d" % (k, r) for k in ("ya", "yb", "yl") for r in range(STEPS)]
 SEMAPHORES = ["ev", "es", "et", "eg", "rarr", "rsent"] + DMAS + ["arr%d" % r for r in range(STEPS)] + ["snt%d" % r for r in range(STEPS)]
 
@@ -250,8 +251,8 @@ def rank_program(g, core, T, topo):
     def act(out, x, func=ACT.Copy, **kw):
         emit("s", S.activation, 1, out, x, func, **kw)
 
-    def plus(out, x, k):
-        act(out, x, ACT.Identity, bias=k)
+    def lin(out, x, a, b):
+        act(out, x, ACT.Identity, scale=a if is_ap(a) else float(a), bias=b if is_ap(b) else float(b))
 
     def quant(n, a, b, x, sn=None):
         emit("v", V.quantize_mx, 2, A(n, a, b), A(sn or "S" + n[1:], a, b), x)
@@ -269,11 +270,11 @@ def rank_program(g, core, T, topo):
         else:
             emit("g", g.iota, 1, out, pattern, base, cm, allow_small_or_imprecise_dtypes=True)
 
-    def scan(out, d0, d1, op0=OP.mult, op1=OP.add):
-        emit("v", V.tensor_tensor_scan, 1, out, d0, d1, 0.0, op0, op1)
+    def spread(out, flat, keys):
+        emit("v", V.tensor_tensor_scan, 1, out, A(keys, 0, out[3] - out[2]), flat, 0.0, OP.add, OP.max)
 
-    names = ["i", "g", "s", "q", "i4", "g1600", "off", "s4", "cl", "kl", "ul0", "ul1", "clu", "cg", "cgp", "a", "a1", "a02", "c4", "c5",
-             "fs", "fb", "t0", "t1", "t2", "t3"]
+    names = ["i", "g", "s", "q", "i4", "r3", "r7", "g1600", "lim", "off", "b16", "s4", "cl", "wl", "kl", "ul0", "ul1", "clu", "cg", "cgp",
+             "a", "a1", "a3", "a02", "c4", "c5", "fs", "fb", "t0", "t1", "t2", "t3", "t4", "t5", "t6", "t7", "t8"]
 
     def sc(n):
         k = names.index(n)
@@ -282,14 +283,28 @@ def rank_program(g, core, T, topo):
     def ix(a, b):
         return A("IDX", a, b)
 
-    def shifted(sem, queues, name, width, src, a, b, reads):
+    def shifted(sem, queues, name, width, src, a, b, reads, slots=range(1, 8)):
         n = 0
-        for k in range(1, 8):
+        for k in slots:
             for d0, s0, rows in ((0, 16 * k, 128 - 16 * k), (128 - 16 * k, 0, 16 * k)):
                 dma(queues[n % len(queues)], sem, T[name][d0:d0 + rows, width * k + a:width * k + b], src[s0:s0 + rows, a:b],
                     reads=reads, writes=[A(name, width * k + a, width * k + b)])
                 n += 1
         close(sem)
+
+    def paint(q, lines):
+        for quarter, row, a, b, s, w in lines:
+            o, n = A("WT", 256 * quarter + 16 * row + a, 256 * quarter + 16 * row + b, s), len(range(a, b, s))
+            if q == "v":
+                fill(o, float(w))
+            elif q == "g":
+                iota(o, [[0, n]], w, 0)
+            else:
+                lin(o, A("JK", 0, n), 1, w)
+
+    def gaps(name):
+        for k in range(8):
+            iota(A(name, LW * k + C, LW * k + LW), [[0, LW - C]], 0, 0)
 
     for k in range(8):
         dma("ys"[k % 2], "d_ln", T.LN[16 * k:16 * k + 16, :], T.ln[:, :], writes=[A("LN", 0, 60)])
@@ -298,191 +313,155 @@ def rank_program(g, core, T, topo):
     close("d_p")
     dma("y", "d_u", T.UT[:, :], T.u[:, :], writes=[A("UT", 0, 512)])
     close("d_u")
-    dma("y", "d_x", T.R[:, 0:4 * C], T.x[:, :], writes=[A("R", 0, 4 * C)])
+    dma("y", "d_x", T.R0[:, 0:4 * C], T.x[:, :], writes=[A("R0", 0, 4 * C)])
     close("d_x")
-    shifted("d_xs", "y", "R", 4 * C, T.x, 0, 4 * C, [])
+    shifted("d_xa", "y", "R0", 4 * C, T.x, 0, 4 * C, [], range(1, 5))
 
+    J16, JW, JC, JK, JL = ix(16, 36), ix(36, 52), ix(52, 62), ix(62, 70), ix(70, 75)
     iota(ix(0, 1), [[0, 1]], 0, 1, True)
     iota(A("TAB", 0, C), [[1, C]], 0, 0)
+    iota(J16, [[16, 20]], 0, 0, True)
+    iota(A("PAT", 32, 49), [[1, 17]], -1, 0)
     iota(A("TAB", C, C + ST), [[1, 80], [1024, 4]], ST, 0)
-    iota(A("IQ", 0, C), [[0, 25], [1, 16]], 0, 0)
-    iota(ix(16, 32), [[1, 16]], 0, 16, True)
-    iota(ix(32, 42), [[8, 2], [64, 5]], 0, 0, True)
-    iota(ix(42, 62), [[16, 20]], 0, 0, True)
-    iota(A("MM", 0, 32), [[1, 8], [-1, 4]], 0, 0)
-    iota(ix(62, 70), [[8, 2], [256, 4]], 0, 16, True)
-    iota(ix(70, 75), [[64, 5]], 0, 0, True)
-    iota(A("IQ4", 0, C), [[0, 100], [1, 4]], 0, 0)
-    for n in ("T0", "TN"):
-        for k in range(8):
-            iota(A(n, LW * k + C, LW * k + LW), [[0, LW - C]], 0, 0)
-    iota(A("ONE", 0, 520), [[0, 520]], 1, 0)
-    for h in range(2):
-        emit("g", g.affine_select, 1, A("ET", 520 * h, 520 * h + 520), A("ONE", 0, 520), [[-1, 520]], OP.is_equal, 0.0, 2 + h, 4)
+    iota(JC, [[8, 2], [64, 5]], 0, 0, True)
+    iota(JW, [[1, 16]], 0, 16, True)
+    iota(JK, [[8, 2], [256, 4]], 0, 16, True)
+    iota(JL, [[64, 5]], 0, 0, True)
+    iota(A("MM", 0, 64), [[1, 16], [-1, 4]], 0, 0)
 
+    fill(A("JK", 0, 32), 0.0)
     fill(A("WT", 0, 1024), 0.0)
-    fill(A("JK", 0, 64), 0.0)
-    for q, row, a, b, s, w in WEIGHTS[1]:
-        o = 256 * q + 16 * row
-        plus(A("WT", o + a, o + b, s), A("JK", 0, len(range(a, b, s))), float(w))
-    for q, row, a, b, s, w in WEIGHTS[0]:
-        o = 256 * q + 16 * row
-        fill(A("WT", o + a, o + b, s), float(w))
-
-    P = ix(0, 1)
     for k, (s, m) in enumerate(((0, 15), (4, 7), (4, 1), (5, 3), (2, 3), (0, 3), (0, 7))):
-        ts(ix(1 + k, 2 + k), P, s, sh, m, an)
-    cp(A("SC", 0, 5), ix(1, 6))
-    R3, R7 = ix(6, 7), ix(7, 8)
+        ts(ix(1 + k, 2 + k), ix(0, 1), s, sh, m, an)
+    cp(A("SC", 0, 7), ix(1, 8))
+    paint("s", WEIGHTS[2])
+    paint("g", WEIGHTS[1])
+    gaps("T0")
     cp(A("LNU", 0, 60), A("LN", 0, 60))
-    ts(sc("cg"), sc("g"), -LW, OP.mult, 8 * LW, OP.add)
+    cp(A("PU", 0, 25), A("LP", 0, 25))
+    lin(sc("g1600"), sc("g"), 4 * C, 0)
 
-    def inverse(i):
-        cp(IND(A("QQ", ST * i, ST * i + ST), A("LNU", 20 * i, 20 * i + 20)), A("TAB", 0, ST))
-
-    def lists(d):
-        i0, i2 = (0, 40) if d == 0 else (40, 0)
-        ts(A("LC%d" % d, 0, 20), ix(42, 62), sc("i"), OP.add)
+    def values(d):
+        i0 = 40 * d
+        ts(A("LC%d" % d, 0, 20), J16, sc("i"), OP.add)
         ts(A("LC%d" % d, 0, 20, p=(0, 32)), A("LN", i0, i0 + 20, p=(0, 32)), C, OP.add)
         act(A("VA", 0, ST), IND(A("TAB", 0, 720), A("LC%d" % d, 0, 20)))
-        ts(A("LB%d" % d, 0, 20, p=(0, 64)), A("LN", i2, i2 + 20, p=(0, 64)), ST, OP.add)
-        cp(A("LB%d" % d, 0, 20, p=(64, 96)), A("LN", i2, i2 + 20, p=(64, 96)))
-        cp(A("LB%d" % d, 0, 20, p=(96, 128)), A("LN", 20, 40, p=(96, 128)))
 
-    def tables(d):
-        win = A("QQ", 640 * d, 640 * d + 640)
-        cp(IND(A("QQ", 640 * d + ST, 640 * d + 640), A("LNU", 20, 40)), A("VA", 0, ST))
-        act(A("FT", 0, ST), IND(win, A("LB%d" % d, 0, 20)))
-        tt(A("MG", 0, ST), IND(win, A("LB%d" % d, 0, 20)), A("M16", 0, ST), OP.mult)
-        scan(A("SN", 0, ST), A("S16", 0, ST), A("MG", 0, ST))
-        cp(A("WN", 0, 20), A("SN", 15, ST, 16))
+    def others(d):
+        act(A("FT", 0, ST), IND(A("QQ", 0, 960 if d else ST), A("LB%d" % d, 0, 20)))
+        act(A("FT", ST, 480), IND(A("FT", 0, ST), A("CL", 0, 10)))
+        spread(A("SN0", 0, ST), A("FT", 0, ST), "K16")
+        ts(A("WN", 0, 20), A("SN0", 15, ST, 16), sc("b16"), OP.add)
         for a in range(4):
             for b in range(4):
                 dma("sy"[b % 2], "d_s%d" % d, T.SRC[32 * b:32 * b + 32, 20 * a:20 * a + 20], T.WN[32 * a:32 * a + 32, :],
                     reads=[A("WN", 0, 20)], writes=[A("SRC", 0, 80)])
         close("d_s%d" % d)
-        tt(A("MG", ST, 480), IND(A("FT", 0, ST), A("CL", 0, 10)), A("M16", 0, 160), OP.mult)
-        scan(A("SN", ST, 480), A("S16", 0, 160), A("MG", ST, 480))
+        spread(A("SN0", ST, 480), A("FT", ST, 480), "K16")
+        ts(A("RL%d" % d, 0, 10), A("SN0", ST + 15, 480, 16), sc("b16"), OP.add)
         cp(A("RL%d" % d, 0, 10, p=(0, 32)), A("CL", 0, 10, p=(0, 32)))
-        cp(A("RL%d" % d, 0, 10, p=(32, 64)), A("SN", ST + 15, 480, 16, p=(32, 64)))
-        cp(A("RL%d" % d, 0, 10, p=(64, 128)), A("SN", ST + 15, 480, 16, p=(64, 128)))
 
     def candidates(d):
-        i0, i2 = (0, 40) if d == 0 else (40, 0)
+        i0, i2 = 40 * d, 40 - 40 * d
         raw = lambda k, h: A("RAW%d" % d, 140 * h + k, 140 * h + 140, NK)
         src = lambda q: A("SRG", 20 * q, 20 * q + 20)
-        plus(A("SRG", 0, 80), A("SRC", 0, 80), sc("cg"))
-        for h in range(2):
-            plus(raw(0, h), src(OWN), 0.0)
-            plus(raw(1, h), src(RZ), float(LEVEL + 6 * LW))
-            plus(raw(2, h), src(RY), float(2 * LEVEL + 7 * LW))
-        plus(raw(4, 1), src(RX), float(4 * LEVEL + 7 * LW))
         ts(raw(3, 0), A("BG", i2, i2 + 20), 3 * LEVEL, OP.add)
         ts(raw(3, 1), A("BG", i2, i2 + 20), sc("cgp"), OP.add)
-        ts(raw(5, 0), A("BG", 20, 40), sc("c5"), OP.add)
-        ts(raw(5, 1), A("BG", 20, 40), 5 * LEVEL, OP.add)
-        ts(raw(6, 0), A("BG", 60, 80), 6 * LEVEL + 13 * LW, OP.add)
-        ts(raw(6, 1), A("BG", 80, 100), 6 * LEVEL, OP.add)
-        ts(A("TM", 0, 20), A("BG", i0, i0 + 20), sc("a02"), OP.mult, sc("c4"), OP.add)
+        lin(raw(5, 0), A("BG", 20, 40), 1, sc("c5"))
+        lin(raw(5, 1), A("BG", 20, 40), 1, 5 * LEVEL)
+        lin(raw(6, 0), A("BG", 60, 80), 1, 6 * LEVEL + 13 * LW)
+        lin(raw(6, 1), A("BG", 80, 100), 1, 6 * LEVEL)
+        lin(A("TM", 0, 20), A("BG", i0, i0 + 20), sc("a02"), sc("c4"))
+        lin(A("SRG", 0, 80), A("SRC", 0, 80), 1, sc("cg"))
+        for h in range(2):
+            lin(raw(0, h), src(OWN), 1, 0)
+            lin(raw(1, h), src(RZ), 1, LEVEL + 6 * LW)
+            ts(raw(2, h), src(RY), 2 * LEVEL + 7 * LW, OP.add)
+        ts(raw(4, 1), src(RX), 4 * LEVEL + 7 * LW, OP.add)
         ts(A("TM", 20, 40), src(RX), sc("a1"), OP.mult)
         tt(raw(4, 0), A("TM", 0, 20), A("TM", 20, 40), OP.add)
+        fill(A("D%d" % d, 0, 1), 0.0)
         tt(A("D%d" % d, 1, 280), A("RAW%d" % d, 0, 279), A("RAW%d" % d, 1, 280), OP.subtract)
         fill(A("D%d" % d, 0, 280, NK), 1.0e12)
 
-    lists(0)
-    inverse(0)
-    ts(A("M16", 0, C), A("IQ", 0, C), sc("i"), OP.is_equal)
-    act(A("S16", 0, C), A("IQ", 0, C), ACT.Sign)
-    ts(sc("s4"), sc("s"), 4, OP.mult)
-    ts(sc("t0"), sc("i4"), 16, OP.mult, sc("s4"), OP.add)
-    ts(sc("cl"), R3, sc("t0"), OP.add)
-    ts(A("CL", 0, 10), ix(32, 42), sc("cl"), OP.add)
-    tables(0)
-
-    ts(ix(80, 96), ix(16, 32), 1023, an)
-    ts(ix(96, 112), ix(80, 96), 8, sh, 0, sh)
-    ts(sc("t1"), sc("q"), 256, OP.mult)
-    ts(ix(112, 128), ix(16, 32), 255, an)
-    ts(A("WL", 0, 16), ix(112, 128), sc("t1"), OP.add)
-    tt(A("WG", 0, 256), IND(A("WT", 0, 1024), A("WL", 0, 16)), A("M16", 0, 256), OP.mult)
-    scan(A("WS", 0, 256), A("S16", 0, 256), A("WG", 0, 256))
-    ts(A("MM", 0, 32), A("MM", 0, 32), sc("s4"), OP.is_equal)
-    fill(A("KW", 0, 1056), 0.0)
-    for k in range(16):
-        act(A("KW", 32 + 64 * k, 64 + 64 * k), A("MM", 0, 32), scale=A("WS", 16 * k + 15, 16 * k + 16))
-    ts(sc("kl"), sc("g"), -255, OP.mult)
-    ts(A("KL", 0, 8), ix(62, 70), sc("kl"), OP.add)
-    for f in range(2):
-        w = IND(A("WT", 0, 1024), A("KL", 4 * f, 4 * f + 4))
-        act(A("WG", 0, 64), w, ACT.Relu, scale=-1.0, accum_out=sc("t%d" % (2 + f)))
-        plus(A("CC", f, f + 1), sc("t%d" % (2 + f)), float(EXTRA[f]))
-
-    quant("QU", 0, 128, A("UT", 0, 512))
-    ts(sc("t0"), R7, 2.5, OP.is_gt)
-    ts(sc("t1"), R7, 5.5, OP.is_gt, sc("t0"), OP.add)
-    ts(sc("a"), R7, 16, OP.mult)
-    ts(sc("ul0"), sc("t1"), -47, OP.mult, sc("a"), OP.add)
-    ts(sc("ul1"), sc("t1"), 49, OP.mult, sc("a"), OP.subtract)
-    ts(A("UL", 0, 8), A("JK", 0, 8), sc("ul0"), OP.add)
-    ts(A("UL", 8, 16), A("JK", 0, 8), sc("ul1"), OP.add, 32, OP.add)
-    for d in range(2):
-        cp(CW("QUP", 128 * d, 128 * d + 128), IND(CW("QU", 0, 128), A("UL", 8 * d, 8 * d + 8)))
-        act(A("SUP", 128 * d, 128 * d + 128), IND(A("SU", 0, 128), A("UL", 8 * d, 8 * d + 8)))
-    ts(sc("fs"), sc("t0"), 2, OP.mult, -1, OP.add)
-    ts(sc("fb"), sc("fs"), -0.5, OP.mult)
-    for d in range(2):
-        fill(A("BT%d" % d, 0, 592), 0.0)
-        quant("QB%d" % d, 20, 148, A("BT%d" % d, 80, 592))
-    fill(A("ZT", 4 * KX, 512), 0.0)
-    quant("QK", 0, 264, A("KW", 0, 1056))
-
-    cp(A("PU", 0, 25), A("LP", 0, 25))
-    ts(sc("g1600"), sc("g"), 4 * C, OP.mult)
-    act(A("T0", 0, C), IND(A("TAB", 0, C), A("PU", 0, 25)), ACT.Identity, bias=sc("g1600"), scale=4.0)
+    values(0)
+    cp(IND(A("QQ", ST, 640), A("LNU", 40, 60)), A("TAB", 0, ST))
+    cp(A("LA", 0, 20, p=(0, 64)), A("LN", 20, 40, p=(0, 64)))
+    cp(A("LA", 0, 20, p=(64, 128)), A("LN", 0, 20, p=(64, 128)))
+    for o, n, k in ((0, 16, "i"), (16, 4, "i4")):
+        ts(A("PAT", 64, 64 + n), A("PAT", 33, 33 + n), sc(k), OP.is_equal, -2 * BIG, OP.mult)
+        ts(A("PAT", 80, 80 + n), A("PAT", 32, 32 + n), sc(k), OP.is_equal, BIG, OP.mult)
+        tt(A("PAT", o, o + n), A("PAT", 64, 64 + n), A("PAT", 80, 80 + n), OP.add)
+    ts(A("LI", 0, 25), A("JK", 0, 25), sc("i"), OP.add)
+    act(A("K16", 0, C), IND(A("PAT", 0, 16), A("LI", 0, 25)))
+    lin(sc("s4"), sc("s"), 4, 0)
+    lin(sc("t0"), sc("i4"), 16, sc("r3"))
+    lin(sc("cl"), sc("s"), 4, sc("t0"))
+    lin(sc("t1"), sc("q"), 1, sc("s"))
+    lin(sc("wl"), sc("t1"), -256, 0)
+    cp(IND(A("QQ", 0, ST), A("LA", 0, 20)), A("VA", 0, ST))
+    for h in range(2):
+        dma("y", "d_qi", T.QI[64 * h:64 * h + 64, :], T.QQ[64:128, 0:ST], reads=[A("QQ", 0, ST)], writes=[A("QI", 0, ST)])
+    close("d_qi")
+    cp(A("LB0", 0, 20), A("LN", 40, 60))
+    cp(A("LB0", 0, 20, p=(96, 128)), A("LN", 20, 40, p=(96, 128)))
+    ts(A("CL", 0, 10), JC, sc("cl"), OP.add)
+    ts(sc("b16"), sc("i"), 15, OP.is_lt, -BIG, OP.mult)
+    ts(A("WL", 0, 16), JW, sc("wl"), OP.add)
+    paint("v", WEIGHTS[0])
+    others(0)
+    act(A("WG", 0, 256), IND(A("WT", 0, 1024), A("WL", 0, 16)))
+    lin(A("T0", 0, C), IND(A("TAB", 0, C), A("PU", 0, 25)), 4, sc("g1600"))
     shifted("d_t0", "y", "T0", LW, T.T0, 0, C, [A("T0", 0, C)])
+    shifted("d_xb", "y", "R0", 4 * C, T.x, 0, 4 * C, [], range(5, 8))
     dma("y", "d_w", T.QW[:, :].bitcast(dt.uint8), T.wc[:, :], writes=[A("QW", 0, 512)])
     dma("y", "d_w", T.SW[:, :], T.ws[:, :], writes=[A("SW", 0, 512)])
     close("d_w")
     dma("y", "d_v", T.VT[:, :], T.v[:, :], writes=[A("VT", 0, 512)])
     close("d_v")
 
-    ts(ix(80, 140), A("LN", 0, 60), 3, an)
-    ts(A("TM", 0, 60), ix(80, 140), 1024, OP.mult, sc("cg"), OP.add)
-    ts(ix(80, 140), A("LN", 0, 60), 2, sh)
-    ts(A("BG", 60, 80), ix(42, 62), sc("i"), OP.add)
-    tt(A("UO", 0, 60), A("TM", 0, 60), ix(80, 140), OP.add)
-    ts(A("BG", 0, 60), A("UO", 0, 60), ST, OP.add)
-    ts(A("BG", 80, 100), A("BG", 60, 80), sc("cg"), OP.add)
-    ts(sc("cgp"), sc("s"), LW, OP.mult, 3 * LEVEL, OP.add)
-    ts(sc("t0"), sc("g"), -3.5, OP.add)
-    ts(sc("a"), sc("t0"), -1, OP.mult, sc("t0"), OP.max)
-    ts(sc("a1"), sc("a"), 2.5, OP.is_equal)
-    ts(sc("t0"), sc("a"), 0.5, OP.is_equal)
-    ts(sc("t1"), sc("a1"), -1, OP.mult, 1, OP.add)
-    ts(sc("a02"), sc("t1"), sc("t0"), OP.subtract)
-    ts(sc("c5"), sc("t1"), NEVER, OP.mult, 5 * LEVEL, OP.add)
-    ts(sc("t1"), sc("a1"), 7 * LW, OP.mult, 4 * LEVEL, OP.add)
-    ts(sc("c4"), sc("t0"), NEVER, OP.mult, sc("t1"), OP.add)
-    ts(A("M4", 0, C), A("IQ4", 0, C), sc("i4"), OP.is_equal)
-    act(A("S4", 0, C), A("IQ4", 0, C), ACT.Sign)
-    ts(sc("off"), R3, sc("g1600"), OP.subtract)
+    quant("QU", 0, 128, A("UT", 0, 512))
+    ts(sc("t2"), sc("r7"), 2.5, OP.is_gt)
+    ts(sc("t3"), sc("r7"), 5.5, OP.is_gt, sc("t2"), OP.add)
+    ts(sc("t4"), sc("r7"), 16, OP.mult)
+    ts(sc("ul0"), sc("t3"), -47, OP.mult, sc("t4"), OP.add)
+    ts(A("UL", 0, 8), A("JK", 0, 8), sc("ul0"), OP.add)
 
-    def scores(src):
+    def pick_u(d):
+        cp(CW("QUP", 128 * d, 128 * d + 128), IND(CW("QU", 0, 128), A("UL", 8 * d, 8 * d + 8)))
+        act(A("SUP", 128 * d, 128 * d + 128), IND(A("SU", 0, 128), A("UL", 8 * d, 8 * d + 8)))
+
+    pick_u(0)
+    spread(A("WS", 0, 256), A("WG", 0, 256), "K16")
+    ts(A("WS", 256, 272), A("WS", 15, 256, 16), sc("b16"), OP.add)
+    ts(A("MM", 0, 64), A("MM", 0, 64), sc("s4"), OP.is_equal)
+    fill(A("MM", 32, 64), 0.0)
+    fill(A("KW", 0, 32), 0.0)
+    for k in range(16):
+        act(A("KW", 32 + 64 * k, 96 + 64 * k), A("MM", 0, 64), scale=A("WS", 256 + k, 257 + k))
+    fill(A("ONE", 0, 520), 1.0)
+    for h in range(2):
+        emit("g", g.affine_select, 1, A("ET", 520 * h, 520 * h + 520), A("ONE", 0, 520), [[-1, 520]], OP.is_equal, 0.0, 2 + h, 4)
+
+    def signs(src):
         for h in range(2):
             quant("QX", 160 * h, 160 * h + 160, A(src, 640 * h, 640 * h + 640))
             mm(h, "UP", 0, "QX", 160 * h, 160)
-        mm(4, "UP", 128, "QX", 0, ST)
         ts(A("SG0", 0, 160), ps(0, 0, 160), 0.0, OP.is_gt)
         act(A("SG0", 160, ST), ps(1, 0, 160), ACT.Sign)
-        ts(A("BT0", 0, 160), IND(A("SG0", 0, ST), A("RL0", 0, 10)), 0.0, OP.is_gt)
-        weigh(0)
 
     def back_signs():
+        mm(4, "UP", 128, "QX", 0, ST)
         act(A("SG1", 0, ST), ps(4, 0, ST), ACT.Sign)
-        act(A("BT1", 0, 160), IND(A("SG1", 0, ST), A("RL1", 0, 10)), ACT.Sign, scale=sc("fs"), bias=sc("fb"))
+
+    def gather_signs(d):
+        if d == 0:
+            ts(A("BT", 0, 160), IND(A("SG0", 0, ST), A("RL0", 0, 10)), 0.0, OP.is_gt)
+        else:
+            act(A("BT", 512, 672), IND(A("SG1", 0, ST), A("RL1", 0, 10)), ACT.Sign, scale=sc("fs"), bias=sc("fb"))
 
     def weigh(d):
-        quant("QB%d" % d, 0, 128, A("BT%d" % d, 0, 512))
+        quant("QB%d" % d, 0, 128, A("BT", 512 * d, 512 * d + 512))
         for f in range(2):
             for m in range(2):
                 mm(2 + 3 * d + f, "K", 128 * f + 8 - 8 * m, "QB%d" % d, 20 * m, 128, m == 0, m == 1)
@@ -495,13 +474,19 @@ def rank_program(g, core, T, topo):
             else:
                 ts(o, k, 0.5, OP.mult, A("CC", 2 + f, 3 + f), OP.add)
 
+    def sums(d):
+        for f in range(2):
+            w = IND(A("WT", 0, 1024), A("KL", 4 * f, 4 * f + 4))
+            act(A("WG", 0, 64), w, ACT.Abs if d else ACT.Relu, scale=0.5 if d else -1.0, accum_out=sc("t%d" % (7 + f)))
+            lin(A("CC", 2 * d + f, 2 * d + f + 1), sc("t%d" % (7 + f)), 1, EXTRA[f])
+
     def choose(d):
         ops = []
         for k, (s, m, bits) in enumerate(FIELDS):
             ops.append(lambda k=k, s=s, m=m + sum(1 << (b - s) for b in bits): ts(A("KC%d" % d, k, 280, NK), A("KI%d" % d, 0, 40), s, sh, m, an))
         return ops + [
             lambda: ts(A("KF%d" % d, 0, 280), A("KC%d" % d, 0, 280), LW, OP.mult),
-            lambda: scan(A("SK%d" % d, 0, 280), A("D%d" % d, 0, 280), A("KF%d" % d, 0, 280), OP.add, OP.min),
+            lambda: emit("v", V.tensor_tensor_scan, 1, A("SK%d" % d, 0, 280), A("D%d" % d, 0, 280), A("KF%d" % d, 0, 280), 0.0, OP.add, OP.min),
             lambda: tt(A("RS%d" % d, 0, 40), A("SK%d" % d, NK - 1, 280, NK), A("RAW%d" % d, NK - 1, 280, NK), OP.add),
             lambda: ts(A("RS%d" % d, 40, 80), A("RS%d" % d, 0, 40), 8 * LW - 1, an),
             lambda: cp(A("LU%d" % d, 0, 40), A("RS%d" % d, 40, 80)),
@@ -515,76 +500,101 @@ def rank_program(g, core, T, topo):
         act(A(out, ST, 640), IND(A(table, 0, 8 * LW), A("LU%d" % d, 20, 40)))
         (act if scalar_only else cp)(A(out, 0, ST), IND(A(table, 0, 8 * LW), A("LU%d" % d, 0, 20)))
 
+    def by_column(d, c0, cm, c1):
+        for f, a, b in ((act, cm, c1), (cp, c0, cm)):
+            if b > a:
+                f(A("MG%d" % d, a, b), IND(A("FL%d" % d, 0, 640), A("CM%d" % d, a // 16, b // 16)))
+
     def offsets(out, d, c0, c1):
-        mg, sn, uo = ("MG", "SN", "UO") if d == 0 else ("MG1", "SN1", "UO1")
-        a, b, last = c0 // 4, c1 // 4, A(sn, c0 + 3, c1, 4)
+        uo, a, b, last = "UO%d" % d, c0 // 4, c1 // 4, A("SN%d" % d, c0 + 3, c1, 4)
         return [
-            lambda: tt(A(mg, c0, c1), IND(A("FL%d" % d, 0, 640), A("CM%d" % d, c0 // 16, c1 // 16)), A("M4", c0, c1), OP.mult),
-            lambda: scan(A(sn, c0, c1), A("S4", c0, c1), A(mg, c0, c1)),
-            lambda: ts(A(uo, a, b), last, sc("g1600"), OP.is_lt, W8, OP.mult),
+            lambda: spread(A("SN%d" % d, c0, c1), A("MG%d" % d, c0, c1), "K4"),
+            lambda: ts(A(uo, a, b), last, sc("lim"), OP.is_lt, W8, OP.mult),
             lambda: tt(A(uo, 100 + a, 100 + b), last, A(uo, a, b), OP.add),
             lambda: ts(A(out, a, b), A(uo, 100 + a, 100 + b), sc("off"), OP.add),
         ]
 
-    def pull(dst, offs, c0, cm, c1):
-        act(A(dst, 4 * cm, 4 * c1), IND(A("R", 0, W8), A(offs, cm // 4, c1 // 4)))
-        if cm > c0:
-            cp(A(dst, 4 * c0, 4 * cm), IND(A("R", 0, W8), A(offs, c0 // 4, cm // 4)))
+    def pull(dst, win, offs, c0, cm, c1):
+        for f, a, b in ((act, cm, c1), (cp, c0, cm)):
+            if b > a:
+                f(A(dst, 4 * a, 4 * b), IND(A(win, 0, W8), A(offs, a // 4, b // 4)))
 
-    inverse(2)
+    signs("R0")
+    fill(A("BT", 160, 1104), 0.0)
+    lin(sc("kl"), sc("g"), -255, 0)
     act(A("MF", 0, ST), A("TAB", 0, ST), scale=1025.0)
-    ts(sc("t0"), sc("i"), 4, OP.mult, sc("q"), OP.add)
-    ts(A("CLU", 0, 5), ix(70, 75), sc("t0"), OP.add)
-    act(A("ML", 0, 80), IND(A("QQ", 640, 960), A("CLU", 0, 5)), ACT.Identity, bias=float(ST))
-    act(A("ML", 80, 160), IND(A("QQ", 0, ST), A("CLU", 0, 5)), ACT.Identity, bias=float(ST))
-    act(A("ML", 160, 240), A("ML", 80, 160), scale=1024.0)
-    scores("R")
-    candidates(0)
-    whole(0)
+    ts(A("KL", 0, 8), JK, sc("kl"), OP.add)
+    quant("QB0", 20, 148, A("BT", 592, 1104))
+    gather_signs(0)
+    cp(IND(A("CF", 0, C), A("PU", 0, 20)), A("MF", 0, ST))
+    quant("QK", 0, 264, A("KW", 0, 1056))
+    weigh(0)
+    sums(0)
+    lin(sc("clu"), sc("i"), 4, sc("q"))
+    lin(sc("cg"), sc("g"), -LW, 8 * LW)
+    lin(sc("cgp"), sc("s"), LW, 3 * LEVEL)
+    act(sc("a"), sc("g"), ACT.Abs, bias=-3.5)
+    ts(A("CLU", 0, 5), JL, sc("clu"), OP.add)
+    lin(A("ML", 0, 80), IND(A("QQ", ST, 640), A("CLU", 0, 5)), 1, ST)
+    lin(A("ML", 80, 160), IND(A("QI", 0, ST), A("CLU", 0, 5)), 1, ST)
+    lin(A("ML", 160, 240), A("ML", 80, 160), 1024, 0)
+    ts(ix(80, 140), A("LN", 0, 60), 3, an)
+    ts(ix(140, 200), A("LN", 0, 60), 2, sh)
+    ts(A("TM", 0, 60), ix(80, 140), 1024, OP.mult, sc("cg"), OP.add)
+    ts(A("BG", 60, 80), J16, sc("i"), OP.add)
+    tt(A("UO0", 0, 60), A("TM", 0, 60), ix(140, 200), OP.add)
+    ts(sc("a1"), sc("a"), 2.5, OP.is_equal)
+    ts(sc("a3"), sc("a"), 0.5, OP.is_equal)
+    lin(A("BG", 0, 60), A("UO0", 0, 60), 1, ST)
+    lin(A("BG", 80, 100), A("BG", 60, 80), 1, sc("cg"))
+    lin(sc("t5"), sc("a1"), -1, 1)
+    lin(sc("a02"), sc("a3"), -1, sc("t5"))
+    lin(sc("c5"), sc("t5"), NEVER, 5 * LEVEL)
+    lin(sc("t6"), sc("a1"), 7 * LW, 4 * LEVEL)
+    lin(sc("c4"), sc("a3"), NEVER, sc("t6"))
     tt(A("MF", ST, C), A("ML", 160, 240), A("ML", 0, 80), OP.add)
-    cp(IND(A("CF", 0, C), A("PU", 0, 25)), A("MF", 0, C))
-    tt(A("MG", 0, C), A("CF", 0, C), A("M16", 0, C), OP.mult)
-    scan(A("SN", 0, C), A("S16", 0, C), A("MG", 0, C))
-    cp(ix(80, 105), A("SN", 15, C, 16))
+    cp(IND(A("CF", 0, C), A("PU", 20, 25)), A("MF", ST, C))
+    ts(A("LI", 26, 51), A("JK", 0, 25), sc("r3"), OP.add)
+    spread(A("SN0", 0, C), A("CF", 0, C), "K16")
+    whole(0)
+    for b in range(4):
+        o = 520 * (b % 2) + 2 - b // 2 * 2
+        quant("QE", 128 * b, 128 * b + 128, A("ET", o, o + 512))
+    candidates(0)
+    act(A("K4", 0, C), IND(A("PAT", 16, 20), A("LI", 26, 51)))
+    ts(ix(80, 105), A("SN0", 15, C, 16), sc("b16"), OP.add)
     ts(ix(110, 135), ix(80, 105), 1023, an)
     cp(A("CM0", 0, 25), ix(110, 135))
+    ts(sc("t0"), sc("i4"), 3, OP.is_lt, BIG, OP.mult)
+    lin(sc("lim"), sc("t0"), 1, sc("g1600"))
+    lin(sc("off"), sc("lim"), -1, sc("r3"))
 
-    def once():
-        ts(ix(110, 135), ix(80, 105), 10, sh)
-        cp(A("CM1", 0, 25), ix(110, 135))
-        for f in range(2):
-            w = IND(A("WT", 0, 1024), A("KL", 4 * f, 4 * f + 4))
-            act(A("WG", 0, 64), w, ACT.Abs, scale=0.5, accum_out=sc("t%d" % (2 + f)))
-            plus(A("CC", 2 + f, 3 + f), sc("t%d" % (2 + f)), float(EXTRA[f]))
-        tt(A("MG", 0, 80), A("ML", 80, 160), A("M16", 0, 80), OP.mult)
-        scan(A("SN", 0, 80), A("S16", 0, 80), A("MG", 0, 80))
-        cp(A("LTL", 0, 5), A("SN", 15, 80, 16))
+    def back_lists():
+        def rest():
+            ts(sc("ul1"), sc("t3"), 49, OP.mult, sc("t4"), OP.subtract)
+            ts(A("UL", 8, 16), A("JK", 0, 8), sc("ul1"), OP.add, 32, OP.add)
+            pick_u(1)
+            lin(sc("fs"), sc("t2"), 2, -1)
+            lin(sc("fb"), sc("fs"), -0.5, 0)
+            quant("QB1", 20, 148, A("BT", 592, 1104))
+            ts(ix(110, 135), ix(80, 105), 10, sh)
+            cp(A("CM1", 0, 25), ix(110, 135))
+            spread(A("SN1", 0, 80), A("ML", 80, 160), "K16")
+            ts(A("LTL", 0, 5), A("SN1", 15, 80, 16), sc("b16"), OP.add)
+            sums(1)
+        ops = [lambda: cp(IND(A("QQ", 640, 960), A("LNU", 20, 40)), A("VA", 0, ST))]
+        for p, a, k in (((0, 32), 0, 640), ((32, 64), 0, 0), ((64, 96), 0, ST), ((96, 128), 20, ST)):
+            ops.append(lambda p=p, a=a, k=k: ts(A("LB1", 0, 20, p=p), A("LN", a, a + 20, p=p), k, OP.add))
+        return ops + [lambda: None] * 4 + [rest]
+
+    values(1)
 
     for r in range(STEPS):
         HQ, HS = "HQ%d" % r, "HS%d" % r
+        OLD, NEW = "R%d" % (r % 2), "R%d" % (1 - r % 2)
         peer = rank ^ MATES[r]
         n_arr = sum(mask_of(topo, T.cores[peer] if c is None else c, core)[1] for c in hops(T, topo, peer, r))
         arrives([A(HQ, 0, KX), A(HS, 0, KX)], "arr%d" % r, n_arr)
-        if r:
-            scores("XT")
-            back_signs()
-            whole(0)
-        run(choose(0))
-        lookup(0, "TN" if r else "T0", "FL0")
-        run(offsets("OFZ", 0, 0, KX))
-        pull("ZT", "OFZ", 0, 48, KX)
-        quant("QS", 0, 128, A("ZT", 0, 512))
-        for k, c in enumerate(hops(T, topo, rank, r)):
-            to = T.cores[peer] if c is None else c
-            m, n = mask_of(topo, core, to)
-            if k == 0:
-                o = T[HQ if c is None else "QR"][:, 0:KX].bitcast(dt.uint8)
-                i, rd = T.QS[:, 0:KX].bitcast(dt.uint8), [A("QS", 0, KX)]
-            else:
-                o = T[HS if c is None else "SR"][:, 0:KX]
-                i, rd = T.SS[:, 0:KX], [A("SS", 0, KX)]
-            remote(o, i, rd, "arr%d" % r if c is None else "rarr", "snt%d" % r, topo.addr(to, core), m, n)
-        close("snt%d" % r)
 
         def products(c0, n):
             for b in range(4):
@@ -599,63 +609,90 @@ def rank_program(g, core, T, topo):
                 act(l, ps(b, 0, n), ACT.Relu, scale=0.015625)
                 if meanwhile:
                     run(meanwhile.pop(0))
-                tt(A("R", 4 * c0 + b, 4 * c1, 4), l, ps(4 + b, 0, n), OP.add)
+                tt(A(NEW, 4 * c0 + b, 4 * c1, 4), l, ps(4 + b, 0, n), OP.add)
 
-        CA = 224
-        if r == 0:
-            for b in range(4):
-                o = 520 * (b % 2) + 2 - b // 2 * 2
-                quant("QE", 128 * b, 128 * b + 128, A("ET", o, o + 512))
-            lists(1)
-        else:
+        def shift(name, queues, c0, c1):
+            shifted("d_%s%d" % (name, r), queues, NEW, 4 * C, T[NEW], 4 * c0, 4 * c1, [A(NEW, 4 * c0, 4 * c1)])
+
+        if r:
+            signs("XT")
+            gather_signs(0)
+            weigh(0)
+            back_signs()
+            gather_signs(1)
+            whole(0)
+        run(choose(0))
+        lookup(0, "TN" if r else "T0", "FL0")
+        if r:
             weigh(1)
-        run(offsets("OFZ", 0, KX, C))
-        pull("ZT", "OFZ", KX, 160, CA)
+        by_column(0, 0, 96, CA)
+        run(offsets("OFZ", 0, 0, CA))
+        pull("ZT", OLD, "OFZ", KX, 160, CA)
         if r:
             whole(1)
         quant(HQ, KX, CA, A("ZT", 4 * KX, 4 * CA), HS)
-        if r == 0:
-            act(A("SG1", 0, ST), ps(4, 0, ST), ACT.Sign)
         products(KX, CA - KX)
-        pull("ZT", "OFZ", CA, 312, C)
+        pull("ZT", OLD, "OFZ", 0, 48, KX)
+        by_column(0, CA, CA, C)
+        quant("QS", 0, 128, A("ZT", 0, 512))
+        for k, c in enumerate(hops(T, topo, rank, r)):
+            to = T.cores[peer] if c is None else c
+            m, n = mask_of(topo, core, to)
+            if k == 0:
+                o = T[HQ if c is None else "QR"][:, 0:KX].bitcast(dt.uint8)
+                i, rd = T.QS[:, 0:KX].bitcast(dt.uint8), [A("QS", 0, KX)]
+            else:
+                o = T[HS if c is None else "SR"][:, 0:KX]
+                i, rd = T.SS[:, 0:KX], [A("SS", 0, KX)]
+            remote(o, i, rd, "arr%d" % r if c is None else "rarr", "snt%d" % r, topo.addr(to, core), m, n)
+        close("snt%d" % r)
+        if r == 0:
+            gaps("TN")
+        of = offsets("OFZ", 0, CA, C)
+        layer(KX, CA, "RA", [[], of[:1], of[1:3], of[3:]])
+        shift("ya", "y", KX, CA)
+        pull("ZT", OLD, "OFZ", CA, 312, C)
         quant(HQ, CA, C, A("ZT", 4 * CA, 4 * C), HS)
-        ch = choose(1) if r else []
-        layer(KX, CA, "RA", [ch[:3], ch[3:5], ch[5:7]])
-        shifted("d_ya%d" % r, "y", "R", 4 * C, T.R, 4 * KX, 4 * CA, [A("R", 4 * KX, 4 * CA)])
         products(CA, C - CA)
-        layer(CA, C, "RB", [ch[7:9], ch[9:12]])
-        shifted("d_yb%d" % r, "y", "R", 4 * C, T.R, 4 * CA, 4 * C, [A("R", 4 * CA, 4 * C)])
+        ch = choose(1) if r else back_lists()
+        layer(CA, C, "RB", [ch[:4], ch[4:7], ch[7:8], ch[8:9]])
+        if r == 0:
+            others(1)
+        shift("yb", "y", CA, C)
         products(0, 128)
-        if r == 0:
-            tables(1)
-            act(A("BT1", 0, 160), IND(A("SG1", 0, ST), A("RL1", 0, 10)), ACT.Sign, scale=sc("fs"), bias=sc("fb"))
-            once()
-        else:
-            lookup(1, "T0", "FL1")
         cols = ST if r < STEPS - 1 else C
-        of = offsets("OFX", 1, 0, cols)
-        layer(0, KX, "RC")
-        shifted("d_yl%d" % r, "sy", "R", 4 * C, T.R, 0, 4 * KX, [A("R", 0, 4 * KX)])
         if r == 0:
+            layer(0, KX, "RC", [ch[9:]])
+            shift("yl", "y", 0, KX)
+            back_signs()
+            gather_signs(1)
             weigh(1)
             candidates(1)
             whole(1)
             run(choose(1))
             lookup(1, "T0", "FL1")
-            quant("QV", 0, 128, A("VT", 0, 512))
-        run(of)
+        else:
+            run(ch[9:])
+            lookup(1, "T0", "FL1")
+            layer(0, KX, "RC")
+            shift("yl", "y", 0, KX)
         if r < STEPS - 1:
             act(A("TN", 0, ST), A("FL1", 0, ST))
             act(A("TN", ST, C), IND(A("FL1", 0, 640), A("LTL", 0, 5)))
             shifted("d_tn%d" % r, "y", "TN", LW, T.TN, 0, C, [A("TN", 0, C)])
-            pull("XT", "OFX", 0, 160, ST)
+        by_column(1, 0, 224, cols)
+        run(offsets("OFX", 1, 0, cols))
+        if r < STEPS - 1:
+            if r == 0:
+                quant("QV", 0, 128, A("VT", 0, 512))
+            pull("XT", NEW, "OFX", 0, 160, ST)
         else:
             lookup(0, "T0", "FLO", True)
             act(A("OPF", 0, C), IND(A("FLO", 0, 640), A("CM0", 0, 25)), scale=0.25)
             for k in range(8):
                 dma("y", "d_op", T.op[k:k + 1, :], T.OPF[16 * k:16 * k + 1, :], reads=[A("OPF", 0, C)])
             close("d_op")
-            pull("XT", "OFX", 0, 200, C)
+            pull("XT", NEW, "OFX", 0, 200, C)
 
     quant("QX", 0, C, A("XT", 0, 4 * C))
     mm(0, "V", 0, "QX", 0, C)

@@ -32,15 +32,16 @@ WEIGHTS = [
 F32, B16, I32, U16 = "float32", "bfloat16", "int32", "uint16"
 SCRATCH = {}
 for _t, _l in (
-    (B16, (("R0", W8), ("R1", W8), ("XT", 4 * C), ("ZT", 4 * C), ("UT", 512), ("VT", 512), ("ET", 1040), ("ONE", 520), ("WT", 1024), ("KW", 1056), ("MM", 64),
-           ("BT", 1104), ("SG0", ST), ("SG1", ST), ("PAT", 96), ("K16", C), ("K4", C), ("JK", 32))),
-    (I32, (("LP", 25), ("LN", 60), ("IDX", 200), ("KI0", 40), ("KI1", 40), ("KC0", 280), ("KC1", 280), ("RS0", 80), ("RS1", 80))),
-    (U16, (("PU", 26), ("LNU", 60), ("LA", 20), ("LC0", 20), ("LC1", 20), ("LB0", 20), ("LB1", 20), ("CL", 10), ("RL0", 10), ("RL1", 10), ("WL", 16),
-           ("KL", 8), ("LI", 52), ("UL", 16), ("CLU", 6), ("CM0", 26), ("CM1", 26), ("LTL", 6), ("LU0", 40), ("LU1", 40), ("OFZ", 100), ("OFX", 100))),
-    (F32, (("TAB", 720), ("SC", 40), ("CC", 4), ("WG", 256), ("WS", 272), ("QQ", 960), ("QI", ST), ("VA", ST), ("FT", 480), ("MG0", C), ("SN0", 480),
-           ("MG1", C), ("SN1", C), ("UO0", 200), ("UO1", 200), ("WN", 20), ("SRC", 80), ("SRG", 80), ("BG", 100), ("TM", 80), ("RAW0", 280), ("RAW1", 280),
-           ("D0", 280), ("D1", 280), ("KF0", 280), ("KF1", 280), ("SK0", 280), ("SK1", 280), ("MF", C), ("ML", 240), ("CF", C),
-           ("T0", 8 * LW), ("TN", 8 * LW), ("FL0", 640), ("FL1", 640), ("FLO", 640), ("OPF", C), ("RA", 512), ("RB", 704), ("RC", 512), ("YO", C))),
+    (B16, (("R0", W8), ("R1", W8), ("XT", 4 * C), ("ZT", 4 * C), ("UT", 512), ("VT", 512), ("ET", 1040), ("ONE", 520), ("WT", 1024), ("KW", 1056),
+           ("MM", 64), ("BT0", 592), ("BT1", 592), ("SG0", ST), ("SG1", ST), ("PAT", 128), ("K16", C), ("K4", C), ("JK", 32))),
+    (I32, (("LP", 25), ("LN", 60), ("IDX", 340), ("KI0", 40), ("KI1", 40), ("KC0", 280), ("KC1", 280), ("RS0", 80), ("RS1", 80))),
+    (U16, (("PU", 26), ("LA", 20), ("LB", 40), ("LC", 20), ("LM", 20), ("UR", 16), ("CL", 10), ("RL0", 10), ("RL1", 10), ("WL", 16),
+           ("KL", 8), ("LI", 52), ("UL", 16), ("CLU", 12), ("CM0", 26), ("CM1", 26), ("LTL", 6), ("LU0", 40), ("LU1", 40), ("OFZ", 100), ("OFX", 100))),
+    (F32, (("TAB", 720), ("SC", 48), ("CC", 4), ("WG", 512), ("WS", 272), ("QQ", 960), ("VA", ST), ("FT", 960), ("FM", ST), ("SP", 1120),
+           ("MG0", C), ("SN0", C), ("MG1", C), ("SN1", C), ("UO0", 200), ("UO1", 200), ("SRA", 176), ("SRG", 256), ("BG", 100), ("TM", 220),
+           ("RAW0", 280), ("RAW1", 280), ("D0", 280), ("D1", 280), ("KF0", 280), ("KF1", 280), ("SK0", 280), ("SK1", 280), ("MF", C), ("ML", 240),
+           ("CF", C), ("T0", 8 * LW), ("TN", 8 * LW), ("FL0", 640), ("FL1", 640), ("FLO", 640), ("OPF", C), ("RA", 512), ("RB", 704), ("RC", 384),
+           ("YO", C))),
 ):
     for _n, _w in _l:
         SCRATCH[_n] = ("sbuf", [128, _w], _t)
@@ -51,8 +52,8 @@ for _n, _w in (("U", 128), ("UP", 256), ("V", 128), ("W", 512), ("E", 512), ("K"
 for _r in range(STEPS):
     SCRATCH["HQ%d" % _r] = ("sbuf", [128, C], CODES)
     SCRATCH["HS%d" % _r] = ("sbuf", [128, C], "uint8")
-DMAS = ["d_ln", "d_p", "d_u", "d_x", "d_xa", "d_xb", "d_v", "d_w", "d_t0", "d_tn0", "d_tn1", "d_out", "d_op", "d_s0", "d_s1", "d_qi"]
-DMAS += ["d_%s%d" % (k, r) for k in ("ya", "yb", "yl") for r in range(STEPS)]
+DMAS = ["d_ln", "d_p", "d_u", "d_x", "d_v", "d_w", "d_tn0", "d_tn1", "d_out", "d_op", "d_qi", "d_o0", "d_o1", "d_y0", "d_y1"]
+DMAS += ["d_x%d" % k for k in range(4)] + ["d_%s%d" % (k, r) for k in ("T0", "SRA", "ya", "yb", "yl") for r in range(3)]
 SEMAPHORES = ["ev", "es", "et", "eg", "rarr", "rsent"] + DMAS + ["arr%d" % r for r in range(STEPS)] + ["snt%d" % r for r in range(STEPS)]
 
 
@@ -106,6 +107,36 @@ def is_ap(x):
     return isinstance(x, tuple) and len(x) > 0 and x[0] in ("A", "I", "C")
 
 
+def region(x):
+    _, n, a, b, s, p = x
+    if n == "PS":
+        return n, (a // 512 * 512, (b + 511) // 512 * 512, 1, p)
+    return n, (a, b, s, p)
+
+
+def meet(p, q):
+    if p[1] <= q[0] or q[1] <= p[0] or p[3][1] <= q[3][0] or q[3][1] <= p[3][0]:
+        return False
+    return not (p[2] == q[2] > 1 and (p[0] - q[0]) % p[2])
+
+
+def sides(nout, args, kw):
+    def parts(xs):
+        out = []
+        for x in xs:
+            if is_ap(x):
+                out += [("A",) + x[1][1:], x[2]] if x[0] == "I" else [("A",) + x[1:]]
+        return out
+    reads, writes = parts(args[nout:]) + parts(x for k, x in kw.items() if k != "accum_out"), parts([kw.get("accum_out")])
+    for x in args[:nout]:
+        if x[0] == "I":
+            writes.append(("A",) + x[1][1:])
+            reads.append(x[2])
+        else:
+            writes.append(("A",) + x[1:])
+    return reads, writes
+
+
 def builder(g, T):
     Q = {"v": g.vector, "s": g.scalar, "t": g.tensor, "g": g, "y": g.sync}
     known = {q: {} for q in Q}
@@ -118,17 +149,6 @@ def builder(g, T):
         if x[0] == "C":
             return T[x[1]][:, x[2]:x[3]].bitcast(dt.uint32)
         return ap(x[1]).indirect(ap(x[2]))
-
-    def region(x):
-        _, n, a, b, s, p = x
-        if n == "PS":
-            return n, (a // 512 * 512, (b + 511) // 512 * 512, 1, p)
-        return n, (a, b, s, p)
-
-    def meet(p, q):
-        if p[1] <= q[0] or q[1] <= p[0] or p[3][1] <= q[3][0] or q[3][1] <= p[3][0]:
-            return False
-        return not (p[2] == q[2] > 1 and (p[0] - q[0]) % p[2])
 
     def wait(q, evs):
         best = {}
@@ -160,22 +180,8 @@ def builder(g, T):
             h[:] = [e for e in h if not (e[0] == reg and e[1] == w and e[3] == q and e[2][0] == ev[0])]
             h.append((reg, w, ev, q))
 
-    def parts(xs):
-        out = []
-        for x in xs:
-            if is_ap(x):
-                out += [("A",) + x[1][1:], x[2]] if x[0] == "I" else [("A",) + x[1:]]
-        return out
-
     def emit(q, fn, nout, *args, acc=False, **kw):
-        writes = parts([kw.get("accum_out")])
-        reads = parts(args[nout:]) + parts(x for k, x in kw.items() if k != "accum_out")
-        for x in args[:nout]:
-            if x[0] == "I":
-                writes.append(("A",) + x[1][1:])
-                reads.append(x[2])
-            else:
-                writes.append(("A",) + x[1:])
+        reads, writes = sides(nout, args, kw)
         hazards(q, reads, writes, acc)
         s = "e" + q
         i = fn(*[ap(x) if is_ap(x) else x for x in args], **{k: ap(x) if is_ap(x) else x for k, x in kw.items()})
@@ -193,7 +199,7 @@ def builder(g, T):
         for k, v in known[q].items():
             o[2][k] = max(v, o[2].get(k, 0))
 
-    def dma(q, sem, out, in_, reads=(), writes=()):
+    def dma(q, sem, out, in_, reads, writes):
         hazards(q, reads, writes)
         Q[q].dma_start(out, in_).then_inc(T.sem[sem], 16)
         total[sem] = total.get(sem, 0) + 16
@@ -224,12 +230,115 @@ def builder(g, T):
     return emit, dma, close, remote, arrives, finish
 
 
+CYCLE, WAKE, SLACK, ISSUE, WAY, BYTE, ROW, CALL = 0.00095, 0.15, 0.05, 0.1, 0.9, 1 / 600e3, 0.02 / 16, 0.5
+
+
+def planner(issue):
+    emit, dma, close, remote, arrives, finish = issue
+    nodes, hist, batches = [], {}, {}
+
+    def node(q, hold, way, load, reads, writes, run, after=()):
+        deps, both = set(after), [(r, False) for r in reads] + [(r, True) for r in writes]
+        for x, w in both:
+            n, reg = region(x)
+            deps |= {k for reg2, w2, k in hist.setdefault(n, []) if (w or w2 or n == "PS") and meet(reg, reg2)}
+        for x, w in both:
+            n, reg = region(x)
+            if w and reg[2] == 1 and reg[3] == (0, 128):
+                hist[n] = [e for e in hist[n] if not (reg[0] <= e[0][0] and e[0][1] <= reg[1])]
+            hist[n].append((reg, w, len(nodes)))
+        nodes.append((q, hold, way, load, deps, run))
+        return len(nodes) - 1
+
+    def size(x):
+        return 16 * size(x[2]) if x[0] == "I" else len(range(x[2], x[3], x[4]))
+
+    def cycles(q, nout, args):
+        full = [x for x in args if is_ap(x)]
+        n = size(full[0])
+        if q in "tg":
+            return 1.2 * (n + 16) if q == "t" else 150 + 2 * n
+        if nout == 2:
+            return 15 + n
+        if any(x[0] == "I" for x in full):
+            return 60 + (3.8 if full[0][0] == "I" else 1.56) * n
+        if len(args) == 4 and len(full) == 3 and "PS" not in (full[1][1], full[2][1]):
+            return max(64, 2 * n)
+        return max(64, n / 2 if q == "v" and all(SCRATCH[x[1]][2] in (B16, U16) for x in full if size(x) > 1) else n)
+
+    def emit_(q, fn, nout, *args, acc=False, **kw):
+        reads, writes = sides(nout, args, kw)
+        node(q, CYCLE * cycles(q, nout, args), 0, 0, reads, writes, lambda: emit(q, fn, nout, *args, acc=acc, **kw))
+
+    def dma_(q, sem, out, in_, reads=(), writes=(), rows=128, width=0):
+        batches.setdefault(sem, []).append((q, reads, writes, rows * (ROW + width * BYTE), lambda: dma(q, sem, out, in_, reads, writes)))
+
+    def remote_(out, in_, reads, rsem, lsem, *rest):
+        batches.setdefault(lsem, []).append(("g", reads, [], 0, lambda: remote(out, in_, reads, rsem, lsem, *rest)))
+
+    def close_(sem, lands=None, way=0):
+        b = batches.pop(sem)
+
+        def run():
+            for o in b:
+                o[4]()
+            close(sem)
+        k = node(b[0][0], len(b) * (ISSUE if lands is None else CALL), WAY, sum(o[3] for o in b), [x for o in b for x in o[1]], [x for o in b for x in o[2]], run)
+        if lands is not None:
+            node(None, 0, way, 0, [], lands, lambda: None, [k])
+
+    def finish_():
+        users = [[] for _ in nodes]
+        for k, o in enumerate(nodes):
+            for d in o[4]:
+                users[d].append(k)
+        gap = lambda d, k: 0 if nodes[d][0] == nodes[k][0] == "t" else WAKE
+        far, after, last = [0.0] * len(nodes), {}, None
+        left, there = [len(o[4]) for o in nodes], [0.0] * len(nodes)
+        for k in reversed(range(len(nodes))):
+            q, hold, way, load = nodes[k][:4]
+            far[k] = hold + way + load + max([far[u] + gap(k, u) for u in users[k]] + [0])
+            if q == "y":
+                if last is not None:
+                    far[k], after[k] = max(far[k], max(hold, load) + far[last]), last
+                    left[last] += 1
+                last = k
+        ready, free = [k for k in range(len(nodes)) if not left[k]], {}
+        start = lambda k: max(there[k], free.get(nodes[k][0], 0))
+        while ready:
+            fits, until = [], {}
+            for k in sorted(ready, key=lambda k: -far[k]):
+                q = nodes[k][0]
+                if start(k) + nodes[k][1] <= until.get(q, 1e9):
+                    fits.append(k)
+                until[q] = min(until.get(q, 1e9), start(k) + SLACK)
+            k = min(fits, key=lambda k: (start(k), -far[k]))
+            q, hold, way, load, deps, run = nodes[k]
+            t = start(k)
+            if q:
+                free[q] = t + hold
+            end = t + hold + way
+            if load:
+                free["engines"] = max(t + ISSUE, free.get("engines", 0)) + load
+                end = max(end, free["engines"] + way)
+            run()
+            ready.remove(k)
+            for u, at in [(u, end + gap(k, u)) for u in users[k]] + ([(after[k], t)] if k in after else []):
+                there[u] = max(there[u], at)
+                left[u] -= 1
+                if not left[u]:
+                    ready.append(u)
+        finish()
+
+    return emit_, dma_, close_, remote_, arrives, finish_
+
+
 def rank_program(g, core, T, topo):
     rank = T.rank_of(core)
     if rank is None:
         relay(g, core, T, topo)
         return
-    emit, dma, close, remote, arrives, finish = builder(g, T)
+    emit, dma, close, remote, arrives, finish = planner(builder(g, T))
     V, S = g.vector, g.scalar
     sh, an = OP.logical_shift_right, OP.bitwise_and
 
@@ -273,23 +382,35 @@ def rank_program(g, core, T, topo):
     def spread(out, flat, keys):
         emit("v", V.tensor_tensor_scan, 1, out, A(keys, 0, out[3] - out[2]), flat, 0.0, OP.add, OP.max)
 
-    names = ["i", "g", "s", "q", "i4", "r3", "r7", "g1600", "lim", "off", "b16", "s4", "cl", "wl", "kl", "ul0", "ul1", "clu", "cg", "cgp",
-             "a", "a1", "a3", "a02", "c4", "c5", "fs", "fb", "t0", "t1", "t2", "t3", "t4", "t5", "t6", "t7", "t8"]
+    def listed(out, flat, at):
+        n = flat[3] - flat[2]
+        spread(A("SP", at, at + n), flat, "K16")
+        ts(out, A("SP", at + 15, at + n, 16), sc("b16"), OP.add)
+
+    names = ["i", "g", "s", "q", "i4", "r3", "r7"]
 
     def sc(n):
+        if n not in names:
+            names.append(n)
         k = names.index(n)
         return A("SC", k, k + 1)
 
     def ix(a, b):
         return A("IDX", a, b)
 
-    def shifted(sem, queues, name, width, src, a, b, reads, slots=range(1, 8)):
-        n = 0
-        for k in slots:
-            for d0, s0, rows in ((0, 16 * k, 128 - 16 * k), (128 - 16 * k, 0, 16 * k)):
-                dma(queues[n % len(queues)], sem, T[name][d0:d0 + rows, width * k + a:width * k + b], src[s0:s0 + rows, a:b],
-                    reads=reads, writes=[A(name, width * k + a, width * k + b)])
-                n += 1
+    def turn(sem, name, to, a, b, by, src=None):
+        for d0, s0, rows in ((0, by, 128 - by), (128 - by, 0, by)):
+            dma("y", sem, T[name][d0:d0 + rows, to:to + b - a], (T[name] if src is None else src)[s0:s0 + rows, a:b], reads=[A(name, a, b)] if src is None else [],
+                writes=[A(name, to, to + b - a)], rows=rows, width=(b - a) * (2 if SCRATCH[name][2] == B16 else 4))
+
+    def shifted(sem, name, width, a, b):
+        for k in range(1, 8):
+            turn(sem, name, width * k + a, a, b, 16 * k)
+        close(sem)
+
+    def doubled(name, width, step):
+        k, sem = 1 << step, "d_%s%d" % (name, step)
+        turn(sem, name, width * k, 0, width * k, 16 * k)
         close(sem)
 
     def paint(q, lines):
@@ -302,292 +423,240 @@ def rank_program(g, core, T, topo):
             else:
                 lin(o, A("JK", 0, n), 1, w)
 
-    def gaps(name):
-        for k in range(8):
-            iota(A(name, LW * k + C, LW * k + LW), [[0, LW - C]], 0, 0)
+    def ln(out, i, p, k=0):
+        ts(out[:5] + (p,), A("LN", 20 * i, 20 * i + 20, p=p), k[:5] + (p,) if is_ap(k) else k, OP.add)
 
     for k in range(8):
-        dma("ys"[k % 2], "d_ln", T.LN[16 * k:16 * k + 16, :], T.ln[:, :], writes=[A("LN", 0, 60)])
+        dma("ys"[k % 2], "d_ln", T.LN[16 * k:16 * k + 16, :], T.ln[:, :], writes=[A("LN", 0, 60)], rows=16)
     close("d_ln")
     dma("y", "d_p", T.LP[:, :], T.p[:, :], writes=[A("LP", 0, 25)])
     close("d_p")
-    dma("y", "d_u", T.UT[:, :], T.u[:, :], writes=[A("UT", 0, 512)])
+    dma("y", "d_u", T.UT[:, :], T.u[:, :], writes=[A("UT", 0, 512)], width=1024)
     close("d_u")
-    dma("y", "d_x", T.R0[:, 0:4 * C], T.x[:, :], writes=[A("R0", 0, 4 * C)])
+    dma("y", "d_x", T.R0[:, 0:4 * C], T.x[:, :], writes=[A("R0", 0, 4 * C)], width=8 * C)
     close("d_x")
-    shifted("d_xa", "y", "R0", 4 * C, T.x, 0, 4 * C, [], range(1, 5))
+    for k in (1, 2):
+        turn("d_x0", "R0", 4 * C * k, 0, 4 * C, 16 * k, T.x)
+    close("d_x0")
 
-    J16, JW, JC, JK, JL = ix(16, 36), ix(36, 52), ix(52, 62), ix(62, 70), ix(70, 75)
+    J16, JW, JC, JK, JL, JR, JH = ix(16, 36), ix(36, 52), ix(52, 62), ix(62, 70), ix(70, 75), ix(76, 92), ix(92, 108)
     iota(ix(0, 1), [[0, 1]], 0, 1, True)
     iota(A("TAB", 0, C), [[1, C]], 0, 0)
     iota(J16, [[16, 20]], 0, 0, True)
-    iota(A("PAT", 32, 49), [[1, 17]], -1, 0)
     iota(A("TAB", C, C + ST), [[1, 80], [1024, 4]], ST, 0)
+    iota(A("PAT", 32, 49), [[1, 17]], -1, 0)
     iota(JC, [[8, 2], [64, 5]], 0, 0, True)
     iota(JW, [[1, 16]], 0, 16, True)
     iota(JK, [[8, 2], [256, 4]], 0, 16, True)
     iota(JL, [[64, 5]], 0, 0, True)
-    iota(A("MM", 0, 64), [[1, 16], [-1, 4]], 0, 0)
-
+    iota(A("MM", 0, 32), [[1, 8], [-1, 4]], 0, 0)
+    iota(JR, [[1, 2], [2, 4], [0, 2]], 8, 0, True)
+    iota(JH, [[0, 8], [16, 2]], 0, 0, True)
     fill(A("JK", 0, 32), 0.0)
     fill(A("WT", 0, 1024), 0.0)
+    for q, lines in zip("vgs", WEIGHTS):
+        paint(q, lines)
+    iota(A("ONE", 0, 520), [[0, 520]], 1, 0)
+    for h in range(2):
+        emit("g", g.affine_select, 1, A("ET", 520 * h, 520 * h + 520), A("ONE", 0, 520), [[-1, 520]], OP.is_equal, 0.0, 2 + h, 4)
+    for b in range(4):
+        o = 520 * (b % 2) + 2 - b // 2 * 2
+        quant("QE", 128 * b, 128 * b + 128, A("ET", o, o + 512))
+    fill(A("T0", C, LW), 0.0)
+    for k in range(8):
+        iota(A("TN", LW * k + C, LW * k + LW), [[0, LW - C]], 0, 0)
+    fill(A("SRA", 160, 176), 0.0)
+    for d in range(2):
+        fill(A("BT%d" % d, 160, 592), 0.0)
+
     for k, (s, m) in enumerate(((0, 15), (4, 7), (4, 1), (5, 3), (2, 3), (0, 3), (0, 7))):
         ts(ix(1 + k, 2 + k), ix(0, 1), s, sh, m, an)
     cp(A("SC", 0, 7), ix(1, 8))
-    paint("s", WEIGHTS[2])
-    paint("g", WEIGHTS[1])
-    gaps("T0")
-    cp(A("LNU", 0, 60), A("LN", 0, 60))
-    cp(A("PU", 0, 25), A("LP", 0, 25))
-    lin(sc("g1600"), sc("g"), 4 * C, 0)
-
-    def values(d):
-        i0 = 40 * d
-        ts(A("LC%d" % d, 0, 20), J16, sc("i"), OP.add)
-        ts(A("LC%d" % d, 0, 20, p=(0, 32)), A("LN", i0, i0 + 20, p=(0, 32)), C, OP.add)
-        act(A("VA", 0, ST), IND(A("TAB", 0, 720), A("LC%d" % d, 0, 20)))
-
-    def others(d):
-        act(A("FT", 0, ST), IND(A("QQ", 0, 960 if d else ST), A("LB%d" % d, 0, 20)))
-        act(A("FT", ST, 480), IND(A("FT", 0, ST), A("CL", 0, 10)))
-        spread(A("SN0", 0, ST), A("FT", 0, ST), "K16")
-        ts(A("WN", 0, 20), A("SN0", 15, ST, 16), sc("b16"), OP.add)
-        for a in range(4):
-            for b in range(4):
-                dma("sy"[b % 2], "d_s%d" % d, T.SRC[32 * b:32 * b + 32, 20 * a:20 * a + 20], T.WN[32 * a:32 * a + 32, :],
-                    reads=[A("WN", 0, 20)], writes=[A("SRC", 0, 80)])
-        close("d_s%d" % d)
-        spread(A("SN0", ST, 480), A("FT", ST, 480), "K16")
-        ts(A("RL%d" % d, 0, 10), A("SN0", ST + 15, 480, 16), sc("b16"), OP.add)
-        cp(A("RL%d" % d, 0, 10, p=(0, 32)), A("CL", 0, 10, p=(0, 32)))
-
-    def candidates(d):
-        i0, i2 = 40 * d, 40 - 40 * d
-        raw = lambda k, h: A("RAW%d" % d, 140 * h + k, 140 * h + 140, NK)
-        src = lambda q: A("SRG", 20 * q, 20 * q + 20)
-        ts(raw(3, 0), A("BG", i2, i2 + 20), 3 * LEVEL, OP.add)
-        ts(raw(3, 1), A("BG", i2, i2 + 20), sc("cgp"), OP.add)
-        lin(raw(5, 0), A("BG", 20, 40), 1, sc("c5"))
-        lin(raw(5, 1), A("BG", 20, 40), 1, 5 * LEVEL)
-        lin(raw(6, 0), A("BG", 60, 80), 1, 6 * LEVEL + 13 * LW)
-        lin(raw(6, 1), A("BG", 80, 100), 1, 6 * LEVEL)
-        lin(A("TM", 0, 20), A("BG", i0, i0 + 20), sc("a02"), sc("c4"))
-        lin(A("SRG", 0, 80), A("SRC", 0, 80), 1, sc("cg"))
-        for h in range(2):
-            lin(raw(0, h), src(OWN), 1, 0)
-            lin(raw(1, h), src(RZ), 1, LEVEL + 6 * LW)
-            ts(raw(2, h), src(RY), 2 * LEVEL + 7 * LW, OP.add)
-        ts(raw(4, 1), src(RX), 4 * LEVEL + 7 * LW, OP.add)
-        ts(A("TM", 20, 40), src(RX), sc("a1"), OP.mult)
-        tt(raw(4, 0), A("TM", 0, 20), A("TM", 20, 40), OP.add)
-        fill(A("D%d" % d, 0, 1), 0.0)
-        tt(A("D%d" % d, 1, 280), A("RAW%d" % d, 0, 279), A("RAW%d" % d, 1, 280), OP.subtract)
-        fill(A("D%d" % d, 0, 280, NK), 1.0e12)
-
-    values(0)
-    cp(IND(A("QQ", ST, 640), A("LNU", 40, 60)), A("TAB", 0, ST))
-    cp(A("LA", 0, 20, p=(0, 64)), A("LN", 20, 40, p=(0, 64)))
-    cp(A("LA", 0, 20, p=(64, 128)), A("LN", 0, 20, p=(64, 128)))
-    for o, n, k in ((0, 16, "i"), (16, 4, "i4")):
-        ts(A("PAT", 64, 64 + n), A("PAT", 33, 33 + n), sc(k), OP.is_equal, -2 * BIG, OP.mult)
-        ts(A("PAT", 80, 80 + n), A("PAT", 32, 32 + n), sc(k), OP.is_equal, BIG, OP.mult)
-        tt(A("PAT", o, o + n), A("PAT", 64, 64 + n), A("PAT", 80, 80 + n), OP.add)
-    ts(A("LI", 0, 25), A("JK", 0, 25), sc("i"), OP.add)
-    act(A("K16", 0, C), IND(A("PAT", 0, 16), A("LI", 0, 25)))
-    lin(sc("s4"), sc("s"), 4, 0)
-    lin(sc("t0"), sc("i4"), 16, sc("r3"))
-    lin(sc("cl"), sc("s"), 4, sc("t0"))
-    lin(sc("t1"), sc("q"), 1, sc("s"))
-    lin(sc("wl"), sc("t1"), -256, 0)
-    cp(IND(A("QQ", 0, ST), A("LA", 0, 20)), A("VA", 0, ST))
-    for h in range(2):
-        dma("y", "d_qi", T.QI[64 * h:64 * h + 64, :], T.QQ[64:128, 0:ST], reads=[A("QQ", 0, ST)], writes=[A("QI", 0, ST)])
-    close("d_qi")
-    cp(A("LB0", 0, 20), A("LN", 40, 60))
-    cp(A("LB0", 0, 20, p=(96, 128)), A("LN", 20, 40, p=(96, 128)))
-    ts(A("CL", 0, 10), JC, sc("cl"), OP.add)
+    for out, x, a, b in (("home", "g", 4 * C, 0), ("t0", "i4", 16, "r3"), ("cl", "s", 4, "t0"), ("t1", "q", 1, "s"), ("wl", "t1", -256, 0),
+                         ("o0", "s", ST, ST), ("o2", "s", -ST, 2 * ST), ("s4", "s", 4, 0), ("r16", "r7", 16, 0), ("kl", "g", -255, 0),
+                         ("clu", "i", 4, "q"), ("cg", "g", -LW, 8 * LW), ("cgp", "s", LW, 3 * LEVEL)):
+        lin(sc(out), sc(x), a, b if isinstance(b, int) else sc(b))
+    act(sc("a"), sc("g"), ACT.Abs, bias=-3.5)
+    ts(sc("a1"), sc("a"), 2.5, OP.is_equal)
+    ts(sc("a3"), sc("a"), 0.5, OP.is_equal)
     ts(sc("b16"), sc("i"), 15, OP.is_lt, -BIG, OP.mult)
-    ts(A("WL", 0, 16), JW, sc("wl"), OP.add)
-    paint("v", WEIGHTS[0])
-    others(0)
-    act(A("WG", 0, 256), IND(A("WT", 0, 1024), A("WL", 0, 16)))
-    lin(A("T0", 0, C), IND(A("TAB", 0, C), A("PU", 0, 25)), 4, sc("g1600"))
-    shifted("d_t0", "y", "T0", LW, T.T0, 0, C, [A("T0", 0, C)])
-    shifted("d_xb", "y", "R0", 4 * C, T.x, 0, 4 * C, [], range(5, 8))
-    dma("y", "d_w", T.QW[:, :].bitcast(dt.uint8), T.wc[:, :], writes=[A("QW", 0, 512)])
-    dma("y", "d_w", T.SW[:, :], T.ws[:, :], writes=[A("SW", 0, 512)])
-    close("d_w")
-    dma("y", "d_v", T.VT[:, :], T.v[:, :], writes=[A("VT", 0, 512)])
-    close("d_v")
-
-    quant("QU", 0, 128, A("UT", 0, 512))
+    ts(sc("b4"), sc("i4"), 3, OP.is_lt, BIG, OP.mult)
     ts(sc("t2"), sc("r7"), 2.5, OP.is_gt)
     ts(sc("t3"), sc("r7"), 5.5, OP.is_gt, sc("t2"), OP.add)
-    ts(sc("t4"), sc("r7"), 16, OP.mult)
-    ts(sc("ul0"), sc("t3"), -47, OP.mult, sc("t4"), OP.add)
-    ts(A("UL", 0, 8), A("JK", 0, 8), sc("ul0"), OP.add)
+    ts(sc("ul0"), sc("t3"), -47, OP.mult, sc("r16"), OP.add)
+    ts(sc("ul1"), sc("t3"), 49, OP.mult, sc("r16"), OP.subtract)
+    for out, x, a, b in (("t5", "a1", -1, 1), ("a02", "a3", -1, "t5"), ("c5", "t5", NEVER, 5 * LEVEL), ("t6", "a1", 7 * LW, 4 * LEVEL),
+                         ("c4", "a3", NEVER, "t6"), ("lim", "b4", 1, "home"), ("off", "lim", -1, "r3"),
+                         ("fs", "t2", 2, -1)):
+        lin(sc(out), sc(x), a, b if isinstance(b, int) else sc(b))
+    lin(sc("fb"), sc("fs"), -0.5, 0)
+    for o, n, k, r, keys in ((0, 16, "i", "i", "K16"), (16, 4, "i4", "r3", "K4")):
+        a, b, l = A("PAT", 64 + o, 64 + o + n), A("PAT", 96 + o, 96 + o + n), A("LI", o // 16 * 26, o // 16 * 26 + 25)
+        ts(a, A("PAT", 33, 33 + n), sc(k), OP.is_equal, -2 * BIG, OP.mult)
+        ts(b, A("PAT", 32, 32 + n), sc(k), OP.is_equal, BIG, OP.mult)
+        tt(A("PAT", o, o + n), a, b, OP.add)
+        ts(l, A("JK", 0, 25), sc(r), OP.add)
+        act(A(keys, 0, C), IND(A("PAT", o, o + n), l))
 
-    def pick_u(d):
-        cp(CW("QUP", 128 * d, 128 * d + 128), IND(CW("QU", 0, 128), A("UL", 8 * d, 8 * d + 8)))
-        act(A("SUP", 128 * d, 128 * d + 128), IND(A("SU", 0, 128), A("UL", 8 * d, 8 * d + 8)))
+    cp(A("PU", 0, 25), A("LP", 0, 25))
+    lin(A("T0", 0, C), IND(A("TAB", 0, C), A("PU", 0, 25)), 4, sc("home"))
+    doubled("T0", LW, 0)
+    ts(A("LC", 0, 20), J16, sc("i"), OP.add)
+    ln(A("LC", 0, 20), 2, (0, 32), C)
+    ln(A("LC", 0, 20), 0, (0, 16), C)
+    act(A("VA", 0, ST), IND(A("TAB", 0, 720), A("LC", 0, 20)))
+    for i, p in ((1, (0, 64)), (2, (64, 128)), (0, (64, 80)), (0, (96, 112))):
+        ln(A("LA", 0, 20), i, p)
+    cp(IND(A("QQ", 0, ST), A("LA", 0, 20)), A("VA", 0, ST))
+    for o, d0, s0, rows in ((1, 0, 64, 64), (1, 64, 64, 64), (2, 0, 80, 48), (2, 48, 64, 16), (2, 64, 80, 48), (2, 112, 64, 16)):
+        dma("y", "d_qi", T.QQ[d0:d0 + rows, ST * o:ST * o + ST], T.QQ[s0:s0 + rows, 0:ST], reads=[A("QQ", 0, ST)], writes=[A("QQ", ST, 960)],
+            rows=rows, width=4 * ST)
+    close("d_qi")
+    turn("d_x1", "R0", 12 * C, 0, 4 * C, 48, T.x)
+    close("d_x1")
+    for i, p in ((0, (0, 96)), (1, (96, 128)), (2, (0, 16)), (2, (32, 48)), (2, (64, 80))):
+        ln(A("LM", 0, 20), i, p)
+    act(A("FM", 0, ST), IND(A("QQ", 0, ST), A("LM", 0, 20)))
+    listed(A("SRA", 0, 20), A("FM", 0, ST), 0)
+    doubled("SRA", 20, 0)
+    doubled("T0", LW, 1)
+    doubled("SRA", 20, 1)
+    turn("d_x2", "R0", 16 * C, 0, 8 * C, 64)
+    close("d_x2")
+    doubled("SRA", 20, 2)
+    doubled("T0", LW, 2)
+    turn("d_x3", "R0", 24 * C, 8 * C, 16 * C, 64)
+    close("d_x3")
+    dma("y", "d_w", T.QW[:, :].bitcast(dt.uint8), T.wc[:, :], writes=[A("QW", 0, 512)], width=2048)
+    dma("y", "d_w", T.SW[:, :], T.ws[:, :], writes=[A("SW", 0, 512)], width=512)
+    close("d_w")
+    dma("y", "d_v", T.VT[:, :], T.v[:, :], writes=[A("VT", 0, 512)], width=1024)
+    close("d_v")
+    quant("QV", 0, 128, A("VT", 0, 512))
+    ts(ix(108, 124), JR, sc("g"), OP.subtract)
+    ts(ix(124, 140), ix(108, 124), 7, an)
+    ts(A("TM", 60, 76), ix(124, 140), 20, OP.mult, sc("i"), OP.add)
+    tt(ix(108, 124), A("TM", 60, 76), JH, OP.add)
+    cp(A("UR", 0, 16), ix(108, 124))
 
-    pick_u(0)
+    ts(A("WL", 0, 16), JW, sc("wl"), OP.add)
+    act(A("WG", 0, 256), IND(A("WT", 0, 1024), A("WL", 0, 16)))
     spread(A("WS", 0, 256), A("WG", 0, 256), "K16")
     ts(A("WS", 256, 272), A("WS", 15, 256, 16), sc("b16"), OP.add)
-    ts(A("MM", 0, 64), A("MM", 0, 64), sc("s4"), OP.is_equal)
+    ts(A("MM", 0, 32), A("MM", 0, 32), sc("s4"), OP.is_equal)
     fill(A("MM", 32, 64), 0.0)
     fill(A("KW", 0, 32), 0.0)
     for k in range(16):
         act(A("KW", 32 + 64 * k, 96 + 64 * k), A("MM", 0, 64), scale=A("WS", 256 + k, 257 + k))
-    fill(A("ONE", 0, 520), 1.0)
-    for h in range(2):
-        emit("g", g.affine_select, 1, A("ET", 520 * h, 520 * h + 520), A("ONE", 0, 520), [[-1, 520]], OP.is_equal, 0.0, 2 + h, 4)
+    quant("QK", 0, 264, A("KW", 0, 1056))
+    ts(A("KL", 0, 8), JK, sc("kl"), OP.add)
+    for k in range(4):
+        d, f = k // 2, k % 2
+        act(A("WG", 256 + 64 * k, 320 + 64 * k), IND(A("WT", 0, 1024), A("KL", 4 * f, 4 * f + 4)), ACT.Abs if d else ACT.Relu, scale=0.5 if d else -1.0,
+            accum_out=sc("w%d" % k))
+        lin(A("CC", k, k + 1), sc("w%d" % k), 1, EXTRA[f])
 
-    def signs(src):
+    ts(ix(140, 200), A("LN", 0, 60), 3, an)
+    ts(ix(200, 260), A("LN", 0, 60), 2, sh)
+    ts(A("TM", 0, 60), ix(140, 200), 1024, OP.mult, sc("cg"), OP.add)
+    tt(A("TM", 80, 140), A("TM", 0, 60), ix(200, 260), OP.add)
+    lin(A("BG", 0, 60), A("TM", 80, 140), 1, ST)
+    ts(A("BG", 60, 80), J16, sc("i"), OP.add)
+    lin(A("BG", 80, 100), A("BG", 60, 80), 1, sc("cg"))
+
+    act(A("MF", 0, ST), A("TAB", 0, ST), scale=1025.0)
+    cp(IND(A("CF", 0, C), A("PU", 0, 20)), A("MF", 0, ST))
+    for d in range(2):
+        ts(A("CLU", 6 * d, 6 * d + 5), JL, sc("clu"), OP.add, sc("o%d" % (2 - 2 * d)), OP.add)
+        lin(A("ML", 80 * d, 80 * d + 80), IND(A("QQ", 0, 960), A("CLU", 6 * d, 6 * d + 5)), 1, ST)
+    lin(A("ML", 160, 240), A("ML", 80, 160), 1024, 0)
+    tt(A("MF", ST, C), A("ML", 160, 240), A("ML", 0, 80), OP.add)
+    cp(IND(A("CF", 0, C), A("PU", 20, 25)), A("MF", ST, C))
+    listed(ix(260, 285), A("CF", 0, C), ST)
+    ts(ix(286, 311), ix(260, 285), 1023, an)
+    cp(A("CM0", 0, 25), ix(286, 311))
+    ts(ix(312, 337), ix(260, 285), 10, sh)
+    cp(A("CM1", 0, 25), ix(312, 337))
+    listed(A("LTL", 0, 5), A("ML", 80, 160), 720)
+
+    quant("QU", 0, 128, A("UT", 0, 512))
+    ts(A("CL", 0, 10), JC, sc("cl"), OP.add)
+    for d in range(2):
+        ts(A("UL", 8 * d, 8 * d + 8), A("JK", 0, 8), sc("ul%d" % d), OP.add, 32 * d, OP.add)
+        cp(CW("QUP", 128 * d, 128 * d + 128), IND(CW("QU", 0, 128), A("UL", 8 * d, 8 * d + 8)))
+        act(A("SUP", 128 * d, 128 * d + 128), IND(A("SU", 0, 128), A("UL", 8 * d, 8 * d + 8)))
+        lb, ft = A("LB", 20 * d, 20 * d + 20), 480 * d
+        ln(lb, 2 - 2 * d, (0, 64))
+        ln(lb, 2 - 2 * d, (64, 96), sc("o%d" % (2 * d)))
+        ln(lb, 1, (96, 128), sc("o%d" % (2 * d)))
+        act(A("FT", ft, ft + ST), IND(A("QQ", 0, 960), lb))
+        act(A("FT", ft + ST, ft + 480), IND(A("FT", ft, ft + ST), A("CL", 0, 10)))
+        listed(A("RL%d" % d, 0, 10), A("FT", ft + ST, ft + 480), 800 + 160 * d)
+        cp(A("RL%d" % d, 0, 10, p=(0, 32)), A("CL", 0, 10, p=(0, 32)))
+        i0, i2, tm = 40 * d, 40 - 40 * d, 140 + 40 * d
+        raw = lambda k, h: A("RAW%d" % d, 140 * h + k, 140 * h + 140, NK)
+        src = lambda q: A("SRG", 128 * d + 32 * q, 128 * d + 32 * q + 20)
+        lin(A("SRG", 128 * d, 128 * d + 128), IND(A("SRA", 0, 176), A("UR", 8 * d, 8 * d + 8)), 1, sc("cg"))
         for h in range(2):
-            quant("QX", 160 * h, 160 * h + 160, A(src, 640 * h, 640 * h + 640))
-            mm(h, "UP", 0, "QX", 160 * h, 160)
-        ts(A("SG0", 0, 160), ps(0, 0, 160), 0.0, OP.is_gt)
-        act(A("SG0", 160, ST), ps(1, 0, 160), ACT.Sign)
+            lin(raw(0, h), src(OWN), 1, 0)
+            lin(raw(1, h), src(RZ), 1, LEVEL + 6 * LW)
+            ts(raw(2, h), src(RY), 2 * LEVEL + 7 * LW, OP.add)
+        ts(raw(3, 0), A("BG", i2, i2 + 20), 3 * LEVEL, OP.add)
+        ts(raw(3, 1), A("BG", i2, i2 + 20), sc("cgp"), OP.add)
+        lin(A("TM", tm, tm + 20), A("BG", i0, i0 + 20), sc("a02"), sc("c4"))
+        ts(A("TM", tm + 20, tm + 40), src(RX), sc("a1"), OP.mult)
+        tt(raw(4, 0), A("TM", tm, tm + 20), A("TM", tm + 20, tm + 40), OP.add)
+        ts(raw(4, 1), src(RX), 4 * LEVEL + 7 * LW, OP.add)
+        lin(raw(5, 0), A("BG", 20, 40), 1, sc("c5"))
+        lin(raw(5, 1), A("BG", 20, 40), 1, 5 * LEVEL)
+        lin(raw(6, 0), A("BG", 60, 80), 1, 6 * LEVEL + 13 * LW)
+        lin(raw(6, 1), A("BG", 80, 100), 1, 6 * LEVEL)
+        tt(A("D%d" % d, 1, 280), A("RAW%d" % d, 0, 279), A("RAW%d" % d, 1, 280), OP.subtract)
+        fill(A("D%d" % d, 0, 280, NK), 1.0e12)
 
-    def back_signs():
-        mm(4, "UP", 128, "QX", 0, ST)
-        act(A("SG1", 0, ST), ps(4, 0, ST), ACT.Sign)
-
-    def gather_signs(d):
+    def signs(d, src=None):
         if d == 0:
-            ts(A("BT", 0, 160), IND(A("SG0", 0, ST), A("RL0", 0, 10)), 0.0, OP.is_gt)
+            for h in range(2):
+                quant("QX", 160 * h, 160 * h + 160, A(src, 640 * h, 640 * h + 640))
+                mm(h, "UP", 0, "QX", 160 * h, 160)
+                ts(A("SG0", 160 * h, 160 * h + 160), ps(h, 0, 160), 0.0, OP.is_gt)
+            cp(A("BT0", 0, 160), IND(A("SG0", 0, ST), A("RL0", 0, 10)))
         else:
-            act(A("BT", 512, 672), IND(A("SG1", 0, ST), A("RL1", 0, 10)), ACT.Sign, scale=sc("fs"), bias=sc("fb"))
-
-    def weigh(d):
-        quant("QB%d" % d, 0, 128, A("BT", 512 * d, 512 * d + 512))
+            mm(4, "UP", 128, "QX", 0, ST)
+            act(A("SG1", 0, ST), ps(4, 0, ST), ACT.Sign)
+            act(A("BT1", 0, 160), IND(A("SG1", 0, ST), A("RL1", 0, 10)), ACT.Sign, scale=sc("fs"), bias=sc("fb"))
+        quant("QB%d" % d, 0, 148, A("BT%d" % d, 0, 592))
         for f in range(2):
             for m in range(2):
                 mm(2 + 3 * d + f, "K", 128 * f + 8 - 8 * m, "QB%d" % d, 20 * m, 128, m == 0, m == 1)
-
-    def whole(d):
-        for f in range(2):
-            o, k = A("KI%d" % d, 20 * f, 20 * f + 20), ps(2 + 3 * d + f, 0, 20)
-            if d == 0:
-                ts(o, k, A("CC", f, f + 1), OP.add)
-            else:
-                ts(o, k, 0.5, OP.mult, A("CC", 2 + f, 3 + f), OP.add)
-
-    def sums(d):
-        for f in range(2):
-            w = IND(A("WT", 0, 1024), A("KL", 4 * f, 4 * f + 4))
-            act(A("WG", 0, 64), w, ACT.Abs if d else ACT.Relu, scale=0.5 if d else -1.0, accum_out=sc("t%d" % (7 + f)))
-            lin(A("CC", 2 * d + f, 2 * d + f + 1), sc("t%d" % (7 + f)), 1, EXTRA[f])
+            ts(A("KI%d" % d, 20 * f, 20 * f + 20), ps(2 + 3 * d + f, 0, 20), 0.5 if d else 1.0, OP.mult, A("CC", 2 * d + f, 2 * d + f + 1), OP.add)
 
     def choose(d):
-        ops = []
         for k, (s, m, bits) in enumerate(FIELDS):
-            ops.append(lambda k=k, s=s, m=m + sum(1 << (b - s) for b in bits): ts(A("KC%d" % d, k, 280, NK), A("KI%d" % d, 0, 40), s, sh, m, an))
-        return ops + [
-            lambda: ts(A("KF%d" % d, 0, 280), A("KC%d" % d, 0, 280), LW, OP.mult),
-            lambda: emit("v", V.tensor_tensor_scan, 1, A("SK%d" % d, 0, 280), A("D%d" % d, 0, 280), A("KF%d" % d, 0, 280), 0.0, OP.add, OP.min),
-            lambda: tt(A("RS%d" % d, 0, 40), A("SK%d" % d, NK - 1, 280, NK), A("RAW%d" % d, NK - 1, 280, NK), OP.add),
-            lambda: ts(A("RS%d" % d, 40, 80), A("RS%d" % d, 0, 40), 8 * LW - 1, an),
-            lambda: cp(A("LU%d" % d, 0, 40), A("RS%d" % d, 40, 80)),
-        ]
+            ts(A("KC%d" % d, k, 280, NK), A("KI%d" % d, 0, 40), s, sh, m + sum(1 << (b - s) for b in bits), an)
+        ts(A("KF%d" % d, 0, 280), A("KC%d" % d, 0, 280), LW, OP.mult)
+        emit("v", V.tensor_tensor_scan, 1, A("SK%d" % d, 0, 280), A("D%d" % d, 0, 280), A("KF%d" % d, 0, 280), 0.0, OP.add, OP.min)
+        tt(A("RS%d" % d, 0, 40), A("SK%d" % d, NK - 1, 280, NK), A("RAW%d" % d, NK - 1, 280, NK), OP.add)
+        ts(A("RS%d" % d, 40, 80), A("RS%d" % d, 0, 40), 8 * LW - 1, an)
+        cp(A("LU%d" % d, 0, 40), A("RS%d" % d, 40, 80))
 
-    def run(ops):
-        for f in ops:
-            f()
-
-    def lookup(d, table, out, scalar_only=False):
+    def lookup(d, table, out, first=cp):
         act(A(out, ST, 640), IND(A(table, 0, 8 * LW), A("LU%d" % d, 20, 40)))
-        (act if scalar_only else cp)(A(out, 0, ST), IND(A(table, 0, 8 * LW), A("LU%d" % d, 0, 20)))
+        first(A(out, 0, ST), IND(A(table, 0, 8 * LW), A("LU%d" % d, 0, 20)))
 
-    def by_column(d, c0, cm, c1):
+    def offsets(out, d, c0, cm, c1):
         for f, a, b in ((act, cm, c1), (cp, c0, cm)):
             if b > a:
                 f(A("MG%d" % d, a, b), IND(A("FL%d" % d, 0, 640), A("CM%d" % d, a // 16, b // 16)))
-
-    def offsets(out, d, c0, c1):
         uo, a, b, last = "UO%d" % d, c0 // 4, c1 // 4, A("SN%d" % d, c0 + 3, c1, 4)
-        return [
-            lambda: spread(A("SN%d" % d, c0, c1), A("MG%d" % d, c0, c1), "K4"),
-            lambda: ts(A(uo, a, b), last, sc("lim"), OP.is_lt, W8, OP.mult),
-            lambda: tt(A(uo, 100 + a, 100 + b), last, A(uo, a, b), OP.add),
-            lambda: ts(A(out, a, b), A(uo, 100 + a, 100 + b), sc("off"), OP.add),
-        ]
+        spread(A("SN%d" % d, c0, c1), A("MG%d" % d, c0, c1), "K4")
+        ts(A(uo, a, b), last, sc("lim"), OP.is_lt, W8, OP.mult)
+        tt(A(uo, 100 + a, 100 + b), last, A(uo, a, b), OP.add)
+        ts(A(out, a, b), A(uo, 100 + a, 100 + b), sc("off"), OP.add)
 
     def pull(dst, win, offs, c0, cm, c1):
         for f, a, b in ((act, cm, c1), (cp, c0, cm)):
-            if b > a:
-                f(A(dst, 4 * a, 4 * b), IND(A(win, 0, W8), A(offs, a // 4, b // 4)))
-
-    signs("R0")
-    fill(A("BT", 160, 1104), 0.0)
-    lin(sc("kl"), sc("g"), -255, 0)
-    act(A("MF", 0, ST), A("TAB", 0, ST), scale=1025.0)
-    ts(A("KL", 0, 8), JK, sc("kl"), OP.add)
-    quant("QB0", 20, 148, A("BT", 592, 1104))
-    gather_signs(0)
-    cp(IND(A("CF", 0, C), A("PU", 0, 20)), A("MF", 0, ST))
-    quant("QK", 0, 264, A("KW", 0, 1056))
-    weigh(0)
-    sums(0)
-    lin(sc("clu"), sc("i"), 4, sc("q"))
-    lin(sc("cg"), sc("g"), -LW, 8 * LW)
-    lin(sc("cgp"), sc("s"), LW, 3 * LEVEL)
-    act(sc("a"), sc("g"), ACT.Abs, bias=-3.5)
-    ts(A("CLU", 0, 5), JL, sc("clu"), OP.add)
-    lin(A("ML", 0, 80), IND(A("QQ", ST, 640), A("CLU", 0, 5)), 1, ST)
-    lin(A("ML", 80, 160), IND(A("QI", 0, ST), A("CLU", 0, 5)), 1, ST)
-    lin(A("ML", 160, 240), A("ML", 80, 160), 1024, 0)
-    ts(ix(80, 140), A("LN", 0, 60), 3, an)
-    ts(ix(140, 200), A("LN", 0, 60), 2, sh)
-    ts(A("TM", 0, 60), ix(80, 140), 1024, OP.mult, sc("cg"), OP.add)
-    ts(A("BG", 60, 80), J16, sc("i"), OP.add)
-    tt(A("UO0", 0, 60), A("TM", 0, 60), ix(140, 200), OP.add)
-    ts(sc("a1"), sc("a"), 2.5, OP.is_equal)
-    ts(sc("a3"), sc("a"), 0.5, OP.is_equal)
-    lin(A("BG", 0, 60), A("UO0", 0, 60), 1, ST)
-    lin(A("BG", 80, 100), A("BG", 60, 80), 1, sc("cg"))
-    lin(sc("t5"), sc("a1"), -1, 1)
-    lin(sc("a02"), sc("a3"), -1, sc("t5"))
-    lin(sc("c5"), sc("t5"), NEVER, 5 * LEVEL)
-    lin(sc("t6"), sc("a1"), 7 * LW, 4 * LEVEL)
-    lin(sc("c4"), sc("a3"), NEVER, sc("t6"))
-    tt(A("MF", ST, C), A("ML", 160, 240), A("ML", 0, 80), OP.add)
-    cp(IND(A("CF", 0, C), A("PU", 20, 25)), A("MF", ST, C))
-    ts(A("LI", 26, 51), A("JK", 0, 25), sc("r3"), OP.add)
-    spread(A("SN0", 0, C), A("CF", 0, C), "K16")
-    whole(0)
-    for b in range(4):
-        o = 520 * (b % 2) + 2 - b // 2 * 2
-        quant("QE", 128 * b, 128 * b + 128, A("ET", o, o + 512))
-    candidates(0)
-    act(A("K4", 0, C), IND(A("PAT", 16, 20), A("LI", 26, 51)))
-    ts(ix(80, 105), A("SN0", 15, C, 16), sc("b16"), OP.add)
-    ts(ix(110, 135), ix(80, 105), 1023, an)
-    cp(A("CM0", 0, 25), ix(110, 135))
-    ts(sc("t0"), sc("i4"), 3, OP.is_lt, BIG, OP.mult)
-    lin(sc("lim"), sc("t0"), 1, sc("g1600"))
-    lin(sc("off"), sc("lim"), -1, sc("r3"))
-
-    def back_lists():
-        def rest():
-            ts(sc("ul1"), sc("t3"), 49, OP.mult, sc("t4"), OP.subtract)
-            ts(A("UL", 8, 16), A("JK", 0, 8), sc("ul1"), OP.add, 32, OP.add)
-            pick_u(1)
-            lin(sc("fs"), sc("t2"), 2, -1)
-            lin(sc("fb"), sc("fs"), -0.5, 0)
-            quant("QB1", 20, 148, A("BT", 592, 1104))
-            ts(ix(110, 135), ix(80, 105), 10, sh)
-            cp(A("CM1", 0, 25), ix(110, 135))
-            spread(A("SN1", 0, 80), A("ML", 80, 160), "K16")
-            ts(A("LTL", 0, 5), A("SN1", 15, 80, 16), sc("b16"), OP.add)
-            sums(1)
-        ops = [lambda: cp(IND(A("QQ", 640, 960), A("LNU", 20, 40)), A("VA", 0, ST))]
-        for p, a, k in (((0, 32), 0, 640), ((32, 64), 0, 0), ((64, 96), 0, ST), ((96, 128), 20, ST)):
-            ops.append(lambda p=p, a=a, k=k: ts(A("LB1", 0, 20, p=p), A("LN", a, a + 20, p=p), k, OP.add))
-        return ops + [lambda: None] * 4 + [rest]
-
-    values(1)
+            f(A(dst, 4 * a, 4 * b), IND(A(win, 0, W8), A(offs, a // 4, b // 4)))
 
     for r in range(STEPS):
         HQ, HS = "HQ%d" % r, "HS%d" % r
@@ -596,46 +665,29 @@ def rank_program(g, core, T, topo):
         n_arr = sum(mask_of(topo, T.cores[peer] if c is None else c, core)[1] for c in hops(T, topo, peer, r))
         arrives([A(HQ, 0, KX), A(HS, 0, KX)], "arr%d" % r, n_arr)
 
-        def products(c0, n):
+        def layer(name, c0, c1):
+            n, m = c1 - c0, max(c1 - c0, 128)
             for b in range(4):
-                mm(b, "W", 128 * b, HQ, c0, n, rs=HS)
-                mm(4 + b, "E", 128 * b, HQ, c0, n, rs=HS)
-
-        def layer(c0, c1, buf, meanwhile=()):
-            n = c1 - c0
-            meanwhile = list(meanwhile)
+                mm(b, "W", 128 * b, HQ, c0, m, rs=HS)
+                mm(4 + b, "E", 128 * b, HQ, c0, m, rs=HS)
             for b in range(4):
-                l = A(buf, n * b, n * b + n)
+                l = A("R" + name, n * b, n * b + n)
                 act(l, ps(b, 0, n), ACT.Relu, scale=0.015625)
-                if meanwhile:
-                    run(meanwhile.pop(0))
                 tt(A(NEW, 4 * c0 + b, 4 * c1, 4), l, ps(4 + b, 0, n), OP.add)
+            shifted("d_y%s%d" % ({"A": "a", "B": "b", "C": "l"}[name], r), NEW, 4 * C, 4 * c0, 4 * c1)
 
-        def shift(name, queues, c0, c1):
-            shifted("d_%s%d" % (name, r), queues, NEW, 4 * C, T[NEW], 4 * c0, 4 * c1, [A(NEW, 4 * c0, 4 * c1)])
-
+        signs(0, "XT" if r else "R0")
         if r:
-            signs("XT")
-            gather_signs(0)
-            weigh(0)
-            back_signs()
-            gather_signs(1)
-            whole(0)
-        run(choose(0))
+            signs(1)
+        choose(0)
         lookup(0, "TN" if r else "T0", "FL0")
-        if r:
-            weigh(1)
-        by_column(0, 0, 96, CA)
-        run(offsets("OFZ", 0, 0, CA))
+        offsets("OFZ", 0, 0, 96, CA)
         pull("ZT", OLD, "OFZ", KX, 160, CA)
-        if r:
-            whole(1)
         quant(HQ, KX, CA, A("ZT", 4 * KX, 4 * CA), HS)
-        products(KX, CA - KX)
         pull("ZT", OLD, "OFZ", 0, 48, KX)
-        by_column(0, CA, CA, C)
         quant("QS", 0, 128, A("ZT", 0, 512))
-        for k, c in enumerate(hops(T, topo, rank, r)):
+        way = hops(T, topo, rank, r)
+        for k, c in enumerate(way):
             to = T.cores[peer] if c is None else c
             m, n = mask_of(topo, core, to)
             if k == 0:
@@ -645,61 +697,43 @@ def rank_program(g, core, T, topo):
                 o = T[HS if c is None else "SR"][:, 0:KX]
                 i, rd = T.SS[:, 0:KX], [A("SS", 0, KX)]
             remote(o, i, rd, "arr%d" % r if c is None else "rarr", "snt%d" % r, topo.addr(to, core), m, n)
-        close("snt%d" % r)
-        if r == 0:
-            gaps("TN")
-        of = offsets("OFZ", 0, CA, C)
-        layer(KX, CA, "RA", [[], of[:1], of[1:3], of[3:]])
-        shift("ya", "y", KX, CA)
+        close("snt%d" % r, [A(HQ, 0, KX), A(HS, 0, KX)], 4.0 if way[0] is not None else 1.5 if r else 2.5)
+        offsets("OFZ", 0, CA, CA, C)
         pull("ZT", OLD, "OFZ", CA, 312, C)
         quant(HQ, CA, C, A("ZT", 4 * CA, 4 * C), HS)
-        products(CA, C - CA)
-        ch = choose(1) if r else back_lists()
-        layer(CA, C, "RB", [ch[:4], ch[4:7], ch[7:8], ch[8:9]])
+        layer("A", KX, CA)
+        layer("B", CA, C)
         if r == 0:
-            others(1)
-        shift("yb", "y", CA, C)
-        products(0, 128)
-        cols = ST if r < STEPS - 1 else C
-        if r == 0:
-            layer(0, KX, "RC", [ch[9:]])
-            shift("yl", "y", 0, KX)
-            back_signs()
-            gather_signs(1)
-            weigh(1)
-            candidates(1)
-            whole(1)
-            run(choose(1))
-            lookup(1, "T0", "FL1")
-        else:
-            run(ch[9:])
-            lookup(1, "T0", "FL1")
-            layer(0, KX, "RC")
-            shift("yl", "y", 0, KX)
+            signs(1)
+        layer("C", 0, KX)
+        choose(1)
+        lookup(1, "T0", "FL1")
         if r < STEPS - 1:
             act(A("TN", 0, ST), A("FL1", 0, ST))
             act(A("TN", ST, C), IND(A("FL1", 0, 640), A("LTL", 0, 5)))
-            shifted("d_tn%d" % r, "y", "TN", LW, T.TN, 0, C, [A("TN", 0, C)])
-        by_column(1, 0, 224, cols)
-        run(offsets("OFX", 1, 0, cols))
-        if r < STEPS - 1:
-            if r == 0:
-                quant("QV", 0, 128, A("VT", 0, 512))
+            shifted("d_tn%d" % r, "TN", LW, 0, C)
+            offsets("OFX", 1, 0, 224, ST)
             pull("XT", NEW, "OFX", 0, 160, ST)
         else:
-            lookup(0, "T0", "FLO", True)
+            offsets("OFX", 1, 0, 224, C)
+            lookup(0, "T0", "FLO", act)
             act(A("OPF", 0, C), IND(A("FLO", 0, 640), A("CM0", 0, 25)), scale=0.25)
             for k in range(8):
-                dma("y", "d_op", T.op[k:k + 1, :], T.OPF[16 * k:16 * k + 1, :], reads=[A("OPF", 0, C)])
+                dma("y", "d_op", T.op[k:k + 1, :], T.OPF[16 * k:16 * k + 1, :], reads=[A("OPF", 0, C)], rows=1)
             close("d_op")
-            pull("XT", NEW, "OFX", 0, 200, C)
 
-    quant("QX", 0, C, A("XT", 0, 4 * C))
-    mm(0, "V", 0, "QX", 0, C)
-    dma("s", "d_out", T.oc[:, :], T.QX[:, :].bitcast(dt.uint8), reads=[A("QX", 0, C)])
+    H = C // 2
+    for h, cm in ((0, 104), (1, 280)):
+        a, b = H * h, H * h + H
+        pull("XT", NEW, "OFX", a, cm, b)
+        quant("QX", a, b, A("XT", 4 * a, 4 * b))
+        mm(h, "V", 0, "QX", a, H)
+        dma("y", "d_o%d" % h, T.oc[:, 4 * a:4 * b], T.QX[:, a:b].bitcast(dt.uint8), reads=[A("QX", a, b)], width=4 * H)
+        close("d_o%d" % h)
+        (cp if h else act)(A("YO", a, b), ps(h, 0, H))
+        dma("sy"[h], "d_y%d" % h, T.y[:, a:b], T.YO[:, a:b], reads=[A("YO", a, b)], width=4 * H)
+        close("d_y%d" % h)
     for k in range(4):
-        dma("y", "d_out", T.osc[4 * k:4 * k + 4, :], T.SX[32 * k:32 * k + 4, :], reads=[A("SX", 0, C)])
-    cp(A("YO", 0, C), ps(0, 0, C))
-    dma("y", "d_out", T.y[:, :], T.YO[:, :], reads=[A("YO", 0, C)])
+        dma("s", "d_out", T.osc[4 * k:4 * k + 4, :], T.SX[32 * k:32 * k + 4, :], reads=[A("SX", 0, C)], rows=4)
     close("d_out")
     finish()

@@ -8,10 +8,11 @@ LW = 512
 OP = AluOpType
 ACT = ActivationFunctionType
 CODES = "float8_e4m3fn_x4"
-NK = 7
+NK = 8
+KW = 40 * NK
 LEVEL, NEVER, BIG = 24 * LW, 512 * LW, 2 ** 23
 
-G2, G1B, G1A, EX, E1, E0, NE = 11, 12, 13, 15, 17, 19, 21
+NE, G2, G1B, G1A, EX, E1, E0 = 10, 12, 13, 14, 16, 18, 20
 FIELDS = [(0, 1, (G2, E1, NE)), (1, 3, (G2, E1)), (3, 1, (G2, E0)), (4, 1, (G2,)), (5, 1, (G1B, G1A, EX)), (6, 1, (G1B, G1A)), (7, 7, ())]
 EXTRA = (2 ** NE + 2 ** G2, 2 ** NE + 2 ** G1A)
 OWN, RZ, RY, RX = 0, 1, 2, 3
@@ -32,14 +33,14 @@ WEIGHTS = [
 F32, B16, I32, U16 = "float32", "bfloat16", "int32", "uint16"
 SCRATCH = {}
 for _t, _l in (
-    (B16, (("R0", W8), ("R1", W8), ("XT", 4 * C), ("ZT", 4 * C), ("UT", 512), ("VT", 512), ("ET", 1040), ("ONE", 520), ("WT", 1024), ("KW", 1056),
+    (B16, (("R0", W8), ("R1", W8), ("XT", 4 * C), ("ZT", 4 * C), ("ZS", 512), ("UT", 512), ("VT", 512), ("ET", 1040), ("ONE", 520), ("WT", 1024), ("KW", 1056),
            ("MM", 64), ("BT0", 592), ("BT1", 592), ("SG0", ST), ("SG1", ST), ("PAT", 128), ("K16", C), ("K4", C), ("JK", 32))),
-    (I32, (("LP", 25), ("LN", 60), ("IDX", 340), ("KI0", 40), ("KI1", 40), ("KC0", 280), ("KC1", 280), ("RS0", 80), ("RS1", 80))),
+    (I32, (("LP", 25), ("LN", 60), ("IDX", 340), ("KI0", 40), ("KI1", 40), ("KC0", KW), ("KC1", KW), ("SK0", KW), ("SK1", KW), ("RS0", 40), ("RS1", 40))),
     (U16, (("PU", 26), ("LA", 20), ("LB", 40), ("LC", 20), ("LM", 20), ("UR", 16), ("CL", 10), ("RL0", 10), ("RL1", 10), ("WL", 16),
            ("KL", 8), ("LI", 52), ("UL", 16), ("CLU", 12), ("CM0", 26), ("CM1", 26), ("LTL", 6), ("LU0", 40), ("LU1", 40), ("OFZ", 100), ("OFX", 100))),
     (F32, (("TAB", 720), ("SC", 48), ("CC", 4), ("WG", 512), ("WS", 272), ("QQ", 960), ("VA", ST), ("FT", 960), ("FM", ST), ("SP", 1120),
            ("MG0", C), ("SN0", C), ("MG1", C), ("SN1", C), ("UO0", 200), ("UO1", 200), ("SRA", 176), ("SRG", 256), ("BG", 100), ("TM", 220),
-           ("RAW0", 280), ("RAW1", 280), ("D0", 280), ("D1", 280), ("KF0", 280), ("KF1", 280), ("SK0", 280), ("SK1", 280), ("MF", C), ("ML", 240),
+           ("RAW0", KW), ("RAW1", KW), ("D0", KW), ("D1", KW), ("MF", C), ("ML", 240),
            ("CF", C), ("T0", 8 * LW), ("TN", 8 * LW), ("FL0", 640), ("FL1", 640), ("FLO", 640), ("OPF", C), ("RA", 512), ("RB", 704), ("RC", 384),
            ("YO", C))),
 ):
@@ -53,7 +54,7 @@ for _r in range(STEPS):
     SCRATCH["HQ%d" % _r] = ("sbuf", [128, C], CODES)
     SCRATCH["HS%d" % _r] = ("sbuf", [128, C], "uint8")
 DMAS = ["d_ln", "d_p", "d_u", "d_x", "d_v", "d_w", "d_tn0", "d_tn1", "d_out", "d_op", "d_qi", "d_o0", "d_o1", "d_y0", "d_y1"]
-DMAS += ["d_x%d" % k for k in range(4)] + ["d_%s%d" % (k, r) for k in ("T0", "SRA", "ya", "yb", "yl") for r in range(3)]
+DMAS += ["d_x%d" % k for k in range(4)] + ["d_%s%d" % (k, r) for k in ("T0", "SRA", "yA", "yB", "yC", "yD") for r in range(3)]
 SEMAPHORES = ["ev", "es", "et", "eg", "rarr", "rsent"] + DMAS + ["arr%d" % r for r in range(STEPS)] + ["snt%d" % r for r in range(STEPS)]
 
 
@@ -230,7 +231,7 @@ def builder(g, T):
     return emit, dma, close, remote, arrives, finish
 
 
-CYCLE, WAKE, SLACK, ISSUE, WAY, BYTE, ROW, CALL = 0.00095, 0.15, 0.05, 0.1, 0.9, 1 / 600e3, 0.02 / 16, 0.5
+CYCLE, WAKE, SLACK, ISSUE, WAY, BYTE, ROW, CALL = 0.0009, 0.22, 0.07, 0.1, 0.9, 1 / 800e3, 0.012 / 16, 0.5
 
 
 def planner(issue):
@@ -398,14 +399,14 @@ def rank_program(g, core, T, topo):
     def ix(a, b):
         return A("IDX", a, b)
 
-    def turn(sem, name, to, a, b, by, src=None):
+    def turn(sem, name, to, a, b, by, src=None, q="y"):
         for d0, s0, rows in ((0, by, 128 - by), (128 - by, 0, by)):
-            dma("y", sem, T[name][d0:d0 + rows, to:to + b - a], (T[name] if src is None else src)[s0:s0 + rows, a:b], reads=[A(name, a, b)] if src is None else [],
+            dma(q, sem, T[name][d0:d0 + rows, to:to + b - a], (T[name] if src is None else src)[s0:s0 + rows, a:b], reads=[A(name, a, b)] if src is None else [],
                 writes=[A(name, to, to + b - a)], rows=rows, width=(b - a) * (2 if SCRATCH[name][2] == B16 else 4))
 
-    def shifted(sem, name, width, a, b):
-        for k in range(1, 8):
-            turn(sem, name, width * k + a, a, b, 16 * k)
+    def shifted(sem, name, width, a, b, slots=range(1, 8), q="y"):
+        for k in slots:
+            turn(sem, name, width * k + a, a, b, 16 * k, q=q)
         close(sem)
 
     def doubled(name, width, step):
@@ -466,6 +467,7 @@ def rank_program(g, core, T, topo):
     for k in range(8):
         iota(A("TN", LW * k + C, LW * k + LW), [[0, LW - C]], 0, 0)
     fill(A("SRA", 160, 176), 0.0)
+    fill(A("ZS", 4 * KX, 512), 0.0)
     for d in range(2):
         fill(A("BT%d" % d, 160, 592), 0.0)
 
@@ -554,7 +556,7 @@ def rank_program(g, core, T, topo):
         d, f = k // 2, k % 2
         act(A("WG", 256 + 64 * k, 320 + 64 * k), IND(A("WT", 0, 1024), A("KL", 4 * f, 4 * f + 4)), ACT.Abs if d else ACT.Relu, scale=0.5 if d else -1.0,
             accum_out=sc("w%d" % k))
-        lin(A("CC", k, k + 1), sc("w%d" % k), 1, EXTRA[f])
+        lin(A("CC", k, k + 1), sc("w%d" % k), LW, LW * EXTRA[f])
 
     ts(ix(140, 200), A("LN", 0, 60), 3, an)
     ts(ix(200, 260), A("LN", 0, 60), 2, sh)
@@ -594,7 +596,9 @@ def rank_program(g, core, T, topo):
         listed(A("RL%d" % d, 0, 10), A("FT", ft + ST, ft + 480), 800 + 160 * d)
         cp(A("RL%d" % d, 0, 10, p=(0, 32)), A("CL", 0, 10, p=(0, 32)))
         i0, i2, tm = 40 * d, 40 - 40 * d, 140 + 40 * d
-        raw = lambda k, h: A("RAW%d" % d, 140 * h + k, 140 * h + 140, NK)
+        raw = lambda k, h: A("RAW%d" % d, KW // 2 * h + k, KW // 2 * h + KW // 2, NK)
+        fill(A("RAW%d" % d, NK - 1, KW, NK), 0.0)
+        fill(A("KC%d" % d, NK - 1, KW, NK), 2 ** 30)
         src = lambda q: A("SRG", 128 * d + 32 * q, 128 * d + 32 * q + 20)
         lin(A("SRG", 128 * d, 128 * d + 128), IND(A("SRA", 0, 176), A("UR", 8 * d, 8 * d + 8)), 1, sc("cg"))
         for h in range(2):
@@ -611,8 +615,8 @@ def rank_program(g, core, T, topo):
         lin(raw(5, 1), A("BG", 20, 40), 1, 5 * LEVEL)
         lin(raw(6, 0), A("BG", 60, 80), 1, 6 * LEVEL + 13 * LW)
         lin(raw(6, 1), A("BG", 80, 100), 1, 6 * LEVEL)
-        tt(A("D%d" % d, 1, 280), A("RAW%d" % d, 0, 279), A("RAW%d" % d, 1, 280), OP.subtract)
-        fill(A("D%d" % d, 0, 280, NK), 1.0e12)
+        tt(A("D%d" % d, 1, KW), A("RAW%d" % d, 0, KW - 1), A("RAW%d" % d, 1, KW), OP.subtract)
+        fill(A("D%d" % d, 0, KW, NK), 1.0e12)
 
     def signs(d, src=None):
         if d == 0:
@@ -629,16 +633,14 @@ def rank_program(g, core, T, topo):
         for f in range(2):
             for m in range(2):
                 mm(2 + 3 * d + f, "K", 128 * f + 8 - 8 * m, "QB%d" % d, 20 * m, 128, m == 0, m == 1)
-            ts(A("KI%d" % d, 20 * f, 20 * f + 20), ps(2 + 3 * d + f, 0, 20), 0.5 if d else 1.0, OP.mult, A("CC", 2 * d + f, 2 * d + f + 1), OP.add)
+            ts(A("KI%d" % d, 20 * f, 20 * f + 20), ps(2 + 3 * d + f, 0, 20), LW // (1 + d), OP.mult, A("CC", 2 * d + f, 2 * d + f + 1), OP.add)
 
     def choose(d):
         for k, (s, m, bits) in enumerate(FIELDS):
-            ts(A("KC%d" % d, k, 280, NK), A("KI%d" % d, 0, 40), s, sh, m + sum(1 << (b - s) for b in bits), an)
-        ts(A("KF%d" % d, 0, 280), A("KC%d" % d, 0, 280), LW, OP.mult)
-        emit("v", V.tensor_tensor_scan, 1, A("SK%d" % d, 0, 280), A("D%d" % d, 0, 280), A("KF%d" % d, 0, 280), 0.0, OP.add, OP.min)
-        tt(A("RS%d" % d, 0, 40), A("SK%d" % d, NK - 1, 280, NK), A("RAW%d" % d, NK - 1, 280, NK), OP.add)
-        ts(A("RS%d" % d, 40, 80), A("RS%d" % d, 0, 40), 8 * LW - 1, an)
-        cp(A("LU%d" % d, 0, 40), A("RS%d" % d, 40, 80))
+            ts(A("KC%d" % d, k, KW, NK), A("KI%d" % d, 0, 40), s, sh, LW * (m + sum(1 << (b - s) for b in bits)), an)
+        emit("v", V.tensor_tensor_scan, 1, A("SK%d" % d, 0, KW), A("D%d" % d, 0, KW), A("KC%d" % d, 0, KW), 0.0, OP.add, OP.min)
+        ts(A("RS%d" % d, 0, 40), A("SK%d" % d, NK - 1, KW, NK), 8 * LW - 1, an)
+        cp(A("LU%d" % d, 0, 40), A("RS%d" % d, 0, 40))
 
     def lookup(d, table, out, first=cp):
         act(A(out, ST, 640), IND(A(table, 0, 8 * LW), A("LU%d" % d, 20, 40)))
@@ -674,18 +676,23 @@ def rank_program(g, core, T, topo):
                 l = A("R" + name, n * b, n * b + n)
                 act(l, ps(b, 0, n), ACT.Relu, scale=0.015625)
                 tt(A(NEW, 4 * c0 + b, 4 * c1, 4), l, ps(4 + b, 0, n), OP.add)
-            shifted("d_y%s%d" % ({"A": "a", "B": "b", "C": "l"}[name], r), NEW, 4 * C, 4 * c0, 4 * c1)
+            if c0:
+                shifted("d_y%s%d" % (name, r), NEW, 4 * C, 4 * c0, 4 * c1)
+            else:
+                shifted("d_yC%d" % r, NEW, 4 * C, 0, 4 * c1, range(1, 5))
+                shifted("d_yD%d" % r, NEW, 4 * C, 0, 4 * c1, range(5, 8), "s")
 
         signs(0, "XT" if r else "R0")
         if r:
             signs(1)
         choose(0)
         lookup(0, "TN" if r else "T0", "FL0")
-        offsets("OFZ", 0, 0, 96, CA)
+        offsets("OFZ", 0, 0, KX, KX)
+        pull("ZS", OLD, "OFZ", 0, 48, KX)
+        quant("QS", 0, 128, A("ZS", 0, 512))
+        offsets("OFZ", 0, KX, KX, CA)
         pull("ZT", OLD, "OFZ", KX, 160, CA)
         quant(HQ, KX, CA, A("ZT", 4 * KX, 4 * CA), HS)
-        pull("ZT", OLD, "OFZ", 0, 48, KX)
-        quant("QS", 0, 128, A("ZT", 0, 512))
         way = hops(T, topo, rank, r)
         for k, c in enumerate(way):
             to = T.cores[peer] if c is None else c

@@ -1,16 +1,19 @@
-from concourse.mybir import dt, AluOpType, ActivationFunctionType
+from concourse.mybir import dt, AluOpType, ActivationFunctionType, AxisListType
 
 C, ST, KX, STEPS, N = 400, 320, 96, 3, 8
 CA = 224
 MATES = [1, 2, 4]
-W8 = 8 * 4 * C
+W4 = 4 * C
+WIN, MID = 15 * W4, 7 * W4
 LW = 512
 OP = AluOpType
 ACT = ActivationFunctionType
 CODES = "float8_e4m3fn_x4"
 NK = 8
 KW = 40 * NK
-LEVEL, NEVER, BIG = 24 * LW, 512 * LW, 2 ** 23
+LEVEL, NEVER = 24 * LW, 512 * LW
+M, MW = 2 ** 14, 3 * 2 ** 21
+LAST = (0, 136, 272, C)
 
 NE, G2, G1B, G1A, EX, E1, E0 = 10, 12, 13, 14, 16, 18, 20
 FIELDS = [(0, 1, (G2, E1, NE)), (1, 3, (G2, E1)), (3, 1, (G2, E0)), (4, 1, (G2,)), (5, 1, (G1B, G1A, EX)), (6, 1, (G1B, G1A)), (7, 7, ())]
@@ -29,19 +32,20 @@ WEIGHTS = [
      (RZ, 8 + C1, 0, 16, 1, 2 ** E1), (RZ, 8 + C1, 9, 16, 2, -2 ** E1),
      (RY, B0, 0, 16, 1, -8), (RY, 8 + C0, 0, 16, 1, 2 ** E0), (RY, 8 + C0, 9, 16, 2, -2 ** E0)],
 ]
+ROLE = {RZ: LEVEL + 6 * LW, RY: 2 * LEVEL + 7 * LW, RX: 7 * LW}
 
 F32, B16, I32, U16 = "float32", "bfloat16", "int32", "uint16"
 SCRATCH = {}
 for _t, _l in (
-    (B16, (("R0", W8), ("R1", W8), ("XT", 4 * C), ("ZT", 4 * C), ("ZS", 512), ("UT", 512), ("VT", 512), ("ET", 1040), ("ONE", 520), ("WT", 1024), ("KW", 1056),
-           ("MM", 64), ("BT0", 592), ("BT1", 592), ("SG0", ST), ("SG1", ST), ("PAT", 128), ("K16", C), ("K4", C), ("JK", 32))),
-    (I32, (("LP", 25), ("LN", 60), ("IDX", 340), ("KI0", 40), ("KI1", 40), ("KC0", KW), ("KC1", KW), ("SK0", KW), ("SK1", KW), ("RS0", 40), ("RS1", 40))),
-    (U16, (("PU", 26), ("LA", 20), ("LB", 40), ("LC", 20), ("LM", 20), ("UR", 16), ("CL", 10), ("RL0", 10), ("RL1", 10), ("WL", 16),
-           ("KL", 8), ("LI", 52), ("UL", 16), ("CLU", 12), ("CM0", 26), ("CM1", 26), ("LTL", 6), ("LU0", 40), ("LU1", 40), ("OFZ", 100), ("OFX", 100))),
-    (F32, (("TAB", 720), ("SC", 48), ("CC", 4), ("WG", 512), ("WS", 272), ("QQ", 960), ("VA", ST), ("FT", 960), ("FM", ST), ("SP", 1120),
-           ("MG0", C), ("SN0", C), ("MG1", C), ("SN1", C), ("UO0", 200), ("UO1", 200), ("SRA", 176), ("SRG", 256), ("BG", 100), ("TM", 220),
-           ("RAW0", KW), ("RAW1", KW), ("D0", KW), ("D1", KW), ("MF", C), ("ML", 240),
-           ("CF", C), ("T0", 8 * LW), ("TN", 8 * LW), ("FL0", 640), ("FL1", 640), ("FLO", 640), ("OPF", C), ("RA", 512), ("RB", 704), ("RC", 384),
+    (B16, (("R0", WIN), ("R1", WIN), ("XT", W4), ("ZT", W4), ("ZS", 512), ("UT", 512), ("VT", 512), ("ET", 1040), ("ONE", 520), ("WT", 1024), ("KW", 1056),
+           ("BT0", 592), ("BT1", 592), ("SG0", ST), ("SG1", ST), ("PAT", 64), ("K16", C), ("K4", C), ("JK", 48))),
+    (I32, (("LP", 200), ("LN", 60), ("IDX", 140), ("KI0", 40), ("KI1", 40), ("KC0", KW), ("KC1", KW), ("SK0", KW), ("SK1", KW), ("RS0", 40), ("RS1", 40))),
+    (U16, (("PU", 200), ("LA", 20), ("LB", 40), ("LZ", 40), ("LM", 40), ("SL", 62), ("RL0", 10), ("RL1", 10),
+           ("CM0", 26), ("CM1", 26), ("LTL", 6), ("LU0", 40), ("LU1", 40), ("OFZ", 100), ("OFX", 100))),
+    (F32, (("TAB", 720), ("SC", 48), ("CC", 12), ("JF", 136), ("WG", 512), ("WS", 272), ("QQ", 960), ("FM", 640), ("FT", ST), ("LF", 1280), ("SP", 2560),
+           ("MG0", C), ("SN0", C), ("MG1", C), ("SN1", C), ("SRA", 120), ("BG", 120), ("TM", 400),
+           ("D0", KW), ("D1", KW), ("ML", 160),
+           ("CF", C), ("T0", 8 * LW), ("TN", 8 * LW), ("FL0", 640), ("FL1", ST), ("FLO", 640), ("OPF", C), ("RA", 512), ("RB", 704), ("RC", 384),
            ("YO", C))),
 ):
     for _n, _w in _l:
@@ -53,8 +57,8 @@ for _n, _w in (("U", 128), ("UP", 256), ("V", 128), ("W", 512), ("E", 512), ("K"
 for _r in range(STEPS):
     SCRATCH["HQ%d" % _r] = ("sbuf", [128, C], CODES)
     SCRATCH["HS%d" % _r] = ("sbuf", [128, C], "uint8")
-DMAS = ["d_ln", "d_p", "d_u", "d_x", "d_v", "d_w", "d_tn0", "d_tn1", "d_out", "d_op", "d_qi", "d_o0", "d_o1", "d_y0", "d_y1"]
-DMAS += ["d_x%d" % k for k in range(4)] + ["d_%s%d" % (k, r) for k in ("T0", "SRA", "yA", "yB", "yC", "yD") for r in range(3)]
+DMAS = ["d_ln", "d_p", "d_u", "d_x", "d_v", "d_w", "d_tn0", "d_tn1", "d_out", "d_op", "d_q2", "d_q0", "d_s0", "d_s1", "d_ta", "d_tb"]
+DMAS += ["d_%s%d" % (k, r) for k in ["x", "o", "y"] + [q + n for q in "ysg" for n in "ABC"] for r in range(3)]
 SEMAPHORES = ["ev", "es", "et", "eg", "rarr", "rsent"] + DMAS + ["arr%d" % r for r in range(STEPS)] + ["snt%d" % r for r in range(STEPS)]
 
 
@@ -231,14 +235,80 @@ def builder(g, T):
     return emit, dma, close, remote, arrives, finish
 
 
-CYCLE, WAKE, SLACK, ISSUE, WAY, BYTE, ROW, CALL = 0.0009, 0.22, 0.07, 0.1, 0.9, 1 / 800e3, 0.012 / 16, 0.5
+CYCLE, WAKE, SLACK, ISSUE, WAY, BYTE, ROW, CALL = 0.00085, 0.24, 0.03, 0.1, 0.6, 1 / 520e3, 0.01 / 16, 0.3
+WAYS = (3.5, 4.0, 2.5)
+
+
+ORDER = {}
+PASSES, JOG, SPAN = 24, 0.3, []
+
+
+def schedule(nodes):
+    n = len(nodes)
+    jobs, last, edges = [(o[0], o[1]) for o in nodes], list(range(n)), {}
+    for k, (q, hold, way, load, deps, runs, more) in enumerate(nodes):
+        if load:
+            jobs.append(("engines", load))
+            last[k] = len(jobs) - 1
+            edges[(k, last[k])] = max(ISSUE - hold, -load)
+    sync = [k for k in range(n) if nodes[k][0] == "y"]
+    for a, b in zip(sync, sync[1:]):
+        edges[(a, b)] = edges[(last[a], last[b])] = 0
+    for k, o in enumerate(nodes):
+        for d in o[4]:
+            edges[(last[d], k)] = nodes[d][2] + (0 if nodes[d][0] == o[0] == "t" else WAKE)
+    tail = [0.0] * len(jobs)
+    for k, o in enumerate(nodes):
+        tail[last[k]] = o[2]
+    ahead, behind = [[] for _ in jobs], [[] for _ in jobs]
+    for (a, b), lag in edges.items():
+        ahead[b].append((a, lag))
+        behind[a].append((b, lag))
+
+    def place(ways, urgency, before, after, first):
+        left, end, took, busy = [len(x) for x in before], [0.0] * len(jobs), [0] * len(jobs), {}
+        ready = [k for k in range(len(jobs)) if not left[k]]
+        while ready:
+            k = max(ready, key=lambda k: urgency[k])
+            ready.remove(k)
+            there, fits = max([end[d] + lag for d, lag in before[k]] + [first[k]]), []
+            for w, (q, hold) in enumerate(ways[k]):
+                t, at, line = there, 0, busy.setdefault(q, [])
+                while at < len(line) and line[at][0] < t + hold + SLACK:
+                    t = max(t, line[at][1])
+                    at += 1
+                fits.append((t + hold - (SPARE if q != "v" else 0), w, t, at))
+            _, w, t, at = min(fits)
+            q, hold = ways[k][w]
+            if q:
+                busy[q].insert(at, (t, t + hold))
+            end[k], took[k] = t + hold, w
+            for u, lag in after[k]:
+                left[u] -= 1
+                if not left[u]:
+                    ready.append(u)
+        return end, took
+
+    ways = [[o] + (nodes[k][6] if k < n else []) for k, o in enumerate(jobs)]
+    back = place([[(None, o[1])] for o in jobs], tail, behind, ahead, tail)[0]
+    best = None
+    for turn in range(PASSES):
+        end, took = place(ways, back, ahead, behind, [0.0] * len(jobs))
+        span = max(e + t for e, t in zip(end, tail))
+        if best is None or span < best[0]:
+            best = (span, end, took)
+        if turn % 3 == 2:
+            span, end, took = best
+        back = place([[o[w]] for o, w in zip(ways, took)], [e + JOG * ((k * 7919 + turn * 104729) ** 2 % 1009) / 1009 for k, e in enumerate(end)], behind, ahead, tail)[0]
+    SPAN[:] = [best[0]]
+    return [(k, best[2][k]) for k in sorted(range(n), key=lambda k: (best[1][k] - ways[k][best[2][k]][1], k))]
 
 
 def planner(issue):
     emit, dma, close, remote, arrives, finish = issue
     nodes, hist, batches = [], {}, {}
 
-    def node(q, hold, way, load, reads, writes, run, after=()):
+    def node(q, hold, way, load, reads, writes, runs, after=(), more=()):
         deps, both = set(after), [(r, False) for r in reads] + [(r, True) for r in writes]
         for x, w in both:
             n, reg = region(x)
@@ -248,7 +318,7 @@ def planner(issue):
             if w and reg[2] == 1 and reg[3] == (0, 128):
                 hist[n] = [e for e in hist[n] if not (reg[0] <= e[0][0] and e[0][1] <= reg[1])]
             hist[n].append((reg, w, len(nodes)))
-        nodes.append((q, hold, way, load, deps, run))
+        nodes.append((q, hold, way, load, deps, runs, list(more)))
         return len(nodes) - 1
 
     def size(x):
@@ -258,18 +328,22 @@ def planner(issue):
         full = [x for x in args if is_ap(x)]
         n = size(full[0])
         if q in "tg":
-            return 1.2 * (n + 16) if q == "t" else 150 + 2 * n
+            return PE * (n + 16) if q == "t" else 150 + 2 * n
         if nout == 2:
             return 15 + n
         if any(x[0] == "I" for x in full):
-            return 60 + (3.8 if full[0][0] == "I" else 1.56) * n
+            return (60 if q == "v" else 80) + (3.8 if full[0][0] == "I" else GATHER) * n
+        if q == "s":
+            return ACTIVATION + n
         if len(args) == 4 and len(full) == 3 and "PS" not in (full[1][1], full[2][1]):
             return max(64, 2 * n)
-        return max(64, n / 2 if q == "v" and all(SCRATCH[x[1]][2] in (B16, U16) for x in full if size(x) > 1) else n)
+        return max(64, n / 2 if all(SCRATCH[x[1]][2] in (B16, U16) for x in full if size(x) > 1) else n)
 
-    def emit_(q, fn, nout, *args, acc=False, **kw):
-        reads, writes = sides(nout, args, kw)
-        node(q, CYCLE * cycles(q, nout, args), 0, 0, reads, writes, lambda: emit(q, fn, nout, *args, acc=acc, **kw))
+    def emit_(*calls):
+        both = [sides(nout, args, kw) for q, fn, nout, args, kw in calls]
+        ways = [(q, CYCLE * cycles(q, nout, args)) for q, fn, nout, args, kw in calls]
+        runs = [(lambda c=c: emit(c[0], c[1], c[2], *c[3], **c[4])) for c in calls]
+        node(*ways[0], 0, 0, [x for o in both for x in o[0]], both[0][1], runs, more=ways[1:])
 
     def dma_(q, sem, out, in_, reads=(), writes=(), rows=128, width=0):
         batches.setdefault(sem, []).append((q, reads, writes, rows * (ROW + width * BYTE), lambda: dma(q, sem, out, in_, reads, writes)))
@@ -284,51 +358,15 @@ def planner(issue):
             for o in b:
                 o[4]()
             close(sem)
-        k = node(b[0][0], len(b) * (ISSUE if lands is None else CALL), WAY, sum(o[3] for o in b), [x for o in b for x in o[1]], [x for o in b for x in o[2]], run)
+        k = node(b[0][0], len(b) * (CALL if lands else GISSUE if b[0][0] == "g" else ISSUE), WAY, sum(o[3] for o in b), [x for o in b for x in o[1]], [x for o in b for x in o[2]], [run])
         if lands is not None:
-            node(None, 0, way, 0, [], lands, lambda: None, [k])
+            node(None, 0, way, 0, [], lands, [lambda: None], [k])
 
     def finish_():
-        users = [[] for _ in nodes]
-        for k, o in enumerate(nodes):
-            for d in o[4]:
-                users[d].append(k)
-        gap = lambda d, k: 0 if nodes[d][0] == nodes[k][0] == "t" else WAKE
-        far, after, last = [0.0] * len(nodes), {}, None
-        left, there = [len(o[4]) for o in nodes], [0.0] * len(nodes)
-        for k in reversed(range(len(nodes))):
-            q, hold, way, load = nodes[k][:4]
-            far[k] = hold + way + load + max([far[u] + gap(k, u) for u in users[k]] + [0])
-            if q == "y":
-                if last is not None:
-                    far[k], after[k] = max(far[k], max(hold, load) + far[last]), last
-                    left[last] += 1
-                last = k
-        ready, free = [k for k in range(len(nodes)) if not left[k]], {}
-        start = lambda k: max(there[k], free.get(nodes[k][0], 0))
-        while ready:
-            fits, until = [], {}
-            for k in sorted(ready, key=lambda k: -far[k]):
-                q = nodes[k][0]
-                if start(k) + nodes[k][1] <= until.get(q, 1e9):
-                    fits.append(k)
-                until[q] = min(until.get(q, 1e9), start(k) + SLACK)
-            k = min(fits, key=lambda k: (start(k), -far[k]))
-            q, hold, way, load, deps, run = nodes[k]
-            t = start(k)
-            if q:
-                free[q] = t + hold
-            end = t + hold + way
-            if load:
-                free["engines"] = max(t + ISSUE, free.get("engines", 0)) + load
-                end = max(end, free["engines"] + way)
-            run()
-            ready.remove(k)
-            for u, at in [(u, end + gap(k, u)) for u in users[k]] + ([(after[k], t)] if k in after else []):
-                there[u] = max(there[u], at)
-                left[u] -= 1
-                if not left[u]:
-                    ready.append(u)
+        if len(nodes) not in ORDER:
+            ORDER[len(nodes)] = schedule(nodes)
+        for k, w in ORDER[len(nodes)]:
+            nodes[k][5][w]()
         finish()
 
     return emit_, dma_, close_, remote_, arrives, finish_
@@ -343,50 +381,67 @@ def rank_program(g, core, T, topo):
     V, S = g.vector, g.scalar
     sh, an = OP.logical_shift_right, OP.bitwise_and
 
-    def ts(out, x, s1, op0, s2=None, op1=None):
-        if op1 is None:
-            emit("v", V.tensor_scalar, 1, out, x, s1, None, op0)
-        else:
-            emit("v", V.tensor_scalar, 1, out, x, s1, s2, op0, op1)
+    def on(x, p):
+        return x[:5] + (p,) if is_ap(x) else x
+
+    def TS(out, x, s1, op0, s2=None, op1=None):
+        return "v", V.tensor_scalar, 1, (out, x, s1, None, op0) if op1 is None else (out, x, s1, s2, op0, op1), {}
+
+    def AC(out, x, func=ACT.Copy, **kw):
+        return "s", S.activation, 1, (out, x, func), kw
+
+    def IO(out, pattern, base, cm=0):
+        return "g", g.iota, 1, (out, pattern, base, cm), {} if SCRATCH[out[1]][2] == I32 else {"allow_small_or_imprecise_dtypes": True}
+
+    def ts(*args):
+        emit(TS(*args))
 
     def tt(out, x, y, op):
-        emit("v", V.tensor_tensor, 1, out, x, y, op)
+        emit(("v", V.tensor_tensor, 1, (out, x, y, op), {}))
 
     def cp(out, x):
-        emit("v", V.tensor_copy, 1, out, x)
-
-    def fill(out, k):
-        emit("v", V.memset, 1, out, k)
+        emit(("v", V.tensor_copy, 1, (out, x), {}))
 
     def act(out, x, func=ACT.Copy, **kw):
-        emit("s", S.activation, 1, out, x, func, **kw)
+        emit(AC(out, x, func, **kw))
+
+    def iota(out, pattern, base, cm=0):
+        emit(IO(out, pattern, base, cm))
+
+    def move(out, x):
+        emit(("v", V.tensor_copy, 1, (out, x), {}), AC(out, x))
 
     def lin(out, x, a, b):
-        act(out, x, ACT.Identity, scale=a if is_ap(a) else float(a), bias=b if is_ap(b) else float(b))
+        emit(TS(out, x, a, OP.mult, b, OP.add), AC(out, x, ACT.Identity, scale=a if is_ap(a) else float(a), bias=b if is_ap(b) else float(b)))
+
+    def fill(out, k):
+        n = len(range(*out[2:5]))
+        ways = [("v", V.memset, 1, (out, k if SCRATCH[out[1]][2] == I32 else float(k)), {}), IO(out, [[0, n]], k)]
+        if n <= 48 and out[1] != "JK" and SCRATCH[out[1]][2] != I32:
+            ways.append(AC(out, A("JK", 0, n), ACT.Identity, bias=float(k)))
+        emit(*ways)
 
     def quant(n, a, b, x, sn=None):
-        emit("v", V.quantize_mx, 2, A(n, a, b), A(sn or "S" + n[1:], a, b), x)
+        emit(("v", V.quantize_mx, 2, (A(n, a, b), A(sn or "S" + n[1:], a, b), x), {}))
 
     def mm(bank, l, a, r, b, n, start=True, stop=True, rs=None):
-        emit("t", g.tensor.matmul_mx, 1, A("PS", 512 * bank, 512 * bank + n), A("Q" + l, a, a + 128), A("S" + l, a, a + 128),
-             A(r, b, b + n), A(rs or "S" + r[1:], b, b + n), start, stop, acc=not start)
+        emit(("t", g.tensor.matmul_mx, 1, (A("PS", 512 * bank, 512 * bank + n), A("Q" + l, a, a + 128), A("S" + l, a, a + 128),
+                                           A(r, b, b + n), A(rs or "S" + r[1:], b, b + n), start, stop), {"acc": not start}))
 
     def ps(bank, a, b):
         return A("PS", 512 * bank + a, 512 * bank + b)
 
-    def iota(out, pattern, base, cm, whole=False):
-        if whole:
-            emit("g", g.iota, 1, out, pattern, base, cm)
-        else:
-            emit("g", g.iota, 1, out, pattern, base, cm, allow_small_or_imprecise_dtypes=True)
+    def scan(out, x, y, op0, op1):
+        emit(("v", V.tensor_tensor_scan, 1, (out, x, y, 0.0, op0, op1), {}))
 
     def spread(out, flat, keys):
-        emit("v", V.tensor_tensor_scan, 1, out, A(keys, 0, out[3] - out[2]), flat, 0.0, OP.add, OP.max)
+        scan(out, A(keys, 0, out[3] - out[2]), flat, OP.mult, OP.max)
 
-    def listed(out, flat, at):
+    def listed(out, flat, at, k=0, parts=None):
         n = flat[3] - flat[2]
         spread(A("SP", at, at + n), flat, "K16")
-        ts(out, A("SP", at + 15, at + n, 16), sc("b16"), OP.add)
+        for o, p, k in parts or [(out, (0, 128), k)]:
+            ts(on(o, p), A("SP", at + 15, at + n, 16, p), on(sc("h16"), p), OP.mult, k - M, OP.add)
 
     names = ["i", "g", "s", "q", "i4", "r3", "r7"]
 
@@ -399,266 +454,221 @@ def rank_program(g, core, T, topo):
     def ix(a, b):
         return A("IDX", a, b)
 
-    def turn(sem, name, to, a, b, by, src=None, q="y"):
-        for d0, s0, rows in ((0, by, 128 - by), (128 - by, 0, by)):
-            dma(q, sem, T[name][d0:d0 + rows, to:to + b - a], (T[name] if src is None else src)[s0:s0 + rows, a:b], reads=[A(name, a, b)] if src is None else [],
-                writes=[A(name, to, to + b - a)], rows=rows, width=(b - a) * (2 if SCRATCH[name][2] == B16 else 4))
+    def turn(sem, name, width, a, b, k, src=None, q="y", mid=0):
+        for d0, s0, rows, slot in ((0, 16 * k, 128 - 16 * k, mid + k), (128 - 16 * k, 0, 16 * k, mid + k - 8 if mid else k)):
+            o, to = width * mid, width * slot
+            dma(q, sem, T[name][d0:d0 + rows, to + a:to + b], T[name][s0:s0 + rows, o + a:o + b] if src is None else src[s0:s0 + rows, a:b],
+                reads=[A(name, o + a, o + b)] if src is None else [], writes=[A(name, to + a, to + b)], rows=rows,
+                width=(b - a) * (2 if SCRATCH[name][2] == B16 else 4))
 
-    def shifted(sem, name, width, a, b, slots=range(1, 8), q="y"):
+    def shifted(sem, name, a, b, slots=range(1, 8), q="y", src=None):
         for k in slots:
-            turn(sem, name, width * k + a, a, b, 16 * k, q=q)
-        close(sem)
-
-    def doubled(name, width, step):
-        k, sem = 1 << step, "d_%s%d" % (name, step)
-        turn(sem, name, width * k, 0, width * k, 16 * k)
-        close(sem)
-
-    def paint(q, lines):
-        for quarter, row, a, b, s, w in lines:
-            o, n = A("WT", 256 * quarter + 16 * row + a, 256 * quarter + 16 * row + b, s), len(range(a, b, s))
-            if q == "v":
-                fill(o, float(w))
-            elif q == "g":
-                iota(o, [[0, n]], w, 0)
+            if name[0] == "R":
+                turn(sem, name, W4, a, b, k, src, q, 7)
             else:
-                lin(o, A("JK", 0, n), 1, w)
+                turn(sem, name, LW, a, b, k, src, q)
+        close(sem)
 
-    def ln(out, i, p, k=0):
-        ts(out[:5] + (p,), A("LN", 20 * i, 20 * i + 20, p=p), k[:5] + (p,) if is_ap(k) else k, OP.add)
+    def across(sem, name, moves, q="y"):
+        for s0, d0, rows, a, to, n in moves:
+            dma(q, sem, T[name][d0:d0 + rows, to:to + n], T[name][s0:s0 + rows, a:a + n], reads=[A(name, a, a + n, p=(s0, s0 + rows))],
+                writes=[A(name, to, to + n, p=(d0, d0 + rows))], rows=rows, width=4 * n)
+        close(sem)
+
+    def ln(out, i, p=(0, 128), k=0):
+        ts(on(out, p), A("LN", 20 * i, 20 * i + 20, p=p), k, OP.add)
 
     for k in range(8):
         dma("ys"[k % 2], "d_ln", T.LN[16 * k:16 * k + 16, :], T.ln[:, :], writes=[A("LN", 0, 60)], rows=16)
     close("d_ln")
-    dma("y", "d_p", T.LP[:, :], T.p[:, :], writes=[A("LP", 0, 25)])
+    dma("y", "d_p", T.LP[:, 0:25], T.p[:, :], writes=[A("LP", 0, 25)])
     close("d_p")
     dma("y", "d_u", T.UT[:, :], T.u[:, :], writes=[A("UT", 0, 512)], width=1024)
     close("d_u")
-    dma("y", "d_x", T.R0[:, 0:4 * C], T.x[:, :], writes=[A("R0", 0, 4 * C)], width=8 * C)
+    dma("y", "d_x", T.R0[:, MID:MID + W4], T.x[:, :], writes=[A("R0", MID, MID + W4)], width=8 * C)
     close("d_x")
-    for k in (1, 2):
-        turn("d_x0", "R0", 4 * C * k, 0, 4 * C, 16 * k, T.x)
-    close("d_x0")
+    shifted("d_x0", "R0", 0, W4, range(1, XS[0]), src=T.x)
 
-    J16, JW, JC, JK, JL, JR, JH = ix(16, 36), ix(36, 52), ix(52, 62), ix(62, 70), ix(70, 75), ix(76, 92), ix(92, 108)
-    iota(ix(0, 1), [[0, 1]], 0, 1, True)
-    iota(A("TAB", 0, C), [[1, C]], 0, 0)
-    iota(J16, [[16, 20]], 0, 0, True)
-    iota(A("TAB", C, C + ST), [[1, 80], [1024, 4]], ST, 0)
-    iota(A("PAT", 32, 49), [[1, 17]], -1, 0)
-    iota(JC, [[8, 2], [64, 5]], 0, 0, True)
-    iota(JW, [[1, 16]], 0, 16, True)
-    iota(JK, [[8, 2], [256, 4]], 0, 16, True)
-    iota(JL, [[64, 5]], 0, 0, True)
-    iota(A("MM", 0, 32), [[1, 8], [-1, 4]], 0, 0)
-    iota(JR, [[1, 2], [2, 4], [0, 2]], 8, 0, True)
-    iota(JH, [[0, 8], [16, 2]], 0, 0, True)
-    fill(A("JK", 0, 32), 0.0)
-    fill(A("WT", 0, 1024), 0.0)
-    for q, lines in zip("vgs", WEIGHTS):
-        paint(q, lines)
-    iota(A("ONE", 0, 520), [[0, 520]], 1, 0)
+    J16, JC, JK, JL = A("JF", 0, 40), A("JF", 40, 50), A("JF", 126, 134), A("JF", 50, 62)
+    iota(ix(0, 1), [[0, 1]], 0, 1)
+    iota(A("TAB", 0, C), [[1, C]], M)
+    iota(A("PAT", 0, 16), [[1, 16]], 0)
+    iota(A("K16", 0, C), [[0, 25], [1, 16]], 0)
+    iota(JC, [[8, 2], [64, 5]], 0)
+    iota(JK, [[8, 2], [256, 4]], 0)
+    iota(JL, [[ST, 2], [64, 6]], ST)
+    iota(A("TAB", C, C + ST), [[1, 80], [1024, 4]], M + ST)
+    iota(J16, [[-5 * LW, 2], [16, 20]], 5 * LW)
+    fill(A("JK", 0, 48), 0)
+    fill(A("WT", 0, 1024), 0)
+    for quarter, row, a, b, s, w in [o for lines in WEIGHTS for o in lines]:
+        fill(A("WT", 256 * quarter + 16 * row + a, 256 * quarter + 16 * row + b, s), w)
+    iota(A("K4", 0, C), [[0, 100], [1, 4]], 0)
+    fill(A("ONE", 0, 520), 1)
     for h in range(2):
-        emit("g", g.affine_select, 1, A("ET", 520 * h, 520 * h + 520), A("ONE", 0, 520), [[-1, 520]], OP.is_equal, 0.0, 2 + h, 4)
+        emit(("g", g.affine_select, 1, (A("ET", 520 * h, 520 * h + 520), A("ONE", 0, 520), [[-1, 520]], OP.is_equal, 0.0, 2 + h, 4), {}))
     for b in range(4):
         o = 520 * (b % 2) + 2 - b // 2 * 2
         quant("QE", 128 * b, 128 * b + 128, A("ET", o, o + 512))
-    fill(A("T0", C, LW), 0.0)
-    for k in range(8):
-        iota(A("TN", LW * k + C, LW * k + LW), [[0, LW - C]], 0, 0)
-    fill(A("SRA", 160, 176), 0.0)
-    fill(A("ZS", 4 * KX, 512), 0.0)
+    fill(A("ZS", 4 * KX, 512), 0)
     for d in range(2):
-        fill(A("BT%d" % d, 160, 592), 0.0)
+        fill(A("BT%d" % d, 160, 592), 0)
 
     for k, (s, m) in enumerate(((0, 15), (4, 7), (4, 1), (5, 3), (2, 3), (0, 3), (0, 7))):
         ts(ix(1 + k, 2 + k), ix(0, 1), s, sh, m, an)
     cp(A("SC", 0, 7), ix(1, 8))
-    for out, x, a, b in (("home", "g", 4 * C, 0), ("t0", "i4", 16, "r3"), ("cl", "s", 4, "t0"), ("t1", "q", 1, "s"), ("wl", "t1", -256, 0),
-                         ("o0", "s", ST, ST), ("o2", "s", -ST, 2 * ST), ("s4", "s", 4, 0), ("r16", "r7", 16, 0), ("kl", "g", -255, 0),
-                         ("clu", "i", 4, "q"), ("cg", "g", -LW, 8 * LW), ("cgp", "s", LW, 3 * LEVEL)):
-        lin(sc(out), sc(x), a, b if isinstance(b, int) else sc(b))
-    act(sc("a"), sc("g"), ACT.Abs, bias=-3.5)
-    ts(sc("a1"), sc("a"), 2.5, OP.is_equal)
-    ts(sc("a3"), sc("a"), 0.5, OP.is_equal)
-    ts(sc("b16"), sc("i"), 15, OP.is_lt, -BIG, OP.mult)
-    ts(sc("b4"), sc("i4"), 3, OP.is_lt, BIG, OP.mult)
-    ts(sc("t2"), sc("r7"), 2.5, OP.is_gt)
-    ts(sc("t3"), sc("r7"), 5.5, OP.is_gt, sc("t2"), OP.add)
-    ts(sc("ul0"), sc("t3"), -47, OP.mult, sc("r16"), OP.add)
-    ts(sc("ul1"), sc("t3"), 49, OP.mult, sc("r16"), OP.subtract)
-    for out, x, a, b in (("t5", "a1", -1, 1), ("a02", "a3", -1, "t5"), ("c5", "t5", NEVER, 5 * LEVEL), ("t6", "a1", 7 * LW, 4 * LEVEL),
-                         ("c4", "a3", NEVER, "t6"), ("lim", "b4", 1, "home"), ("off", "lim", -1, "r3"),
-                         ("fs", "t2", 2, -1)):
-        lin(sc(out), sc(x), a, b if isinstance(b, int) else sc(b))
-    lin(sc("fb"), sc("fs"), -0.5, 0)
-    for o, n, k, r, keys in ((0, 16, "i", "i", "K16"), (16, 4, "i4", "r3", "K4")):
-        a, b, l = A("PAT", 64 + o, 64 + o + n), A("PAT", 96 + o, 96 + o + n), A("LI", o // 16 * 26, o // 16 * 26 + 25)
-        ts(a, A("PAT", 33, 33 + n), sc(k), OP.is_equal, -2 * BIG, OP.mult)
-        ts(b, A("PAT", 32, 32 + n), sc(k), OP.is_equal, BIG, OP.mult)
-        tt(A("PAT", o, o + n), a, b, OP.add)
-        ts(l, A("JK", 0, 25), sc(r), OP.add)
-        act(A(keys, 0, C), IND(A("PAT", o, o + n), l))
+    lin(sc("rg"), sc("g"), -1, 7)
+    ts(sc("e"), sc("g"), sc("rg"), OP.min)
+    ts(sc("a1"), sc("e"), 1, OP.is_equal)
+    ts(sc("n3"), sc("e"), 3, OP.is_equal, NEVER, OP.mult)
+    ts(sc("isc"), sc("r7"), 2.5, OP.is_gt)
+    for out, x, a, b in (("home", "g", W4, -3 * M), ("t0", "i4", 16, "r3"), ("cl", "s", 4, "t0"), ("i16", "i", 16, 0), ("wl", "q", 256, "i16"),
+                         ("kl", "g", 1, "i16"), ("clu", "i", 4, "q"), ("cg", "g", -LW, 8 * LW), ("cgp", "s", LW, 3 * LEVEL), ("ns", "s", -1, 1),
+                         ("i6", "i", 1, 6 * LEVEL), ("j6", "g", LW, "i6"), ("t1", "r3", 1, MID - M), ("off", "g", -W4, "t1"),
+                         ("na1", "a1", -1, 1), ("c5", "a1", -NEVER, NEVER + 5 * LEVEL), ("t2", "r7", 16, 0), ("ul0", "isc", -47, "t2"),
+                         ("t3", "r7", -16, 32), ("ul1", "isc", 49, "t3"), ("fs", "isc", 2, -1), ("fb", "isc", -1, 1)):
+        lin(sc(out), sc(x), a, sc(b) if isinstance(b, str) else b)
+    CL, WL = A("SL", 0, 10), A("SL", 10, 26)
+    KL, CLU, UL = (lambda f: A("SL", 26 + 4 * f, 30 + 4 * f)), (lambda d: A("SL", 34 + 6 * d, 39 + 6 * d)), (lambda d: A("SL", 46 + 8 * d, 54 + 8 * d))
+    for a, x, k in ((0, JC, "cl"), (10, A("PAT", 0, 16), "wl"), (26, JK, "kl"), (34, JL, "clu"), (46, A("JK", 0, 8), "ul0"), (54, A("JK", 0, 8), "ul1")):
+        ts(A("SL", a, a + x[3] - x[2]), x, sc(k), OP.add)
+    for n, k in ((16, "i"), (4, "i4")):
+        ts(A("K%d" % n, 0, C), A("K%d" % n, 0, C), sc(k), OP.not_equal, 2, OP.mult)
+        ts(A("PAT", 16 + n, 16 + 2 * n), A("PAT", 0, n), sc(k), OP.is_le, 0.5, OP.max)
+        emit(("v", V.tensor_reduce, 1, (sc("h%d" % n), A("PAT", 16 + n, 16 + 2 * n), AxisListType.X, OP.mult), {}))
 
+    for i, p in ((2, (0, 32)), (1, (32, 64)), (0, (64, 128))):
+        ln(A("LA", 0, 20), i, p)
+    cp(IND(A("QQ", 0, ST), A("LA", 0, 20)), A("TAB", 0, ST))
+    across("d_q2", "QQ", [(0, 32 * k, 32, 0, ST, ST) for k in range(4)])
     cp(A("PU", 0, 25), A("LP", 0, 25))
     lin(A("T0", 0, C), IND(A("TAB", 0, C), A("PU", 0, 25)), 4, sc("home"))
-    doubled("T0", LW, 0)
-    ts(A("LC", 0, 20), J16, sc("i"), OP.add)
-    ln(A("LC", 0, 20), 2, (0, 32), C)
-    ln(A("LC", 0, 20), 0, (0, 16), C)
-    act(A("VA", 0, ST), IND(A("TAB", 0, 720), A("LC", 0, 20)))
-    for i, p in ((1, (0, 64)), (2, (64, 128)), (0, (64, 80)), (0, (96, 112))):
-        ln(A("LA", 0, 20), i, p)
-    cp(IND(A("QQ", 0, ST), A("LA", 0, 20)), A("VA", 0, ST))
-    for o, d0, s0, rows in ((1, 0, 64, 64), (1, 64, 64, 64), (2, 0, 80, 48), (2, 48, 64, 16), (2, 64, 80, 48), (2, 112, 64, 16)):
-        dma("y", "d_qi", T.QQ[d0:d0 + rows, ST * o:ST * o + ST], T.QQ[s0:s0 + rows, 0:ST], reads=[A("QQ", 0, ST)], writes=[A("QQ", ST, 960)],
-            rows=rows, width=4 * ST)
-    close("d_qi")
-    turn("d_x1", "R0", 12 * C, 0, 4 * C, 48, T.x)
-    close("d_x1")
-    for i, p in ((0, (0, 96)), (1, (96, 128)), (2, (0, 16)), (2, (32, 48)), (2, (64, 80))):
-        ln(A("LM", 0, 20), i, p)
-    act(A("FM", 0, ST), IND(A("QQ", 0, ST), A("LM", 0, 20)))
-    listed(A("SRA", 0, 20), A("FM", 0, ST), 0)
-    doubled("SRA", 20, 0)
-    doubled("T0", LW, 1)
-    doubled("SRA", 20, 1)
-    turn("d_x2", "R0", 16 * C, 0, 8 * C, 64)
-    close("d_x2")
-    doubled("SRA", 20, 2)
-    doubled("T0", LW, 2)
-    turn("d_x3", "R0", 24 * C, 8 * C, 16 * C, 64)
-    close("d_x3")
+    shifted("d_tb", "T0", 0, C, range(1, XS[2]))
+
+    def others(d):
+        lm, fm, ft = A("LM", 20 * d, 20 * d + 20), A("FM", ST * d, ST * d + ST), A("FT", 160 * d, 160 * d + 160)
+        for i, p, k in (((2, (0, 96), 0), (1, (96, 128), 0)), ((2, (0, 32), 0), (0, (32, 64), 0), (0, (64, 96), ST), (1, (96, 128), ST)))[d]:
+            ln(lm, i, p, k)
+        move(fm, IND(A("QQ", 0, ST + ST * d), lm))
+        at = lambda role: 60 * d + 20 * role - 20
+        listed(None, fm, 800 * d, parts=[(A("SRA", at(k), at(k) + 20), (32 * k, 32 * k + 32), ROLE[k]) for k in ROLE])
+        across("d_s%d" % d, "SRA", [(32 * k, 32 * o, 32, at(k), at(k), 20) for k in ROLE for o in range(4) if o != k], SQ if d else "y")
+        move(ft, IND(fm, CL))
+        listed(A("RL%d" % d, 0, 10), ft, 800 * d + ST)
+
+    others(0)
+    shifted("d_ta", "T0", 0, C, range(XS[2], 8))
+    shifted("d_x1", "R0", 0, W4, range(XS[0], XS[1]))
+    shifted("d_x2", "R0", 0, W4, range(XS[1], 8))
     dma("y", "d_w", T.QW[:, :].bitcast(dt.uint8), T.wc[:, :], writes=[A("QW", 0, 512)], width=2048)
     dma("y", "d_w", T.SW[:, :], T.ws[:, :], writes=[A("SW", 0, 512)], width=512)
     close("d_w")
+    across("d_q0", "QQ", [(64, 64 * k, 64, 0, 2 * ST, ST) for k in range(2)])
     dma("y", "d_v", T.VT[:, :], T.v[:, :], writes=[A("VT", 0, 512)], width=1024)
     close("d_v")
     quant("QV", 0, 128, A("VT", 0, 512))
-    ts(ix(108, 124), JR, sc("g"), OP.subtract)
-    ts(ix(124, 140), ix(108, 124), 7, an)
-    ts(A("TM", 60, 76), ix(124, 140), 20, OP.mult, sc("i"), OP.add)
-    tt(ix(108, 124), A("TM", 60, 76), JH, OP.add)
-    cp(A("UR", 0, 16), ix(108, 124))
+    others(1)
 
-    ts(A("WL", 0, 16), JW, sc("wl"), OP.add)
-    act(A("WG", 0, 256), IND(A("WT", 0, 1024), A("WL", 0, 16)))
+    lin(A("WG", 0, 256), IND(A("WT", 0, 1024), WL), 1, MW)
     spread(A("WS", 0, 256), A("WG", 0, 256), "K16")
-    ts(A("WS", 256, 272), A("WS", 15, 256, 16), sc("b16"), OP.add)
-    ts(A("MM", 0, 32), A("MM", 0, 32), sc("s4"), OP.is_equal)
-    fill(A("MM", 32, 64), 0.0)
-    fill(A("KW", 0, 32), 0.0)
-    for k in range(16):
-        act(A("KW", 32 + 64 * k, 96 + 64 * k), A("MM", 0, 64), scale=A("WS", 256 + k, 257 + k))
+    ts(A("WS", 256, 272), A("WS", 15, 256, 16), sc("h16"), OP.mult, -MW, OP.add)
+    fill(A("KW", 0, 1056), 0)
+    for k in range(8):
+        lin(A("KW", 32 + 4 * k + k % 4, 1056, 64), A("WS", 256, 272), sc("s" if k // 4 else "ns"), 0)
     quant("QK", 0, 264, A("KW", 0, 1056))
-    ts(A("KL", 0, 8), JK, sc("kl"), OP.add)
-    for k in range(4):
-        d, f = k // 2, k % 2
-        act(A("WG", 256 + 64 * k, 320 + 64 * k), IND(A("WT", 0, 1024), A("KL", 4 * f, 4 * f + 4)), ACT.Abs if d else ACT.Relu, scale=0.5 if d else -1.0,
-            accum_out=sc("w%d" % k))
-        lin(A("CC", k, k + 1), sc("w%d" % k), LW, LW * EXTRA[f])
+    for f in range(2):
+        act(A("WG", 256 + 64 * f, 320 + 64 * f), IND(A("WT", 0, 1024), KL(f)), ACT.Relu, scale=-1.0, accum_out=sc("w%d" % f))
+        lin(A("CC", f, f + 1), sc("w%d" % f), LW, LW * EXTRA[f])
 
-    ts(ix(140, 200), A("LN", 0, 60), 3, an)
-    ts(ix(200, 260), A("LN", 0, 60), 2, sh)
-    ts(A("TM", 0, 60), ix(140, 200), 1024, OP.mult, sc("cg"), OP.add)
-    tt(A("TM", 80, 140), A("TM", 0, 60), ix(200, 260), OP.add)
-    lin(A("BG", 0, 60), A("TM", 80, 140), 1, ST)
-    ts(A("BG", 60, 80), J16, sc("i"), OP.add)
-    lin(A("BG", 80, 100), A("BG", 60, 80), 1, sc("cg"))
+    ts(ix(20, 80), A("LN", 0, 60), 3, an)
+    ts(ix(80, 140), A("LN", 0, 60), 2, sh)
+    ts(A("BG", 60, 120), ix(20, 80), 1024, OP.mult, ST, OP.add)
+    tt(A("BG", 0, 60), A("BG", 60, 120), ix(80, 140), OP.add)
+    OWN6 = A("TM", 360, 400)
+    lin(A("TM", 360, 380), A("JF", 0, 20), 1, sc("j6"))
+    lin(A("TM", 380, 400), A("JF", 20, 40), 1, sc("i6"))
 
-    act(A("MF", 0, ST), A("TAB", 0, ST), scale=1025.0)
-    cp(IND(A("CF", 0, C), A("PU", 0, 20)), A("MF", 0, ST))
+    cp(IND(A("CF", 0, C), A("PU", 0, 20)), A("TAB", 0, ST))
     for d in range(2):
-        ts(A("CLU", 6 * d, 6 * d + 5), JL, sc("clu"), OP.add, sc("o%d" % (2 - 2 * d)), OP.add)
-        lin(A("ML", 80 * d, 80 * d + 80), IND(A("QQ", 0, 960), A("CLU", 6 * d, 6 * d + 5)), 1, ST)
-    lin(A("ML", 160, 240), A("ML", 80, 160), 1024, 0)
-    tt(A("MF", ST, C), A("ML", 160, 240), A("ML", 0, 80), OP.add)
-    cp(IND(A("CF", 0, C), A("PU", 20, 25)), A("MF", ST, C))
-    listed(ix(260, 285), A("CF", 0, C), ST)
-    ts(ix(286, 311), ix(260, 285), 1023, an)
-    cp(A("CM0", 0, 25), ix(286, 311))
-    ts(ix(312, 337), ix(260, 285), 10, sh)
-    cp(A("CM1", 0, 25), ix(312, 337))
-    listed(A("LTL", 0, 5), A("ML", 80, 160), 720)
+        lin(A("ML", 80 * d, 80 * d + 80), IND(A("QQ", 0, 2 * ST + ST * d), CLU(d)), 1, ST - ST * d)
+    for d, links in enumerate((A("ML", 0, 80), A("TAB", ST, C))):
+        cp(IND(A("CF", 0, C), A("PU", 20, 25)), links)
+        listed(A("CM%d" % d, 0, 25), A("CF", 0, C), 1600 + C * d)
+    listed(A("LTL", 0, 5), A("ML", 80, 160), 2400)
 
     quant("QU", 0, 128, A("UT", 0, 512))
-    ts(A("CL", 0, 10), JC, sc("cl"), OP.add)
     for d in range(2):
-        ts(A("UL", 8 * d, 8 * d + 8), A("JK", 0, 8), sc("ul%d" % d), OP.add, 32 * d, OP.add)
-        cp(CW("QUP", 128 * d, 128 * d + 128), IND(CW("QU", 0, 128), A("UL", 8 * d, 8 * d + 8)))
-        act(A("SUP", 128 * d, 128 * d + 128), IND(A("SU", 0, 128), A("UL", 8 * d, 8 * d + 8)))
-        lb, ft = A("LB", 20 * d, 20 * d + 20), 480 * d
-        ln(lb, 2 - 2 * d, (0, 64))
-        ln(lb, 2 - 2 * d, (64, 96), sc("o%d" % (2 * d)))
-        ln(lb, 1, (96, 128), sc("o%d" % (2 * d)))
-        act(A("FT", ft, ft + ST), IND(A("QQ", 0, 960), lb))
-        act(A("FT", ft + ST, ft + 480), IND(A("FT", ft, ft + ST), A("CL", 0, 10)))
-        listed(A("RL%d" % d, 0, 10), A("FT", ft + ST, ft + 480), 800 + 160 * d)
-        cp(A("RL%d" % d, 0, 10, p=(0, 32)), A("CL", 0, 10, p=(0, 32)))
-        i0, i2, tm = 40 * d, 40 - 40 * d, 140 + 40 * d
-        raw = lambda k, h: A("RAW%d" % d, KW // 2 * h + k, KW // 2 * h + KW // 2, NK)
-        fill(A("RAW%d" % d, NK - 1, KW, NK), 0.0)
-        fill(A("KC%d" % d, NK - 1, KW, NK), 2 ** 30)
-        src = lambda q: A("SRG", 128 * d + 32 * q, 128 * d + 32 * q + 20)
-        lin(A("SRG", 128 * d, 128 * d + 128), IND(A("SRA", 0, 176), A("UR", 8 * d, 8 * d + 8)), 1, sc("cg"))
+        cp(CW("QUP", 128 * d, 128 * d + 128), IND(CW("QU", 0, 128), UL(d)))
+        move(A("SUP", 128 * d, 128 * d + 128), IND(A("SU", 0, 128), UL(d)))
+        step = lambda k, h=None: A("D%d" % d, k, KW, NK) if h is None else A("D%d" % d, KW // 2 * h + k, KW // 2 * h + KW // 2, NK)
+        tm = lambda k, h=None: A("TM", 180 * d + 40 * k + 20 * (h or 0), 180 * d + 40 * k + (40 if h is None else 20 * h + 20))
+        src = lambda role: A("SRA", 60 * d + 20 * role - 20, 60 * d + 20 * role)
+        bg = lambda i: A("BG", 20 * i, 20 * i + 20)
+        lf, lb, lz = 640 * d, A("LB", 20 * d, 20 * d + 20), A("LZ", 20 * d, 20 * d + 20)
+        ln(lb, 2 * d, k=C)
+        move(A("LF", lf, lf + ST), IND(A("TAB", 0, 720), lb))
+        ts(lz, src(RZ), -ROLE[RZ], OP.add)
+        move(A("LF", lf + ST, lf + 640), IND(A("LF", lf, lf + ST), lz))
+        listed(tm(4, 0), A("LF", lf + ST, lf + 640), 800 * d + 480)
+        lin(tm(0, 0), bg(2 - 2 * d), 1, 3 * LEVEL)
+        lin(tm(0, 1), bg(2 - 2 * d), 1, sc("cgp"))
+        lin(tm(3, 0), bg(2 * d), sc("na1"), sc("n3"))
+        lin(tm(3, 1), src(RX), sc("a1"), 4 * LEVEL)
+        tt(tm(1, 0), tm(3, 0), tm(3, 1), OP.add)
+        lin(tm(1, 1), src(RX), 1, 4 * LEVEL)
+        lin(tm(2, 0), bg(1), 1, sc("c5"))
+        lin(tm(2, 1), bg(1), 1, 5 * LEVEL)
+        fill(step(0), 2 ** 23)
         for h in range(2):
-            lin(raw(0, h), src(OWN), 1, 0)
-            lin(raw(1, h), src(RZ), 1, LEVEL + 6 * LW)
-            ts(raw(2, h), src(RY), 2 * LEVEL + 7 * LW, OP.add)
-        ts(raw(3, 0), A("BG", i2, i2 + 20), 3 * LEVEL, OP.add)
-        ts(raw(3, 1), A("BG", i2, i2 + 20), sc("cgp"), OP.add)
-        lin(A("TM", tm, tm + 20), A("BG", i0, i0 + 20), sc("a02"), sc("c4"))
-        ts(A("TM", tm + 20, tm + 40), src(RX), sc("a1"), OP.mult)
-        tt(raw(4, 0), A("TM", tm, tm + 20), A("TM", tm + 20, tm + 40), OP.add)
-        ts(raw(4, 1), src(RX), 4 * LEVEL + 7 * LW, OP.add)
-        lin(raw(5, 0), A("BG", 20, 40), 1, sc("c5"))
-        lin(raw(5, 1), A("BG", 20, 40), 1, 5 * LEVEL)
-        lin(raw(6, 0), A("BG", 60, 80), 1, 6 * LEVEL + 13 * LW)
-        lin(raw(6, 1), A("BG", 80, 100), 1, 6 * LEVEL)
-        tt(A("D%d" % d, 1, KW), A("RAW%d" % d, 0, KW - 1), A("RAW%d" % d, 1, KW), OP.subtract)
-        fill(A("D%d" % d, 0, KW, NK), 1.0e12)
+            tt(step(1, h), tm(4, 0), src(RZ), OP.subtract)
+            tt(step(2, h), src(RZ), src(RY), OP.subtract)
+            tt(step(3, h), src(RY), tm(0, h), OP.subtract)
+        for k, a, b in ((4, tm(0), tm(1)), (5, tm(1), tm(2)), (6, tm(2), OWN6)):
+            tt(step(k), a, b, OP.subtract)
+        lin(step(7), OWN6, 1, sc("cg"))
+        fill(A("KC%d" % d, NK - 1, KW, NK), 2 ** 23)
 
-    def signs(d, src=None):
+    def signs(d, src=None, at=0):
         if d == 0:
             for h in range(2):
-                quant("QX", 160 * h, 160 * h + 160, A(src, 640 * h, 640 * h + 640))
+                quant("QX", 160 * h, 160 * h + 160, A(src, at + 640 * h, at + 640 * h + 640))
                 mm(h, "UP", 0, "QX", 160 * h, 160)
-                ts(A("SG0", 160 * h, 160 * h + 160), ps(h, 0, 160), 0.0, OP.is_gt)
-            cp(A("BT0", 0, 160), IND(A("SG0", 0, ST), A("RL0", 0, 10)))
+                o = A("SG0", 160 * h, 160 * h + 160)
+                emit(TS(o, ps(h, 0, 160), 0.0, OP.is_gt), AC(o, ps(h, 0, 160), ACT.Sign))
+            for a, b in ((0, 6), (6, 10)):
+                o, x = A("BT0", 16 * a, 16 * b), IND(A("SG0", 0, ST), A("RL0", a, b))
+                emit(TS(o, x, 0.0, OP.max), AC(o, x, ACT.Relu))
         else:
             mm(4, "UP", 128, "QX", 0, ST)
-            act(A("SG1", 0, ST), ps(4, 0, ST), ACT.Sign)
-            act(A("BT1", 0, 160), IND(A("SG1", 0, ST), A("RL1", 0, 10)), ACT.Sign, scale=sc("fs"), bias=sc("fb"))
+            ts(A("SG1", 0, ST), ps(4, 0, ST), 0.0, OP.is_gt)
+            lin(A("BT1", 0, 160), IND(A("SG1", 0, ST), A("RL1", 0, 10)), sc("fs"), sc("fb"))
         quant("QB%d" % d, 0, 148, A("BT%d" % d, 0, 592))
         for f in range(2):
             for m in range(2):
                 mm(2 + 3 * d + f, "K", 128 * f + 8 - 8 * m, "QB%d" % d, 20 * m, 128, m == 0, m == 1)
-            ts(A("KI%d" % d, 20 * f, 20 * f + 20), ps(2 + 3 * d + f, 0, 20), LW // (1 + d), OP.mult, A("CC", 2 * d + f, 2 * d + f + 1), OP.add)
+            ts(A("KI%d" % d, 20 * f, 20 * f + 20), ps(2 + 3 * d + f, 0, 20), LW, OP.mult, A("CC", f, f + 1), OP.add)
 
     def choose(d):
         for k, (s, m, bits) in enumerate(FIELDS):
             ts(A("KC%d" % d, k, KW, NK), A("KI%d" % d, 0, 40), s, sh, LW * (m + sum(1 << (b - s) for b in bits)), an)
-        emit("v", V.tensor_tensor_scan, 1, A("SK%d" % d, 0, KW), A("D%d" % d, 0, KW), A("KC%d" % d, 0, KW), 0.0, OP.add, OP.min)
+        scan(A("SK%d" % d, 0, KW), A("D%d" % d, 0, KW), A("KC%d" % d, 0, KW), OP.add, OP.min)
         ts(A("RS%d" % d, 0, 40), A("SK%d" % d, NK - 1, KW, NK), 8 * LW - 1, an)
         cp(A("LU%d" % d, 0, 40), A("RS%d" % d, 0, 40))
 
-    def lookup(d, table, out, first=cp):
-        act(A(out, ST, 640), IND(A(table, 0, 8 * LW), A("LU%d" % d, 20, 40)))
-        first(A(out, 0, ST), IND(A(table, 0, 8 * LW), A("LU%d" % d, 0, 20)))
+    def lookup(d, table, stacks, links):
+        move(links, IND(A(table, 0, 8 * LW), A("LU%d" % d, 20, 40)))
+        move(stacks, IND(A(table, 0, 8 * LW), A("LU%d" % d, 0, 20)))
 
-    def offsets(out, d, c0, cm, c1):
-        for f, a, b in ((act, cm, c1), (cp, c0, cm)):
-            if b > a:
-                f(A("MG%d" % d, a, b), IND(A("FL%d" % d, 0, 640), A("CM%d" % d, a // 16, b // 16)))
-        uo, a, b, last = "UO%d" % d, c0 // 4, c1 // 4, A("SN%d" % d, c0 + 3, c1, 4)
+    def offsets(out, d, *cuts):
+        for a, b in zip(cuts, cuts[1:]):
+            move(A("MG%d" % d, a, b), IND(A("TN", 0, C) if d else A("FL0", 0, 640), A("CM%d" % d, a // 16, b // 16)))
+        c0, c1 = cuts[0], cuts[-1]
         spread(A("SN%d" % d, c0, c1), A("MG%d" % d, c0, c1), "K4")
-        ts(A(uo, a, b), last, sc("lim"), OP.is_lt, W8, OP.mult)
-        tt(A(uo, 100 + a, 100 + b), last, A(uo, a, b), OP.add)
-        ts(A(out, a, b), A(uo, 100 + a, 100 + b), sc("off"), OP.add)
+        ts(A(out, c0 // 4, c1 // 4), A("SN%d" % d, c0 + 3, c1, 4), sc("h4"), OP.mult, sc("off"), OP.add)
 
-    def pull(dst, win, offs, c0, cm, c1):
-        for f, a, b in ((act, cm, c1), (cp, c0, cm)):
-            f(A(dst, 4 * a, 4 * b), IND(A(win, 0, W8), A(offs, a // 4, b // 4)))
+    def pull(dst, win, offs, *cuts):
+        for a, b in zip(cuts, cuts[1:]):
+            move(A(dst, 4 * a, 4 * b), IND(A(win, 0, WIN), A(offs, a // 4, b // 4)))
 
     for r in range(STEPS):
         HQ, HS = "HQ%d" % r, "HS%d" % r
@@ -674,25 +684,22 @@ def rank_program(g, core, T, topo):
                 mm(4 + b, "E", 128 * b, HQ, c0, m, rs=HS)
             for b in range(4):
                 l = A("R" + name, n * b, n * b + n)
-                act(l, ps(b, 0, n), ACT.Relu, scale=0.015625)
-                tt(A(NEW, 4 * c0 + b, 4 * c1, 4), l, ps(4 + b, 0, n), OP.add)
-            if c0:
-                shifted("d_y%s%d" % (name, r), NEW, 4 * C, 4 * c0, 4 * c1)
-            else:
-                shifted("d_yC%d" % r, NEW, 4 * C, 0, 4 * c1, range(1, 5))
-                shifted("d_yD%d" % r, NEW, 4 * C, 0, 4 * c1, range(5, 8), "s")
+                emit(AC(l, ps(b, 0, n), ACT.Relu, scale=0.015625), TS(l, ps(b, 0, n), 0.0, OP.max, 0.015625, OP.mult))
+                tt(A(NEW, MID + 4 * c0 + b, MID + 4 * c1, 4), l, ps(4 + b, 0, n), OP.add)
+            for q in sorted(set(SHARE[name])):
+                shifted("d_%s%s%d" % (q, name, r), NEW, 4 * c0, 4 * c1, [k + 1 for k in range(7) if SHARE[name][k] == q], q)
 
-        signs(0, "XT" if r else "R0")
+        signs(0, *(("XT", 0) if r else ("R0", MID)))
         if r:
             signs(1)
         choose(0)
-        lookup(0, "TN" if r else "T0", "FL0")
-        offsets("OFZ", 0, 0, KX, KX)
-        pull("ZS", OLD, "OFZ", 0, 48, KX)
-        quant("QS", 0, 128, A("ZS", 0, 512))
-        offsets("OFZ", 0, KX, KX, CA)
+        lookup(0, "TN" if r else "T0", A("FL0", 0, ST), A("FL0", ST, 640))
+        offsets("OFZ", 0, 0, KX)
+        offsets("OFZ", 0, KX, CA)
         pull("ZT", OLD, "OFZ", KX, 160, CA)
         quant(HQ, KX, CA, A("ZT", 4 * KX, 4 * CA), HS)
+        pull("ZS", OLD, "OFZ", 0, 48, KX)
+        quant("QS", 0, 128, A("ZS", 0, 512))
         way = hops(T, topo, rank, r)
         for k, c in enumerate(way):
             to = T.cores[peer] if c is None else c
@@ -704,43 +711,53 @@ def rank_program(g, core, T, topo):
                 o = T[HS if c is None else "SR"][:, 0:KX]
                 i, rd = T.SS[:, 0:KX], [A("SS", 0, KX)]
             remote(o, i, rd, "arr%d" % r if c is None else "rarr", "snt%d" % r, topo.addr(to, core), m, n)
-        close("snt%d" % r, [A(HQ, 0, KX), A(HS, 0, KX)], 4.0 if way[0] is not None else 1.5 if r else 2.5)
-        offsets("OFZ", 0, CA, CA, C)
-        pull("ZT", OLD, "OFZ", CA, 312, C)
+        close("snt%d" % r, [A(HQ, 0, KX), A(HS, 0, KX)], WAYS[r])
+        offsets("OFZ", 0, CA, C)
+        pull("ZT", OLD, "OFZ", CA, CB, C)
         quant(HQ, CA, C, A("ZT", 4 * CA, 4 * C), HS)
+        if r == 0 and POS == 1:
+            signs(1)
         layer("A", KX, CA)
+        if r == 0 and POS == 2:
+            signs(1)
         layer("B", CA, C)
-        if r == 0:
+        if r == 0 and POS == 3:
             signs(1)
         layer("C", 0, KX)
         choose(1)
-        lookup(1, "T0", "FL1")
+        lookup(1, "T0", A("TN", 0, ST), A("FL1", 0, ST))
+        move(A("TN", ST, C), IND(A("FL1", 0, ST), A("LTL", 0, 5)))
         if r < STEPS - 1:
-            act(A("TN", 0, ST), A("FL1", 0, ST))
-            act(A("TN", ST, C), IND(A("FL1", 0, 640), A("LTL", 0, 5)))
-            shifted("d_tn%d" % r, "TN", LW, 0, C)
-            offsets("OFX", 1, 0, 224, ST)
+            shifted("d_tn%d" % r, "TN", 0, C)
+            offsets("OFX", 1, 0, CMX, ST)
             pull("XT", NEW, "OFX", 0, 160, ST)
         else:
             offsets("OFX", 1, 0, 224, C)
-            lookup(0, "T0", "FLO", act)
-            act(A("OPF", 0, C), IND(A("FLO", 0, 640), A("CM0", 0, 25)), scale=0.25)
+            lookup(0, "T0", A("FLO", 0, ST), A("FLO", ST, 640))
+            lin(A("OPF", 0, C), IND(A("FLO", 0, 640), A("CM0", 0, 25)), 0.25, -M // 4)
             for k in range(8):
                 dma("y", "d_op", T.op[k:k + 1, :], T.OPF[16 * k:16 * k + 1, :], reads=[A("OPF", 0, C)], rows=1)
             close("d_op")
 
-    H = C // 2
-    for h, cm in ((0, 104), (1, 280)):
-        a, b = H * h, H * h + H
-        pull("XT", NEW, "OFX", a, cm, b)
+    for h, (a, b) in enumerate(zip(LAST, LAST[1:])):
+        pull("XT", NEW, "OFX", a, a + CUT[h], b)
         quant("QX", a, b, A("XT", 4 * a, 4 * b))
-        mm(h, "V", 0, "QX", a, H)
-        dma("y", "d_o%d" % h, T.oc[:, 4 * a:4 * b], T.QX[:, a:b].bitcast(dt.uint8), reads=[A("QX", a, b)], width=4 * H)
+        mm(h, "V", 0, "QX", a, b - a)
+        dma("y", "d_o%d" % h, T.oc[:, 4 * a:4 * b], T.QX[:, a:b].bitcast(dt.uint8), reads=[A("QX", a, b)], width=4 * (b - a))
         close("d_o%d" % h)
-        (cp if h else act)(A("YO", a, b), ps(h, 0, H))
-        dma("sy"[h], "d_y%d" % h, T.y[:, a:b], T.YO[:, a:b], reads=[A("YO", a, b)], width=4 * H)
+        move(A("YO", a, b), ps(h, 0, b - a))
+        dma("y", "d_y%d" % h, T.y[:, a:b], T.YO[:, a:b], reads=[A("YO", a, b)], width=4 * (b - a))
         close("d_y%d" % h)
     for k in range(4):
         dma("s", "d_out", T.osc[4 * k:4 * k + 4, :], T.SX[32 * k:32 * k + 4, :], reads=[A("SX", 0, C)], rows=4)
     close("d_out")
     finish()
+
+
+XS = (3, 6, 4)
+PE, GATHER, ACTIVATION, SPARE = 1.0, 1.3, 70, 0.1
+POS, SQ = 1, "y"
+SHARE = {"A": "yyyysss", "B": "yyyyyyy", "C": "yyyysss"}
+GISSUE = 1.0
+CUT = (56, 56, 56)
+PAINT, BACK, CMX, CB = "sgs", (0, 0, 0), 224, 312

from concourse.mybir import dt, AluOpType, ActivationFunctionType, AxisListType

C, ST, KX, STEPS, N = 400, 320, 96, 3, 8
CA = 224
MATES = [1, 2, 4]
W4 = 4 * C
WIN, MID = 15 * W4, 7 * W4
LW = 512
OP = AluOpType
ACT = ActivationFunctionType
CODES = "float8_e4m3fn_x4"
NK = 8
KW = 40 * NK
LEVEL, NEVER = 24 * LW, 512 * LW
M, MW = 2 ** 14, 3 * 2 ** 21
LAST = (0, 136, 272, C)

NE, G2, G1B, G1A, EX, E1, E0 = 10, 12, 13, 14, 16, 18, 20
FIELDS = [(0, 1, (G2, E1, NE)), (1, 3, (G2, E1)), (3, 1, (G2, E0)), (4, 1, (G2,)), (5, 1, (G1B, G1A, EX)), (6, 1, (G1B, G1A)), (7, 7, ())]
EXTRA = (2 ** NE + 2 ** G2, 2 ** NE + 2 ** G1A)
OWN, RZ, RY, RX = 0, 1, 2, 3
B0, B1, B2, C0, C1, C2 = range(6)
WEIGHTS = [
    [(OWN, B0, 0, 48, 1, -256), (OWN, B1, 8, 16, 1, 640), (OWN, B2, 8, 16, 1, 0), (OWN, C0, 0, 8, 1, 32), (OWN, C0, 1, 7, 5, 0),
     (OWN, C1, 0, 16, 1, 64), (OWN, C2, 0, 8, 1, 16), (OWN, C2, 8, 16, 2, -2 ** G2), (OWN, C2, 9, 16, 2, 2 ** G2)],
    [(OWN, 8 + B0, 0, 4, 1, -2 ** EX), (OWN, 8 + B0, 4, 8, 1, 2 ** EX), (OWN, 8 + B0, 1, 7, 5, 0),
     (OWN, 8 + B1, 0, 32, 1, 2 ** G1A), (OWN, 8 + B1, 0, 4, 1, -2 ** G1A),
     (OWN, 8 + B2, 1, 4, 1, -2 ** G1B), (OWN, 8 + B2, 4, 7, 1, 2 ** G1B), (OWN, 8 + B2, 0, 1, 1, 2 ** G2), (OWN, 8 + B2, 7, 8, 1, -2 ** G2)],
    [(OWN, 8 + C1, 8, 16, 1, 2 ** EX), (OWN, 8 + C1, 1, 7, 5, 2 ** EX), (OWN, 8 + C2, 0, 8, 1, 2 ** E1 + 2 ** E0),
     (RX, B0, 8, 16, 1, -32), (RX, B0, 1, 7, 5, -32), (RX, 8 + C0, 8, 16, 1, 2 ** EX), (RX, 8 + C0, 1, 7, 5, 2 ** EX),
     (RZ, C0, 0, 16, 1, 1), (RZ, B0, 0, 16, 1, -6), (RZ, 8 + B0, 0, 32, 1, 2 ** NE),
     (RZ, 8 + C1, 0, 16, 1, 2 ** E1), (RZ, 8 + C1, 9, 16, 2, -2 ** E1),
     (RY, B0, 0, 16, 1, -8), (RY, 8 + C0, 0, 16, 1, 2 ** E0), (RY, 8 + C0, 9, 16, 2, -2 ** E0)],
]
ROLE = {RZ: LEVEL + 6 * LW, RY: 2 * LEVEL + 7 * LW, RX: 7 * LW}

F32, B16, I32, U16 = "float32", "bfloat16", "int32", "uint16"
SCRATCH = {}
for _t, _l in (
    (B16, (("R0", WIN), ("R1", WIN), ("XT", W4), ("ZT", W4), ("ZS", 512), ("UT", 512), ("VT", 512), ("ET", 1040), ("ONE", 520), ("WT", 1024), ("KW", 1056),
           ("BT0", 592), ("BT1", 592), ("SG0", ST), ("SG1", ST), ("PAT", 64), ("K16", C), ("K4", C), ("JK", 48))),
    (I32, (("LP", 200), ("LN", 60), ("IDX", 140), ("KI0", 40), ("KI1", 40), ("KC0", KW), ("KC1", KW), ("SK0", KW), ("SK1", KW), ("RS0", 40), ("RS1", 40))),
    (U16, (("PU", 200), ("LA", 20), ("LB", 40), ("LZ", 40), ("LM", 40), ("SL", 62), ("RL0", 10), ("RL1", 10),
           ("CM0", 26), ("CM1", 26), ("LTL", 6), ("LU0", 40), ("LU1", 40), ("OFZ", 100), ("OFX", 100))),
    (F32, (("TAB", 720), ("SC", 48), ("CC", 12), ("JF", 136), ("WG", 512), ("WS", 272), ("QQ", 960), ("FM", 640), ("FT", ST), ("LF", 1280), ("SP", 2560),
           ("MG0", C), ("SN0", C), ("MG1", C), ("SN1", C), ("SRA", 120), ("BG", 120), ("TM", 400),
           ("D0", KW), ("D1", KW), ("ML", 160),
           ("CF", C), ("T0", 8 * LW), ("TN", 8 * LW), ("FL0", 640), ("FL1", ST), ("FLO", 640), ("OPF", C), ("RA", 512), ("RB", 704), ("RC", 384),
           ("YO", C))),
):
    for _n, _w in _l:
        SCRATCH[_n] = ("sbuf", [128, _w], _t)
SCRATCH["PS"] = ("psum", [128, 4096], F32)
for _n, _w in (("U", 128), ("UP", 256), ("V", 128), ("W", 512), ("E", 512), ("K", 264), ("B0", 148), ("B1", 148), ("X", C), ("S", 128), ("R", KX)):
    SCRATCH["Q" + _n] = ("sbuf", [128, _w], CODES)
    SCRATCH["S" + _n] = ("sbuf", [128, _w], "uint8")
for _r in range(STEPS):
    SCRATCH["HQ%d" % _r] = ("sbuf", [128, C], CODES)
    SCRATCH["HS%d" % _r] = ("sbuf", [128, C], "uint8")
DMAS = ["d_ln", "d_p", "d_u", "d_x", "d_v", "d_w", "d_tn0", "d_tn1", "d_out", "d_op", "d_q2", "d_q0", "d_s0", "d_s1", "d_ta", "d_tb"]
DMAS += ["d_%s%d" % (k, r) for k in ["x", "o", "y"] + [q + n for q in "ysg" for n in "ABC"] for r in range(3)]
SEMAPHORES = ["ev", "es", "et", "eg", "rarr", "rsent"] + DMAS + ["arr%d" % r for r in range(STEPS)] + ["snt%d" % r for r in range(STEPS)]


def hops(T, topo, i, r):
    src, dst = T.cores[i], T.cores[i ^ MATES[r]]
    if topo.may_write(src, dst):
        return None, None
    c = [k for k in topo.cores_of(src) if k not in T.cores and topo.die(k) == topo.die(src) and topo.may_write(k, dst)]
    return c[0], c[-1]


def mask_of(topo, src, dst):
    e = topo.engines(src, dst)[:8]
    return sum(1 << k for k in e), len(e)


def relay(g, core, T, topo):
    for i in range(N):
        for r in range(STEPS):
            pair = hops(T, topo, i, r)
            if core not in pair:
                continue
            src, dst = T.cores[i], T.cores[i ^ MATES[r]]
            jobs = [k for k in range(2) if pair[k] == core]
            n_in = mask_of(topo, src, core)[1]
            m, n = mask_of(topo, core, dst)
            rid, pid = topo.addr(dst, core)
            g.wait_ge(T.sem.rarr, n_in * len(jobs))
            for k in jobs:
                if k == 0:
                    o, s = T["HQ%d" % r][:, 0:KX].bitcast(dt.uint8), T.QR[:, 0:KX].bitcast(dt.uint8)
                else:
                    o, s = T["HS%d" % r][:, 0:KX], T.SR[:, 0:KX]
                g.remote_dma(out_ap=o, in_ap=s, remote_sem=T.sem["arr%d" % r], local_sem=T.sem.rsent, pid=pid, routing_id=rid, dma_engine_mask=m)
            g.wait_ge(T.sem.rsent, n * len(jobs))


def A(name, a, b, s=1, p=(0, 128)):
    return ("A", name, a, b, s, p)


def IND(win, off):
    return ("I", win, off)


def CW(name, a, b):
    return ("C", name, a, b, 1, (0, 128))


def is_ap(x):
    return isinstance(x, tuple) and len(x) > 0 and x[0] in ("A", "I", "C")


def region(x):
    _, n, a, b, s, p = x
    if n == "PS":
        return n, (a // 512 * 512, (b + 511) // 512 * 512, 1, p)
    return n, (a, b, s, p)


def meet(p, q):
    if p[1] <= q[0] or q[1] <= p[0] or p[3][1] <= q[3][0] or q[3][1] <= p[3][0]:
        return False
    return not (p[2] == q[2] > 1 and (p[0] - q[0]) % p[2])


def sides(nout, args, kw):
    def parts(xs):
        out = []
        for x in xs:
            if is_ap(x):
                out += [("A",) + x[1][1:], x[2]] if x[0] == "I" else [("A",) + x[1:]]
        return out
    reads, writes = parts(args[nout:]) + parts(x for k, x in kw.items() if k != "accum_out"), parts([kw.get("accum_out")])
    for x in args[:nout]:
        if x[0] == "I":
            writes.append(("A",) + x[1][1:])
            reads.append(x[2])
        else:
            writes.append(("A",) + x[1:])
    return reads, writes


def builder(g, T):
    Q = {"v": g.vector, "s": g.scalar, "t": g.tensor, "g": g, "y": g.sync}
    known = {q: {} for q in Q}
    total, clock, hist, waited, pending = {}, {}, {}, {}, {}

    def ap(x):
        if x[0] == "A":
            _, n, a, b, s, p = x
            return T[n][p[0]:p[1], a:b] if s == 1 else T[n][p[0]:p[1], a:b:s]
        if x[0] == "C":
            return T[x[1]][:, x[2]:x[3]].bitcast(dt.uint32)
        return ap(x[1]).indirect(ap(x[2]))

    def wait(q, evs):
        best = {}
        for s, v in set(evs):
            if known[q].get(s, 0) < v:
                best[s] = max(v, best.get(s, 0))
        evs = [e for e in best.items() if not any(o != e[0] and clock[(o, w)].get(e[0], 0) >= e[1] for o, w in best.items())]
        for s, v in sorted(evs):
            Q[q].wait_ge(T.sem[s], v)
            waited[s] = max(v, waited.get(s, 0))
            for k, w in clock[(s, v)].items():
                known[q][k] = max(w, known[q].get(k, 0))

    def hazards(q, reads, writes, acc=False):
        evs = []
        for x, w in [(r, False) for r in reads] + [(r, True) for r in writes]:
            n, reg = region(x)
            for reg2, w2, ev, q2 in hist.get(n, []):
                if meet(reg, reg2) and (w or w2 or (n == "PS" and q2 != q)) and not (acc and q2 == q):
                    evs.append(ev)
        wait(q, evs)

    def note(q, reads, writes, ev):
        for x, w in [(r, False) for r in reads] + [(r, True) for r in writes]:
            n, reg = region(x)
            h = hist.setdefault(n, [])
            if w and reg[2] == 1 and reg[3] == (0, 128):
                h[:] = [e for e in h if not (reg[0] <= e[0][0] and e[0][1] <= reg[1])]
            h[:] = [e for e in h if not (e[0] == reg and e[1] == w and e[3] == q and e[2][0] == ev[0])]
            h.append((reg, w, ev, q))

    def emit(q, fn, nout, *args, acc=False, **kw):
        reads, writes = sides(nout, args, kw)
        hazards(q, reads, writes, acc)
        s = "e" + q
        i = fn(*[ap(x) if is_ap(x) else x for x in args], **{k: ap(x) if is_ap(x) else x for k, x in kw.items()})
        i.then_inc(T.sem[s], 1)
        total[s] = total.get(s, 0) + 1
        c = dict(known[q])
        c[s] = total[s]
        clock[(s, total[s])] = c
        note(q, reads, writes, (s, total[s]))

    def batch(sem, q, reads, writes):
        o = pending.setdefault(sem, [[], [], {}])
        o[0] += list(reads)
        o[1] += list(writes)
        for k, v in known[q].items():
            o[2][k] = max(v, o[2].get(k, 0))

    def dma(q, sem, out, in_, reads, writes):
        hazards(q, reads, writes)
        Q[q].dma_start(out, in_).then_inc(T.sem[sem], 16)
        total[sem] = total.get(sem, 0) + 16
        batch(sem, q, reads, writes)

    def close(sem):
        reads, writes, c = pending.pop(sem)
        c[sem] = total[sem]
        clock[(sem, total[sem])] = c
        note("dma", reads, writes, (sem, total[sem]))

    def remote(out, in_, reads, rsem, lsem, addr, m, n):
        hazards("g", reads, [])
        g.remote_dma(out_ap=out, in_ap=in_, remote_sem=T.sem[rsem], local_sem=T.sem[lsem], pid=addr[1], routing_id=addr[0], dma_engine_mask=m)
        total[lsem] = total.get(lsem, 0) + n
        batch(lsem, "g", reads, [])

    def arrives(writes, sem, n):
        total[sem] = n
        clock[(sem, n)] = {sem: n}
        note("remote", [], writes, (sem, n))

    def finish():
        for s in sorted(total):
            if waited.get(s, 0) < total[s]:
                g.wait_ge(T.sem[s], total[s])

    return emit, dma, close, remote, arrives, finish


CYCLE, WAKE, SLACK, ISSUE, WAY, BYTE, ROW, CALL = 0.00085, 0.24, 0.03, 0.1, 0.6, 1 / 520e3, 0.01 / 16, 0.3
WAYS = (3.5, 4.0, 2.5)


ORDER = {}
PASSES, JOG, SPAN = 24, 0.3, []


def schedule(nodes):
    n = len(nodes)
    jobs, last, edges = [(o[0], o[1]) for o in nodes], list(range(n)), {}
    for k, (q, hold, way, load, deps, runs, more) in enumerate(nodes):
        if load:
            jobs.append(("engines", load))
            last[k] = len(jobs) - 1
            edges[(k, last[k])] = max(ISSUE - hold, -load)
    sync = [k for k in range(n) if nodes[k][0] == "y"]
    for a, b in zip(sync, sync[1:]):
        edges[(a, b)] = edges[(last[a], last[b])] = 0
    for k, o in enumerate(nodes):
        for d in o[4]:
            edges[(last[d], k)] = nodes[d][2] + (0 if nodes[d][0] == o[0] == "t" else WAKE)
    tail = [0.0] * len(jobs)
    for k, o in enumerate(nodes):
        tail[last[k]] = o[2]
    ahead, behind = [[] for _ in jobs], [[] for _ in jobs]
    for (a, b), lag in edges.items():
        ahead[b].append((a, lag))
        behind[a].append((b, lag))

    def place(ways, urgency, before, after, first):
        left, end, took, busy = [len(x) for x in before], [0.0] * len(jobs), [0] * len(jobs), {}
        ready = [k for k in range(len(jobs)) if not left[k]]
        while ready:
            k = max(ready, key=lambda k: urgency[k])
            ready.remove(k)
            there, fits = max([end[d] + lag for d, lag in before[k]] + [first[k]]), []
            for w, (q, hold) in enumerate(ways[k]):
                t, at, line = there, 0, busy.setdefault(q, [])
                while at < len(line) and line[at][0] < t + hold + SLACK:
                    t = max(t, line[at][1])
                    at += 1
                fits.append((t + hold - (SPARE if q != "v" else 0), w, t, at))
            _, w, t, at = min(fits)
            q, hold = ways[k][w]
            if q:
                busy[q].insert(at, (t, t + hold))
            end[k], took[k] = t + hold, w
            for u, lag in after[k]:
                left[u] -= 1
                if not left[u]:
                    ready.append(u)
        return end, took

    ways = [[o] + (nodes[k][6] if k < n else []) for k, o in enumerate(jobs)]
    back = place([[(None, o[1])] for o in jobs], tail, behind, ahead, tail)[0]
    best = None
    for turn in range(PASSES):
        end, took = place(ways, back, ahead, behind, [0.0] * len(jobs))
        span = max(e + t for e, t in zip(end, tail))
        if best is None or span < best[0]:
            best = (span, end, took)
        if turn % 3 == 2:
            span, end, took = best
        back = place([[o[w]] for o, w in zip(ways, took)], [e + JOG * ((k * 7919 + turn * 104729) ** 2 % 1009) / 1009 for k, e in enumerate(end)], behind, ahead, tail)[0]
    SPAN[:] = [best[0]]
    return [(k, best[2][k]) for k in sorted(range(n), key=lambda k: (best[1][k] - ways[k][best[2][k]][1], k))]


def planner(issue):
    emit, dma, close, remote, arrives, finish = issue
    nodes, hist, batches = [], {}, {}

    def node(q, hold, way, load, reads, writes, runs, after=(), more=()):
        deps, both = set(after), [(r, False) for r in reads] + [(r, True) for r in writes]
        for x, w in both:
            n, reg = region(x)
            deps |= {k for reg2, w2, k in hist.setdefault(n, []) if (w or w2 or n == "PS") and meet(reg, reg2)}
        for x, w in both:
            n, reg = region(x)
            if w and reg[2] == 1 and reg[3] == (0, 128):
                hist[n] = [e for e in hist[n] if not (reg[0] <= e[0][0] and e[0][1] <= reg[1])]
            hist[n].append((reg, w, len(nodes)))
        nodes.append((q, hold, way, load, deps, runs, list(more)))
        return len(nodes) - 1

    def size(x):
        return 16 * size(x[2]) if x[0] == "I" else len(range(x[2], x[3], x[4]))

    def cycles(q, nout, args):
        full = [x for x in args if is_ap(x)]
        n = size(full[0])
        if q in "tg":
            return PE * (n + 16) if q == "t" else 150 + 2 * n
        if nout == 2:
            return 15 + n
        if any(x[0] == "I" for x in full):
            return (60 if q == "v" else 80) + (3.8 if full[0][0] == "I" else GATHER) * n
        if q == "s":
            return ACTIVATION + n
        if len(args) == 4 and len(full) == 3 and "PS" not in (full[1][1], full[2][1]):
            return max(64, 2 * n)
        return max(64, n / 2 if all(SCRATCH[x[1]][2] in (B16, U16) for x in full if size(x) > 1) else n)

    def emit_(*calls):
        both = [sides(nout, args, kw) for q, fn, nout, args, kw in calls]
        ways = [(q, CYCLE * cycles(q, nout, args)) for q, fn, nout, args, kw in calls]
        runs = [(lambda c=c: emit(c[0], c[1], c[2], *c[3], **c[4])) for c in calls]
        node(*ways[0], 0, 0, [x for o in both for x in o[0]], both[0][1], runs, more=ways[1:])

    def dma_(q, sem, out, in_, reads=(), writes=(), rows=128, width=0):
        batches.setdefault(sem, []).append((q, reads, writes, rows * (ROW + width * BYTE), lambda: dma(q, sem, out, in_, reads, writes)))

    def remote_(out, in_, reads, rsem, lsem, *rest):
        batches.setdefault(lsem, []).append(("g", reads, [], 0, lambda: remote(out, in_, reads, rsem, lsem, *rest)))

    def close_(sem, lands=None, way=0):
        b = batches.pop(sem)

        def run():
            for o in b:
                o[4]()
            close(sem)
        k = node(b[0][0], len(b) * (CALL if lands else GISSUE if b[0][0] == "g" else ISSUE), WAY, sum(o[3] for o in b), [x for o in b for x in o[1]], [x for o in b for x in o[2]], [run])
        if lands is not None:
            node(None, 0, way, 0, [], lands, [lambda: None], [k])

    def finish_():
        if len(nodes) not in ORDER:
            ORDER[len(nodes)] = schedule(nodes)
        for k, w in ORDER[len(nodes)]:
            nodes[k][5][w]()
        finish()

    return emit_, dma_, close_, remote_, arrives, finish_


def rank_program(g, core, T, topo):
    rank = T.rank_of(core)
    if rank is None:
        relay(g, core, T, topo)
        return
    emit, dma, close, remote, arrives, finish = planner(builder(g, T))
    V, S = g.vector, g.scalar
    sh, an = OP.logical_shift_right, OP.bitwise_and

    def on(x, p):
        return x[:5] + (p,) if is_ap(x) else x

    def TS(out, x, s1, op0, s2=None, op1=None):
        return "v", V.tensor_scalar, 1, (out, x, s1, None, op0) if op1 is None else (out, x, s1, s2, op0, op1), {}

    def AC(out, x, func=ACT.Copy, **kw):
        return "s", S.activation, 1, (out, x, func), kw

    def IO(out, pattern, base, cm=0):
        return "g", g.iota, 1, (out, pattern, base, cm), {} if SCRATCH[out[1]][2] == I32 else {"allow_small_or_imprecise_dtypes": True}

    def ts(*args):
        emit(TS(*args))

    def tt(out, x, y, op):
        emit(("v", V.tensor_tensor, 1, (out, x, y, op), {}))

    def cp(out, x):
        emit(("v", V.tensor_copy, 1, (out, x), {}))

    def act(out, x, func=ACT.Copy, **kw):
        emit(AC(out, x, func, **kw))

    def iota(out, pattern, base, cm=0):
        emit(IO(out, pattern, base, cm))

    def move(out, x):
        emit(("v", V.tensor_copy, 1, (out, x), {}), AC(out, x))

    def lin(out, x, a, b):
        emit(TS(out, x, a, OP.mult, b, OP.add), AC(out, x, ACT.Identity, scale=a if is_ap(a) else float(a), bias=b if is_ap(b) else float(b)))

    def fill(out, k):
        n = len(range(*out[2:5]))
        ways = [("v", V.memset, 1, (out, k if SCRATCH[out[1]][2] == I32 else float(k)), {}), IO(out, [[0, n]], k)]
        if n <= 48 and out[1] != "JK" and SCRATCH[out[1]][2] != I32:
            ways.append(AC(out, A("JK", 0, n), ACT.Identity, bias=float(k)))
        emit(*ways)

    def quant(n, a, b, x, sn=None):
        emit(("v", V.quantize_mx, 2, (A(n, a, b), A(sn or "S" + n[1:], a, b), x), {}))

    def mm(bank, l, a, r, b, n, start=True, stop=True, rs=None):
        emit(("t", g.tensor.matmul_mx, 1, (A("PS", 512 * bank, 512 * bank + n), A("Q" + l, a, a + 128), A("S" + l, a, a + 128),
                                           A(r, b, b + n), A(rs or "S" + r[1:], b, b + n), start, stop), {"acc": not start}))

    def ps(bank, a, b):
        return A("PS", 512 * bank + a, 512 * bank + b)

    def scan(out, x, y, op0, op1):
        emit(("v", V.tensor_tensor_scan, 1, (out, x, y, 0.0, op0, op1), {}))

    def spread(out, flat, keys):
        scan(out, A(keys, 0, out[3] - out[2]), flat, OP.mult, OP.max)

    def listed(out, flat, at, k=0, parts=None):
        n = flat[3] - flat[2]
        spread(A("SP", at, at + n), flat, "K16")
        for o, p, k in parts or [(out, (0, 128), k)]:
            ts(on(o, p), A("SP", at + 15, at + n, 16, p), on(sc("h16"), p), OP.mult, k - M, OP.add)

    names = ["i", "g", "s", "q", "i4", "r3", "r7"]

    def sc(n):
        if n not in names:
            names.append(n)
        k = names.index(n)
        return A("SC", k, k + 1)

    def ix(a, b):
        return A("IDX", a, b)

    def turn(sem, name, width, a, b, k, src=None, q="y", mid=0):
        for d0, s0, rows, slot in ((0, 16 * k, 128 - 16 * k, mid + k), (128 - 16 * k, 0, 16 * k, mid + k - 8 if mid else k)):
            o, to = width * mid, width * slot
            dma(q, sem, T[name][d0:d0 + rows, to + a:to + b], T[name][s0:s0 + rows, o + a:o + b] if src is None else src[s0:s0 + rows, a:b],
                reads=[A(name, o + a, o + b)] if src is None else [], writes=[A(name, to + a, to + b)], rows=rows,
                width=(b - a) * (2 if SCRATCH[name][2] == B16 else 4))

    def shifted(sem, name, a, b, slots=range(1, 8), q="y", src=None):
        for k in slots:
            if name[0] == "R":
                turn(sem, name, W4, a, b, k, src, q, 7)
            else:
                turn(sem, name, LW, a, b, k, src, q)
        close(sem)

    def across(sem, name, moves, q="y"):
        for s0, d0, rows, a, to, n in moves:
            dma(q, sem, T[name][d0:d0 + rows, to:to + n], T[name][s0:s0 + rows, a:a + n], reads=[A(name, a, a + n, p=(s0, s0 + rows))],
                writes=[A(name, to, to + n, p=(d0, d0 + rows))], rows=rows, width=4 * n)
        close(sem)

    def ln(out, i, p=(0, 128), k=0):
        ts(on(out, p), A("LN", 20 * i, 20 * i + 20, p=p), k, OP.add)

    for k in range(8):
        dma("ys"[k % 2], "d_ln", T.LN[16 * k:16 * k + 16, :], T.ln[:, :], writes=[A("LN", 0, 60)], rows=16)
    close("d_ln")
    dma("y", "d_p", T.LP[:, 0:25], T.p[:, :], writes=[A("LP", 0, 25)])
    close("d_p")
    dma("y", "d_u", T.UT[:, :], T.u[:, :], writes=[A("UT", 0, 512)], width=1024)
    close("d_u")
    dma("y", "d_x", T.R0[:, MID:MID + W4], T.x[:, :], writes=[A("R0", MID, MID + W4)], width=8 * C)
    close("d_x")
    shifted("d_x0", "R0", 0, W4, range(1, XS[0]), src=T.x)

    J16, JC, JK, JL = A("JF", 0, 40), A("JF", 40, 50), A("JF", 126, 134), A("JF", 50, 62)
    iota(ix(0, 1), [[0, 1]], 0, 1)
    iota(A("TAB", 0, C), [[1, C]], M)
    iota(A("PAT", 0, 16), [[1, 16]], 0)
    iota(A("K16", 0, C), [[0, 25], [1, 16]], 0)
    iota(JC, [[8, 2], [64, 5]], 0)
    iota(JK, [[8, 2], [256, 4]], 0)
    iota(JL, [[ST, 2], [64, 6]], ST)
    iota(A("TAB", C, C + ST), [[1, 80], [1024, 4]], M + ST)
    iota(J16, [[-5 * LW, 2], [16, 20]], 5 * LW)
    fill(A("JK", 0, 48), 0)
    fill(A("WT", 0, 1024), 0)
    for quarter, row, a, b, s, w in [o for lines in WEIGHTS for o in lines]:
        fill(A("WT", 256 * quarter + 16 * row + a, 256 * quarter + 16 * row + b, s), w)
    iota(A("K4", 0, C), [[0, 100], [1, 4]], 0)
    fill(A("ONE", 0, 520), 1)
    for h in range(2):
        emit(("g", g.affine_select, 1, (A("ET", 520 * h, 520 * h + 520), A("ONE", 0, 520), [[-1, 520]], OP.is_equal, 0.0, 2 + h, 4), {}))
    for b in range(4):
        o = 520 * (b % 2) + 2 - b // 2 * 2
        quant("QE", 128 * b, 128 * b + 128, A("ET", o, o + 512))
    fill(A("ZS", 4 * KX, 512), 0)
    for d in range(2):
        fill(A("BT%d" % d, 160, 592), 0)

    for k, (s, m) in enumerate(((0, 15), (4, 7), (4, 1), (5, 3), (2, 3), (0, 3), (0, 7))):
        ts(ix(1 + k, 2 + k), ix(0, 1), s, sh, m, an)
    cp(A("SC", 0, 7), ix(1, 8))
    lin(sc("rg"), sc("g"), -1, 7)
    ts(sc("e"), sc("g"), sc("rg"), OP.min)
    ts(sc("a1"), sc("e"), 1, OP.is_equal)
    ts(sc("n3"), sc("e"), 3, OP.is_equal, NEVER, OP.mult)
    ts(sc("isc"), sc("r7"), 2.5, OP.is_gt)
    for out, x, a, b in (("home", "g", W4, -3 * M), ("t0", "i4", 16, "r3"), ("cl", "s", 4, "t0"), ("i16", "i", 16, 0), ("wl", "q", 256, "i16"),
                         ("kl", "g", 1, "i16"), ("clu", "i", 4, "q"), ("cg", "g", -LW, 8 * LW), ("cgp", "s", LW, 3 * LEVEL), ("ns", "s", -1, 1),
                         ("i6", "i", 1, 6 * LEVEL), ("j6", "g", LW, "i6"), ("t1", "r3", 1, MID - M), ("off", "g", -W4, "t1"),
                         ("na1", "a1", -1, 1), ("c5", "a1", -NEVER, NEVER + 5 * LEVEL), ("t2", "r7", 16, 0), ("ul0", "isc", -47, "t2"),
                         ("t3", "r7", -16, 32), ("ul1", "isc", 49, "t3"), ("fs", "isc", 2, -1), ("fb", "isc", -1, 1)):
        lin(sc(out), sc(x), a, sc(b) if isinstance(b, str) else b)
    CL, WL = A("SL", 0, 10), A("SL", 10, 26)
    KL, CLU, UL = (lambda f: A("SL", 26 + 4 * f, 30 + 4 * f)), (lambda d: A("SL", 34 + 6 * d, 39 + 6 * d)), (lambda d: A("SL", 46 + 8 * d, 54 + 8 * d))
    for a, x, k in ((0, JC, "cl"), (10, A("PAT", 0, 16), "wl"), (26, JK, "kl"), (34, JL, "clu"), (46, A("JK", 0, 8), "ul0"), (54, A("JK", 0, 8), "ul1")):
        ts(A("SL", a, a + x[3] - x[2]), x, sc(k), OP.add)
    for n, k in ((16, "i"), (4, "i4")):
        ts(A("K%d" % n, 0, C), A("K%d" % n, 0, C), sc(k), OP.not_equal, 2, OP.mult)
        ts(A("PAT", 16 + n, 16 + 2 * n), A("PAT", 0, n), sc(k), OP.is_le, 0.5, OP.max)
        emit(("v", V.tensor_reduce, 1, (sc("h%d" % n), A("PAT", 16 + n, 16 + 2 * n), AxisListType.X, OP.mult), {}))

    for i, p in ((2, (0, 32)), (1, (32, 64)), (0, (64, 128))):
        ln(A("LA", 0, 20), i, p)
    cp(IND(A("QQ", 0, ST), A("LA", 0, 20)), A("TAB", 0, ST))
    across("d_q2", "QQ", [(0, 32 * k, 32, 0, ST, ST) for k in range(4)])
    cp(A("PU", 0, 25), A("LP", 0, 25))
    lin(A("T0", 0, C), IND(A("TAB", 0, C), A("PU", 0, 25)), 4, sc("home"))
    shifted("d_tb", "T0", 0, C, range(1, XS[2]))

    def others(d):
        lm, fm, ft = A("LM", 20 * d, 20 * d + 20), A("FM", ST * d, ST * d + ST), A("FT", 160 * d, 160 * d + 160)
        for i, p, k in (((2, (0, 96), 0), (1, (96, 128), 0)), ((2, (0, 32), 0), (0, (32, 64), 0), (0, (64, 96), ST), (1, (96, 128), ST)))[d]:
            ln(lm, i, p, k)
        move(fm, IND(A("QQ", 0, ST + ST * d), lm))
        at = lambda role: 60 * d + 20 * role - 20
        listed(None, fm, 800 * d, parts=[(A("SRA", at(k), at(k) + 20), (32 * k, 32 * k + 32), ROLE[k]) for k in ROLE])
        across("d_s%d" % d, "SRA", [(32 * k, 32 * o, 32, at(k), at(k), 20) for k in ROLE for o in range(4) if o != k], SQ if d else "y")
        move(ft, IND(fm, CL))
        listed(A("RL%d" % d, 0, 10), ft, 800 * d + ST)

    others(0)
    shifted("d_ta", "T0", 0, C, range(XS[2], 8))
    shifted("d_x1", "R0", 0, W4, range(XS[0], XS[1]))
    shifted("d_x2", "R0", 0, W4, range(XS[1], 8))
    dma("y", "d_w", T.QW[:, :].bitcast(dt.uint8), T.wc[:, :], writes=[A("QW", 0, 512)], width=2048)
    dma("y", "d_w", T.SW[:, :], T.ws[:, :], writes=[A("SW", 0, 512)], width=512)
    close("d_w")
    across("d_q0", "QQ", [(64, 64 * k, 64, 0, 2 * ST, ST) for k in range(2)])
    dma("y", "d_v", T.VT[:, :], T.v[:, :], writes=[A("VT", 0, 512)], width=1024)
    close("d_v")
    quant("QV", 0, 128, A("VT", 0, 512))
    others(1)

    lin(A("WG", 0, 256), IND(A("WT", 0, 1024), WL), 1, MW)
    spread(A("WS", 0, 256), A("WG", 0, 256), "K16")
    ts(A("WS", 256, 272), A("WS", 15, 256, 16), sc("h16"), OP.mult, -MW, OP.add)
    fill(A("KW", 0, 1056), 0)
    for k in range(8):
        lin(A("KW", 32 + 4 * k + k % 4, 1056, 64), A("WS", 256, 272), sc("s" if k // 4 else "ns"), 0)
    quant("QK", 0, 264, A("KW", 0, 1056))
    for f in range(2):
        act(A("WG", 256 + 64 * f, 320 + 64 * f), IND(A("WT", 0, 1024), KL(f)), ACT.Relu, scale=-1.0, accum_out=sc("w%d" % f))
        lin(A("CC", f, f + 1), sc("w%d" % f), LW, LW * EXTRA[f])

    ts(ix(20, 80), A("LN", 0, 60), 3, an)
    ts(ix(80, 140), A("LN", 0, 60), 2, sh)
    ts(A("BG", 60, 120), ix(20, 80), 1024, OP.mult, ST, OP.add)
    tt(A("BG", 0, 60), A("BG", 60, 120), ix(80, 140), OP.add)
    OWN6 = A("TM", 360, 400)
    lin(A("TM", 360, 380), A("JF", 0, 20), 1, sc("j6"))
    lin(A("TM", 380, 400), A("JF", 20, 40), 1, sc("i6"))

    cp(IND(A("CF", 0, C), A("PU", 0, 20)), A("TAB", 0, ST))
    for d in range(2):
        lin(A("ML", 80 * d, 80 * d + 80), IND(A("QQ", 0, 2 * ST + ST * d), CLU(d)), 1, ST - ST * d)
    for d, links in enumerate((A("ML", 0, 80), A("TAB", ST, C))):
        cp(IND(A("CF", 0, C), A("PU", 20, 25)), links)
        listed(A("CM%d" % d, 0, 25), A("CF", 0, C), 1600 + C * d)
    listed(A("LTL", 0, 5), A("ML", 80, 160), 2400)

    quant("QU", 0, 128, A("UT", 0, 512))
    for d in range(2):
        cp(CW("QUP", 128 * d, 128 * d + 128), IND(CW("QU", 0, 128), UL(d)))
        move(A("SUP", 128 * d, 128 * d + 128), IND(A("SU", 0, 128), UL(d)))
        step = lambda k, h=None: A("D%d" % d, k, KW, NK) if h is None else A("D%d" % d, KW // 2 * h + k, KW // 2 * h + KW // 2, NK)
        tm = lambda k, h=None: A("TM", 180 * d + 40 * k + 20 * (h or 0), 180 * d + 40 * k + (40 if h is None else 20 * h + 20))
        src = lambda role: A("SRA", 60 * d + 20 * role - 20, 60 * d + 20 * role)
        bg = lambda i: A("BG", 20 * i, 20 * i + 20)
        lf, lb, lz = 640 * d, A("LB", 20 * d, 20 * d + 20), A("LZ", 20 * d, 20 * d + 20)
        ln(lb, 2 * d, k=C)
        move(A("LF", lf, lf + ST), IND(A("TAB", 0, 720), lb))
        ts(lz, src(RZ), -ROLE[RZ], OP.add)
        move(A("LF", lf + ST, lf + 640), IND(A("LF", lf, lf + ST), lz))
        listed(tm(4, 0), A("LF", lf + ST, lf + 640), 800 * d + 480)
        lin(tm(0, 0), bg(2 - 2 * d), 1, 3 * LEVEL)
        lin(tm(0, 1), bg(2 - 2 * d), 1, sc("cgp"))
        lin(tm(3, 0), bg(2 * d), sc("na1"), sc("n3"))
        lin(tm(3, 1), src(RX), sc("a1"), 4 * LEVEL)
        tt(tm(1, 0), tm(3, 0), tm(3, 1), OP.add)
        lin(tm(1, 1), src(RX), 1, 4 * LEVEL)
        lin(tm(2, 0), bg(1), 1, sc("c5"))
        lin(tm(2, 1), bg(1), 1, 5 * LEVEL)
        fill(step(0), 2 ** 23)
        for h in range(2):
            tt(step(1, h), tm(4, 0), src(RZ), OP.subtract)
            tt(step(2, h), src(RZ), src(RY), OP.subtract)
            tt(step(3, h), src(RY), tm(0, h), OP.subtract)
        for k, a, b in ((4, tm(0), tm(1)), (5, tm(1), tm(2)), (6, tm(2), OWN6)):
            tt(step(k), a, b, OP.subtract)
        lin(step(7), OWN6, 1, sc("cg"))
        fill(A("KC%d" % d, NK - 1, KW, NK), 2 ** 23)

    def signs(d, src=None, at=0):
        if d == 0:
            for h in range(2):
                quant("QX", 160 * h, 160 * h + 160, A(src, at + 640 * h, at + 640 * h + 640))
                mm(h, "UP", 0, "QX", 160 * h, 160)
                o = A("SG0", 160 * h, 160 * h + 160)
                emit(TS(o, ps(h, 0, 160), 0.0, OP.is_gt), AC(o, ps(h, 0, 160), ACT.Sign))
            for a, b in ((0, 6), (6, 10)):
                o, x = A("BT0", 16 * a, 16 * b), IND(A("SG0", 0, ST), A("RL0", a, b))
                emit(TS(o, x, 0.0, OP.max), AC(o, x, ACT.Relu))
        else:
            mm(4, "UP", 128, "QX", 0, ST)
            ts(A("SG1", 0, ST), ps(4, 0, ST), 0.0, OP.is_gt)
            lin(A("BT1", 0, 160), IND(A("SG1", 0, ST), A("RL1", 0, 10)), sc("fs"), sc("fb"))
        quant("QB%d" % d, 0, 148, A("BT%d" % d, 0, 592))
        for f in range(2):
            for m in range(2):
                mm(2 + 3 * d + f, "K", 128 * f + 8 - 8 * m, "QB%d" % d, 20 * m, 128, m == 0, m == 1)
            ts(A("KI%d" % d, 20 * f, 20 * f + 20), ps(2 + 3 * d + f, 0, 20), LW, OP.mult, A("CC", f, f + 1), OP.add)

    def choose(d):
        for k, (s, m, bits) in enumerate(FIELDS):
            ts(A("KC%d" % d, k, KW, NK), A("KI%d" % d, 0, 40), s, sh, LW * (m + sum(1 << (b - s) for b in bits)), an)
        scan(A("SK%d" % d, 0, KW), A("D%d" % d, 0, KW), A("KC%d" % d, 0, KW), OP.add, OP.min)
        ts(A("RS%d" % d, 0, 40), A("SK%d" % d, NK - 1, KW, NK), 8 * LW - 1, an)
        cp(A("LU%d" % d, 0, 40), A("RS%d" % d, 0, 40))

    def lookup(d, table, stacks, links):
        move(links, IND(A(table, 0, 8 * LW), A("LU%d" % d, 20, 40)))
        move(stacks, IND(A(table, 0, 8 * LW), A("LU%d" % d, 0, 20)))

    def offsets(out, d, *cuts):
        for a, b in zip(cuts, cuts[1:]):
            move(A("MG%d" % d, a, b), IND(A("TN", 0, C) if d else A("FL0", 0, 640), A("CM%d" % d, a // 16, b // 16)))
        c0, c1 = cuts[0], cuts[-1]
        spread(A("SN%d" % d, c0, c1), A("MG%d" % d, c0, c1), "K4")
        ts(A(out, c0 // 4, c1 // 4), A("SN%d" % d, c0 + 3, c1, 4), sc("h4"), OP.mult, sc("off"), OP.add)

    def pull(dst, win, offs, *cuts):
        for a, b in zip(cuts, cuts[1:]):
            move(A(dst, 4 * a, 4 * b), IND(A(win, 0, WIN), A(offs, a // 4, b // 4)))

    for r in range(STEPS):
        HQ, HS = "HQ%d" % r, "HS%d" % r
        OLD, NEW = "R%d" % (r % 2), "R%d" % (1 - r % 2)
        peer = rank ^ MATES[r]
        n_arr = sum(mask_of(topo, T.cores[peer] if c is None else c, core)[1] for c in hops(T, topo, peer, r))
        arrives([A(HQ, 0, KX), A(HS, 0, KX)], "arr%d" % r, n_arr)

        def layer(name, c0, c1):
            n, m = c1 - c0, max(c1 - c0, 128)
            for b in range(4):
                mm(b, "W", 128 * b, HQ, c0, m, rs=HS)
                mm(4 + b, "E", 128 * b, HQ, c0, m, rs=HS)
            for b in range(4):
                l = A("R" + name, n * b, n * b + n)
                emit(AC(l, ps(b, 0, n), ACT.Relu, scale=0.015625), TS(l, ps(b, 0, n), 0.0, OP.max, 0.015625, OP.mult))
                tt(A(NEW, MID + 4 * c0 + b, MID + 4 * c1, 4), l, ps(4 + b, 0, n), OP.add)
            for q in sorted(set(SHARE[name])):
                shifted("d_%s%s%d" % (q, name, r), NEW, 4 * c0, 4 * c1, [k + 1 for k in range(7) if SHARE[name][k] == q], q)

        signs(0, *(("XT", 0) if r else ("R0", MID)))
        if r:
            signs(1)
        choose(0)
        lookup(0, "TN" if r else "T0", A("FL0", 0, ST), A("FL0", ST, 640))
        offsets("OFZ", 0, 0, KX)
        offsets("OFZ", 0, KX, CA)
        pull("ZT", OLD, "OFZ", KX, 160, CA)
        quant(HQ, KX, CA, A("ZT", 4 * KX, 4 * CA), HS)
        pull("ZS", OLD, "OFZ", 0, 48, KX)
        quant("QS", 0, 128, A("ZS", 0, 512))
        way = hops(T, topo, rank, r)
        for k, c in enumerate(way):
            to = T.cores[peer] if c is None else c
            m, n = mask_of(topo, core, to)
            if k == 0:
                o = T[HQ if c is None else "QR"][:, 0:KX].bitcast(dt.uint8)
                i, rd = T.QS[:, 0:KX].bitcast(dt.uint8), [A("QS", 0, KX)]
            else:
                o = T[HS if c is None else "SR"][:, 0:KX]
                i, rd = T.SS[:, 0:KX], [A("SS", 0, KX)]
            remote(o, i, rd, "arr%d" % r if c is None else "rarr", "snt%d" % r, topo.addr(to, core), m, n)
        close("snt%d" % r, [A(HQ, 0, KX), A(HS, 0, KX)], WAYS[r])
        offsets("OFZ", 0, CA, C)
        pull("ZT", OLD, "OFZ", CA, CB, C)
        quant(HQ, CA, C, A("ZT", 4 * CA, 4 * C), HS)
        if r == 0 and POS == 1:
            signs(1)
        layer("A", KX, CA)
        if r == 0 and POS == 2:
            signs(1)
        layer("B", CA, C)
        if r == 0 and POS == 3:
            signs(1)
        layer("C", 0, KX)
        choose(1)
        lookup(1, "T0", A("TN", 0, ST), A("FL1", 0, ST))
        move(A("TN", ST, C), IND(A("FL1", 0, ST), A("LTL", 0, 5)))
        if r < STEPS - 1:
            shifted("d_tn%d" % r, "TN", 0, C)
            offsets("OFX", 1, 0, CMX, ST)
            pull("XT", NEW, "OFX", 0, 160, ST)
        else:
            offsets("OFX", 1, 0, 224, C)
            lookup(0, "T0", A("FLO", 0, ST), A("FLO", ST, 640))
            lin(A("OPF", 0, C), IND(A("FLO", 0, 640), A("CM0", 0, 25)), 0.25, -M // 4)
            for k in range(8):
                dma("y", "d_op", T.op[k:k + 1, :], T.OPF[16 * k:16 * k + 1, :], reads=[A("OPF", 0, C)], rows=1)
            close("d_op")

    for h, (a, b) in enumerate(zip(LAST, LAST[1:])):
        pull("XT", NEW, "OFX", a, a + CUT[h], b)
        quant("QX", a, b, A("XT", 4 * a, 4 * b))
        mm(h, "V", 0, "QX", a, b - a)
        dma("y", "d_o%d" % h, T.oc[:, 4 * a:4 * b], T.QX[:, a:b].bitcast(dt.uint8), reads=[A("QX", a, b)], width=4 * (b - a))
        close("d_o%d" % h)
        move(A("YO", a, b), ps(h, 0, b - a))
        dma("y", "d_y%d" % h, T.y[:, a:b], T.YO[:, a:b], reads=[A("YO", a, b)], width=4 * (b - a))
        close("d_y%d" % h)
    for k in range(4):
        dma("s", "d_out", T.osc[4 * k:4 * k + 4, :], T.SX[32 * k:32 * k + 4, :], reads=[A("SX", 0, C)], rows=4)
    close("d_out")
    finish()


XS = (3, 6, 4)
PE, GATHER, ACTIVATION, SPARE = 1.0, 1.3, 70, 0.1
POS, SQ = 1, "y"
SHARE = {"A": "yyyysss", "B": "yyyyyyy", "C": "yyyysss"}
GISSUE = 1.0
CUT = (56, 56, 56)
PAINT, BACK, CMX, CB = "sgs", (0, 0, 0), 224, 312
